import numpy as np
import ml_dtypes


def mxq(x, axis, fmt="e4m3"):
    dtype, down = {"e4m3": (ml_dtypes.float8_e4m3fn, 7), "e5m2": (ml_dtypes.float8_e5m2, 14)}[fmt]
    v = np.moveaxis(np.asarray(x, np.float32).astype(ml_dtypes.bfloat16).astype(np.float64), axis, -1)
    blocks = v.reshape(v.shape[:-1] + (-1, 32))
    amax = np.abs(blocks).max(-1, keepdims=True)
    byte = np.maximum(np.where(amax > 0, np.frexp(amax)[1] - 1 + 127, 0) - down, 1)
    scale = np.exp2(byte - 127.0)
    codes = (blocks / scale).astype(np.float32).astype(dtype).astype(np.float64)
    return np.moveaxis((codes * scale).reshape(v.shape), -1, axis)


WIDE = False


def mx_kscale(k):
    if not WIDE:
        return np.ones(k)
    levels = np.array([24, -24, 12, -12, 0])
    if k % 512:
        return np.exp2(np.random.permutation(np.resize(levels, k // 32))).repeat(32)
    a = np.empty((k // 512, 16))
    for p in range(k // 512):
        a[p, :8] = np.random.permutation(np.resize(levels, 8))
        for g in range(8):
            far = levels[np.abs(levels - a[p, g]) >= 10]
            a[p, g + 8] = far[np.random.randint(len(far))]
    return np.exp2(a.ravel()).repeat(32)


def f64(x):
    return np.asarray(x).astype(np.float64)


def striped(idx):
    return np.tile(idx.reshape(-1, 16).T, (8, 1)).astype(np.uint16)


def unstriped(offs):
    return offs[:16].T.reshape(-1).astype(np.int64)


E2M1 = np.array([0.0, 0.5, 1.0, 1.5, 2.0, 3.0, 4.0, 6.0, -0.0, -0.5, -1.0, -1.5, -2.0, -3.0, -4.0, -6.0])


def pack_weight(w, fmt):
    k, n = w.shape
    w = f64(np.asarray(w, np.float32).astype(ml_dtypes.bfloat16)).reshape(k // 32, 32, n)
    amax = np.abs(w).max(1)
    if fmt == "e4m3":
        byte = np.frexp(amax)[1] - 1 + 127 - 7
    else:
        mant, ex = np.frexp(amax / 6.0)
        byte = np.where(mant > 0.5, ex, ex - 1) + 127
    byte = np.clip(np.where(amax > 0, byte, 1), 1, 254)
    scaled = (w * np.exp2(127.0 - byte)[:, None, :]).reshape(k, n).astype(np.float32)
    by_word = np.ascontiguousarray(scaled.reshape(k // 512, 128, 4, n).transpose(0, 1, 3, 2))
    if fmt == "e4m3":
        words = by_word.astype(ml_dtypes.float8_e4m3fn).view(np.uint8)
    else:
        c = by_word.astype(ml_dtypes.float4_e2m1fn).view(np.uint8) & 0xF
        words = (c[..., 0::2] | (c[..., 1::2] << 4)).reshape(k // 512, 128, 2 * n)
    return np.ascontiguousarray(words), np.ascontiguousarray(byte.astype(np.uint8).reshape(k // 512, 16, n))


def unpack_weight(words, scales, fmt):
    g, _, n = scales.shape
    words = np.ascontiguousarray(words).reshape(g, 128, n, -1)
    if fmt == "e4m3":
        vals = words.view(ml_dtypes.float8_e4m3fn).astype(np.float64)
    else:
        nib = np.empty((g, 128, n, 4), np.uint8)
        nib[..., 0::2] = words & 0xF
        nib[..., 1::2] = words >> 4
        vals = E2M1[nib]
    vals = vals * np.repeat(np.exp2(scales.astype(np.float64) - 127.0), 8, axis=1)[..., None]
    return vals.transpose(0, 1, 3, 2).reshape(g * 512, n)


K, M, N, T, J = 1024, 512, 512, 2048, 1024


def setup_inputs():
    n = np.random.standard_normal
    s = mx_kscale(K)[:, None]
    s2 = mx_kscale(M)[:, None]
    h = np.tanh(n((N, T)))
    p_tab = pack_weight(h * s2, "e4m3")
    p_wn = pack_weight(n((K, N)) / np.sqrt(K) / s, "e4m3")
    p_un = pack_weight(n((M, N)) / np.sqrt(M) / s2, "e2m1")
    return {
        "x": (n((K, J)) * s).astype(np.float32),
        "tab_words": p_tab[0],
        "tab_scales": p_tab[1],
        "wn_words": p_wn[0],
        "wn_scales": p_wn[1],
        "un_words": p_un[0],
        "un_scales": p_un[1],
        "bn": (0.3 * n(N)).astype(np.float32),
        "hT": (h).astype(np.float32),
        "wgo": np.tile(np.random.uniform(0.5, 2.0, J), (128, 1)).astype(np.float32),
        "offs": striped(np.random.permutation(T)[:J]),
    }


def reference(x, tab_words, tab_scales, wn_words, wn_scales, un_words, un_scales, bn, hT, wgo, offs):
    idx = unstriped(offs)
    x_ = mxq(f64(x), 0, "e4m3")
    tab_ = unpack_weight(tab_words, tab_scales, "e4m3")[:, idx]
    wn_ = unpack_weight(wn_words, wn_scales, "e4m3")
    un_ = unpack_weight(un_words, un_scales, "e2m1")
    sn = wn_.T @ x_ + un_.T @ tab_
    out = np.zeros((N, T))
    out[:, idx] = f64(wgo)[0] * (np.tanh(sn + f64(bn)[:, None]) + f64(hT)[:, idx])
    return out

@@ -1,0 +1,223 @@
+from contextlib import ExitStack
+
+import concourse.mybir as mybir
+from concourse.masks import make_identity
+
+K, M, N, T, J = 1024, 512, 512, 2048, 1024
+FLOPS = 2 * (K + M) * N * J
+
+F32 = mybir.dt.float32
+BF16 = mybir.dt.bfloat16
+I32 = mybir.dt.int32
+U32 = mybir.dt.uint32
+U16 = mybir.dt.uint16
+U8 = mybir.dt.uint8
+FP8X4 = mybir.dt.float8_e4m3fn_x4
+FP4X4 = mybir.dt.float4_e2m1fn_x4
+ACT = mybir.ActivationFunctionType
+
+P = 128
+PACK = 4
+K_PASS = P * PACK
+PASSES = K // K_PASS
+N_TILES = N // P
+QUARTER = 256
+HALF = 512
+OUT_TILES = 3
+
+
+def tile_list_tgn_rnn_kernel(
+    tc, x, tab_words, tab_scales, wn_words, wn_scales, un_words, un_scales, bn, hT, wgo, offs, out
+):
+    nc = tc.nc
+    with ExitStack() as ctx:
+        keep = ctx.enter_context(tc.tile_pool(name="keep", bufs=1))
+        ring = ctx.enter_context(tc.tile_pool(name="ring", bufs=3))
+        psum = ctx.enter_context(tc.psum_pool(name="psum", bufs=2))
+
+        offsets = keep.tile([P, J // 16], U16, name="offsets")
+        tab_w = keep.tile([P, T], I32, name="tab_w", tag="window0", align_bytes=64)
+        tab_s = keep.tile([P, T // 4], I32, name="tab_s", tag="window1", align_bytes=64)
+        v_w = keep.tile([P, J], U32, name="v_w", align_bytes=64)
+        v_s = keep.tile([P, J], U8, name="v_s", align_bytes=64)
+        wn_w = keep.tile([P, PASSES, N], I32, name="wn_w", align_bytes=64)
+        wn_s = keep.tile([P, PASSES, N // 4], I32, name="wn_s", align_bytes=64)
+        un_w = keep.tile([P, 2 * N], U8, name="un_w", align_bytes=64)
+        un_s = keep.tile([P, N // 4], I32, name="un_s", align_bytes=64)
+        x_raw = {}
+        x_bf = keep.tile([P, PASSES, J, PACK], BF16, name="x_bf", align_bytes=64)
+        x_w = keep.tile([P, PASSES, J], U32, name="x_w", align_bytes=64)
+        x_s = keep.tile([P, PASSES, J], U8, name="x_s", align_bytes=64)
+        h_all = {}
+        h_picked = [keep.tile([P, J], F32, name="h_picked%d" % c) for c in range(N_TILES)]
+        placed = [keep.tile([P, T], F32, name="placed%d" % c) for c in range(OUT_TILES)]
+        ident = keep.tile([P, P], F32, name="ident")
+        vec_rows = keep.tile([P, P], F32, name="vec_rows")
+        vec_cols = keep.tile([P, 16], F32, name="vec_cols")
+        warm = keep.tile([P, 8], F32, name="warm")
+
+        def listed(j0, width):
+            return offsets[:, j0 // 16 : (j0 + width) // 16]
+
+        def load_x(a, j0, width):
+            rows = x[a * K_PASS : (a + 1) * K_PASS, j0 : j0 + width]
+            raw = keep.tile([P, PACK, width], F32, name="x_raw", bufs=2)
+            for q0 in range(0, width, QUARTER):
+                x_raw[a, j0 + q0] = raw[:, :, q0 : q0 + QUARTER]
+            nc.sync.dma_start(out=raw[:], in_=rows.rearrange("(p i) j -> p i j", i=PACK))
+
+        def load_h(c):
+            h_all[c] = keep.tile([P, T], F32, name="h_all", tag="window%d" % (c % 2), align_bytes=64)
+            nc.sync.dma_start(out=h_all[c][:], in_=hT[c * P : (c + 1) * P, :])
+
+        def interleave(a, j0):
+            src = x_raw[a, j0].rearrange("p i (c e) -> p c i e", e=4)
+            dst = x_bf[:, a, j0 : j0 + QUARTER, :].rearrange("p (c e) i -> p c i e", e=4)
+            nc.scalar.activation(out=dst, in_=src, func=ACT.Copy)
+
+        def quantise(a, j0, width):
+            nc.vector.quantize_mx(
+                out=x_w[:, a, j0 : j0 + width].bitcast(FP8X4),
+                scales=x_s[:, a, j0 : j0 + width],
+                in_=x_bf[:, a, j0 : j0 + width, :].rearrange("p j i -> p (j i)"),
+            )
+
+        def gather_h(c, j0, width):
+            nc.vector.tensor_copy(
+                out=h_picked[c][:, j0 : j0 + width], in_=h_all[c][:].indirect(listed(j0, width))
+            )
+
+        def update(c, j0, width):
+            cols = slice(c * P, (c + 1) * P)
+            group = HALF if width == HALF else P
+            sn = psum.tile([P, HALF], F32, name="sn")
+            for g0 in range(0, width, group):
+                js = slice(j0 + g0, j0 + g0 + group)
+                acc = sn[:, g0 : g0 + group]
+                for a in range(PASSES):
+                    nc.tensor.matmul_mx(
+                        out=acc,
+                        lhsT=wn_w[:, a, cols].bitcast(FP8X4),
+                        lhsT_scale=wn_s[:].bitcast(U8)[:, a, cols],
+                        rhs=x_w[:, a, js].bitcast(FP8X4),
+                        rhs_scale=x_s[:, a, js],
+                        start=(a == 0),
+                        stop=False,
+                    )
+                nc.tensor.matmul_mx(
+                    out=acc,
+                    lhsT=un_w[:, 2 * c * P : 2 * (c + 1) * P].bitcast(FP4X4),
+                    lhsT_scale=un_s[:].bitcast(U8)[:, cols],
+                    rhs=v_w[:, js].bitcast(FP8X4),
+                    rhs_scale=v_s[:, js],
+                    start=False,
+                    stop=True,
+                )
+            step = ring.tile([P, HALF], F32, name="step")
+            nc.scalar.activation(
+                out=step[:, :width], in_=sn[:, :width], func=ACT.Tanh, bias=vec_cols[:, 8 + c : 9 + c]
+            )
+            summed = psum.tile([P, HALF], F32, name="summed", bufs=3)
+            for b0 in range(0, width, P):
+                blk = slice(b0, b0 + P)
+                nc.tensor.matmul(
+                    out=summed[:, blk], lhsT=h_picked[c][:, j0 + b0 : j0 + b0 + P], rhs=ident[:],
+                    start=True, stop=False, is_transpose=True,
+                )
+                nc.tensor.matmul(
+                    out=summed[:, blk], lhsT=step[:, blk], rhs=ident[:],
+                    start=False, stop=True, is_transpose=True,
+                )
+            weighted = ring.tile([P, HALF], F32, name="weighted")
+            for b0 in range(0, width, P):
+                jb = (j0 + b0) // P
+                nc.scalar.activation(
+                    out=weighted[:, b0 : b0 + P], in_=summed[:, b0 : b0 + P], func=ACT.Copy,
+                    scale=vec_cols[:, jb : jb + 1],
+                )
+            back = psum.tile([P, HALF], F32, name="back", bufs=3)
+            for b0 in range(0, width, P):
+                nc.tensor.transpose(back[:, b0 : b0 + P], weighted[:, b0 : b0 + P], ident[:])
+            result = ring.tile([P, HALF], F32, name="result")
+            nc.scalar.copy(out=result[:, :width], in_=back[:, :width])
+            nc.vector.tensor_copy(
+                out=placed[c % OUT_TILES][:].indirect(listed(j0, width)), in_=result[:, :width]
+            )
+
+        def store(c):
+            nc.sync.dma_start(out=out[c * P : (c + 1) * P, :], in_=placed[c % OUT_TILES][:])
+
+        make_identity(nc, ident[:])
+        nc.gpsimd.memset(tab_s[:], 0)
+        nc.gpsimd.memset(un_s[:], 0)
+        nc.vector.memset(wn_s[:], 0)
+        nc.vector.memset(vec_rows[:], 0.0)
+        nc.vector.memset(warm[:], 0.0)
+
+        nc.sync.dma_start(offsets[:], offs)
+        nc.sync.dma_start(out=tab_w[:], in_=tab_words[0].rearrange("p t i -> p (t i)").bitcast(I32))
+        for a in range(PASSES):
+            load_x(a, 0, QUARTER)
+        nc.sync.dma_start(out=wn_w[:], in_=wn_words.rearrange("a p n i -> p a (n i)").bitcast(I32))
+        nc.sync.dma_start(out=un_w[:].bitcast(I32), in_=un_words[0].bitcast(I32))
+        for q in range(4):
+            nc.gpsimd.dma_start(
+                out=tab_s[32 * q : 32 * q + 4, :], in_=tab_scales[0, 4 * q : 4 * q + 4, :].bitcast(I32)
+            )
+        for q in range(4):
+            nc.scalar.dma_start(
+                out=wn_s[32 * q : 32 * q + 4, :, :],
+                in_=wn_scales[:, 4 * q : 4 * q + 4, :].bitcast(I32).rearrange("a r w -> r a w"),
+            )
+        nc.scalar.activation(out=warm[:, 4:5], in_=warm[:, 0:1], func=ACT.Tanh)
+        nc.gpsimd.dma_start(out=vec_rows[0:8, :], in_=wgo[0].rearrange("(c p) -> c p", p=P))
+        nc.gpsimd.dma_start(out=vec_rows[8:12, :], in_=bn.rearrange("(c p) -> c p", p=P))
+        for q in range(4):
+            nc.gpsimd.dma_start(
+                out=un_s[32 * q : 32 * q + 4, :], in_=un_scales[0, 4 * q : 4 * q + 4, :].bitcast(I32)
+            )
+
+        turned = psum.tile([P, HALF], F32, name="back", bufs=3)
+        nc.tensor.transpose(turned[:, :P], vec_rows[:], ident[:])
+        nc.scalar.copy(out=vec_cols[:, :12], in_=turned[:, :12])
+
+        nc.vector.tensor_copy(out=v_w[:], in_=tab_w[:].bitcast(U32).indirect(offsets[:]))
+        nc.vector.tensor_copy(out=v_s[:], in_=tab_s[:].bitcast(U8).indirect(offsets[:]))
+        load_h(0)
+        load_h(1)
+
+        for a in range(PASSES):
+            interleave(a, 0)
+            quantise(a, 0, QUARTER)
+        for a in range(PASSES):
+            load_x(a, QUARTER, QUARTER)
+        for c in range(OUT_TILES):
+            for c0 in range(0, T, HALF):
+                nc.vector.memset(placed[c][:, c0 : c0 + HALF], 0.0)
+        gather_h(0, 0, QUARTER)
+        gather_h(0, QUARTER, J - QUARTER)
+        load_h(2)
+        update(0, 0, QUARTER)
+        gather_h(1, 0, J)
+        update(1, 0, QUARTER)
+        for a in range(PASSES):
+            interleave(a, QUARTER)
+            quantise(a, QUARTER, QUARTER)
+        for a in range(PASSES):
+            load_x(a, HALF, HALF)
+        load_h(3)
+        gather_h(2, 0, J)
+        update(0, QUARTER, QUARTER)
+        update(1, QUARTER, QUARTER)
+        update(2, 0, HALF)
+        for a in range(PASSES):
+            interleave(a, HALF)
+            interleave(a, HALF + QUARTER)
+            quantise(a, HALF, HALF)
+        gather_h(3, 0, J)
+        for c in range(OUT_TILES):
+            update(c, HALF, HALF)
+            store(c)
+        update(3, 0, HALF)
+        update(3, HALF, HALF)
+        store(3)

@@ -36,38 +36,36 @@ def tile_list_tgn_rnn_kernel(
         psum = ctx.enter_context(tc.psum_pool(name="psum", bufs=2))
 
         offsets = keep.tile([P, J // 16], U16, name="offsets")
-        tab_w = keep.tile([P, T], I32, name="tab_w", tag="window0", align_bytes=64)
-        tab_s = keep.tile([P, T // 4], I32, name="tab_s", tag="window1", align_bytes=64)
+        tab_w = keep.tile([P, T], I32, name="tab_w", tag="slot2", align_bytes=64)
+        tab_s = keep.tile([P, T // 4], I32, name="tab_s", tag="slot5", align_bytes=64)
         v_w = keep.tile([P, J], U32, name="v_w", align_bytes=64)
         v_s = keep.tile([P, J], U8, name="v_s", align_bytes=64)
-        wn_w = keep.tile([P, PASSES, N], I32, name="wn_w", align_bytes=64)
         wn_s = keep.tile([P, PASSES, N // 4], I32, name="wn_s", align_bytes=64)
-        un_w = keep.tile([P, 2 * N], U8, name="un_w", align_bytes=64)
         un_s = keep.tile([P, N // 4], I32, name="un_s", align_bytes=64)
         x_raw = {}
         x_bf = keep.tile([P, PASSES, J, PACK], BF16, name="x_bf", align_bytes=64)
         x_w = keep.tile([P, PASSES, J], U32, name="x_w", align_bytes=64)
         x_s = keep.tile([P, PASSES, J], U8, name="x_s", align_bytes=64)
         h_all = {}
-        h_picked = [keep.tile([P, J], F32, name="h_picked%d" % c) for c in range(N_TILES)]
-        placed = [keep.tile([P, T], F32, name="placed%d" % c) for c in range(OUT_TILES)]
+        h_picked = {}
+        placed = [keep.tile([P, T], F32, name="placed%d" % c) for c in range(OUT_TILES - 1)]
         ident = keep.tile([P, P], F32, name="ident")
         vec_rows = keep.tile([P, P], F32, name="vec_rows")
         vec_cols = keep.tile([P, 16], F32, name="vec_cols")
-        warm = keep.tile([P, 8], F32, name="warm")
+        warm = keep.tile([P, 8], F32, name="warm", tag="slot1", align_bytes=64)
 
         def listed(j0, width):
             return offsets[:, j0 // 16 : (j0 + width) // 16]
 
-        def load_x(a, j0, width):
+        def load_x(a, j0, width, slot):
             rows = x[a * K_PASS : (a + 1) * K_PASS, j0 : j0 + width]
-            raw = keep.tile([P, PACK, width], F32, name="x_raw", bufs=2)
+            raw = keep.tile([P, PACK, width], F32, name="x_raw", tag=slot, align_bytes=64)
             for q0 in range(0, width, QUARTER):
                 x_raw[a, j0 + q0] = raw[:, :, q0 : q0 + QUARTER]
             nc.sync.dma_start(out=raw[:], in_=rows.rearrange("(p i) j -> p i j", i=PACK))
 
-        def load_h(c):
-            h_all[c] = keep.tile([P, T], F32, name="h_all", tag="window%d" % (c % 2), align_bytes=64)
+        def load_h(c, slot):
+            h_all[c] = keep.tile([P, T], F32, name="h_all", tag=slot, align_bytes=64)
             nc.sync.dma_start(out=h_all[c][:], in_=hT[c * P : (c + 1) * P, :])
 
         def interleave(a, j0):
@@ -82,10 +80,11 @@ def tile_list_tgn_rnn_kernel(
                 in_=x_bf[:, a, j0 : j0 + width, :].rearrange("p j i -> p (j i)"),
             )
 
-        def gather_h(c, j0, width):
-            nc.vector.tensor_copy(
-                out=h_picked[c][:, j0 : j0 + width], in_=h_all[c][:].indirect(listed(j0, width))
-            )
+        def gather_h(c, j0, width, slot):
+            picked = keep.tile([P, width], F32, name="picked", tag=slot, align_bytes=64)
+            for b0 in range(0, width, P):
+                h_picked[c, j0 + b0] = picked[:, b0 : b0 + P]
+            nc.vector.tensor_copy(out=picked[:], in_=h_all[c][:].indirect(listed(j0, width)))
 
         def update(c, j0, width):
             cols = slice(c * P, (c + 1) * P)
@@ -97,7 +96,7 @@ def tile_list_tgn_rnn_kernel(
                 for a in range(PASSES):
                     nc.tensor.matmul_mx(
                         out=acc,
-                        lhsT=wn_w[:, a, cols].bitcast(FP8X4),
+                        lhsT=words[:, a * N + c * P : a * N + (c + 1) * P].bitcast(FP8X4),
                         lhsT_scale=wn_s[:].bitcast(U8)[:, a, cols],
                         rhs=x_w[:, a, js].bitcast(FP8X4),
                         rhs_scale=x_s[:, a, js],
@@ -106,7 +105,7 @@ def tile_list_tgn_rnn_kernel(
                     )
                 nc.tensor.matmul_mx(
                     out=acc,
-                    lhsT=un_w[:, 2 * c * P : 2 * (c + 1) * P].bitcast(FP4X4),
+                    lhsT=words[:, PASSES * N :].bitcast(U8)[:, 2 * c * P : 2 * (c + 1) * P].bitcast(FP4X4),
                     lhsT_scale=un_s[:].bitcast(U8)[:, cols],
                     rhs=v_w[:, js].bitcast(FP8X4),
                     rhs_scale=v_s[:, js],
@@ -121,7 +120,7 @@ def tile_list_tgn_rnn_kernel(
             for b0 in range(0, width, P):
                 blk = slice(b0, b0 + P)
                 nc.tensor.matmul(
-                    out=summed[:, blk], lhsT=h_picked[c][:, j0 + b0 : j0 + b0 + P], rhs=ident[:],
+                    out=summed[:, blk], lhsT=h_picked[c, j0 + b0], rhs=ident[:],
                     start=True, stop=False, is_transpose=True,
                 )
                 nc.tensor.matmul(
@@ -147,74 +146,81 @@ def tile_list_tgn_rnn_kernel(
         def store(c):
             nc.sync.dma_start(out=out[c * P : (c + 1) * P, :], in_=placed[c % OUT_TILES][:])
 
-        make_identity(nc, ident[:])
-        nc.gpsimd.memset(tab_s[:], 0)
-        nc.gpsimd.memset(un_s[:], 0)
-        nc.vector.memset(wn_s[:], 0)
-        nc.vector.memset(vec_rows[:], 0.0)
+        nc.vector.memset(tab_s[:], 0)
         nc.vector.memset(warm[:], 0.0)
+        nc.gpsimd.memset(vec_rows[:], 0.0)
+        nc.gpsimd.memset(un_s[:], 0)
 
         nc.sync.dma_start(offsets[:], offs)
         nc.sync.dma_start(out=tab_w[:], in_=tab_words[0].rearrange("p t i -> p (t i)").bitcast(I32))
-        for a in range(PASSES):
-            load_x(a, 0, QUARTER)
-        nc.sync.dma_start(out=wn_w[:], in_=wn_words.rearrange("a p n i -> p a (n i)").bitcast(I32))
-        nc.sync.dma_start(out=un_w[:].bitcast(I32), in_=un_words[0].bitcast(I32))
-        for q in range(4):
-            nc.gpsimd.dma_start(
-                out=tab_s[32 * q : 32 * q + 4, :], in_=tab_scales[0, 4 * q : 4 * q + 4, :].bitcast(I32)
-            )
+        load_x(0, 0, QUARTER, "slot3")
+        load_x(1, 0, QUARTER, "slot4")
         for q in range(4):
             nc.scalar.dma_start(
-                out=wn_s[32 * q : 32 * q + 4, :, :],
-                in_=wn_scales[:, 4 * q : 4 * q + 4, :].bitcast(I32).rearrange("a r w -> r a w"),
+                out=tab_s[32 * q : 32 * q + 4, :], in_=tab_scales[0, 4 * q : 4 * q + 4, :].bitcast(I32)
             )
         nc.scalar.activation(out=warm[:, 4:5], in_=warm[:, 0:1], func=ACT.Tanh)
+        load_h(0, "slot1")
         nc.gpsimd.dma_start(out=vec_rows[0:8, :], in_=wgo[0].rearrange("(c p) -> c p", p=P))
         nc.gpsimd.dma_start(out=vec_rows[8:12, :], in_=bn.rearrange("(c p) -> c p", p=P))
+        make_identity(nc, ident[:])
         for q in range(4):
             nc.gpsimd.dma_start(
                 out=un_s[32 * q : 32 * q + 4, :], in_=un_scales[0, 4 * q : 4 * q + 4, :].bitcast(I32)
             )
 
+        nc.vector.tensor_copy(out=v_s[:], in_=tab_s[:].bitcast(U8).indirect(offsets[:]))
+        nc.vector.tensor_copy(out=v_w[:], in_=tab_w[:].bitcast(U32).indirect(offsets[:]))
+        for c0 in range(0, T, HALF):
+            nc.vector.memset(placed[0][:, c0 : c0 + HALF], 0.0)
+        nc.vector.memset(wn_s[:], 0)
+        for q in range(4):
+            nc.sync.dma_start(
+                out=wn_s[32 * q : 32 * q + 4, :, :],
+                in_=wn_scales[:, 4 * q : 4 * q + 4, :].bitcast(I32).rearrange("a r w -> r a w"),
+            )
+        words = keep.tile([P, PASSES * N + N // 2], I32, name="words", tag="slot5", align_bytes=64)
+        nc.sync.dma_start(
+            out=words[:, : PASSES * N].rearrange("p (a n) -> p a n", a=PASSES),
+            in_=wn_words.rearrange("a p n i -> p a (n i)").bitcast(I32),
+        )
+        nc.sync.dma_start(out=words[:, PASSES * N :], in_=un_words[0].bitcast(I32))
+
         turned = psum.tile([P, HALF], F32, name="back", bufs=3)
         nc.tensor.transpose(turned[:, :P], vec_rows[:], ident[:])
         nc.scalar.copy(out=vec_cols[:, :12], in_=turned[:, :12])
 
-        nc.vector.tensor_copy(out=v_w[:], in_=tab_w[:].bitcast(U32).indirect(offsets[:]))
-        nc.vector.tensor_copy(out=v_s[:], in_=tab_s[:].bitcast(U8).indirect(offsets[:]))
-        load_h(0)
-        load_h(1)
-
         for a in range(PASSES):
             interleave(a, 0)
             quantise(a, 0, QUARTER)
-        for a in range(PASSES):
-            load_x(a, QUARTER, QUARTER)
-        for c in range(OUT_TILES):
+        load_h(1, "slot3")
+        load_x(0, QUARTER, QUARTER, "slot2")
+        load_x(1, QUARTER, QUARTER, "slot4")
+        gather_h(0, 0, QUARTER, "slot6")
+        gather_h(0, QUARTER, J - QUARTER, "picked0")
+        placed.append(keep.tile([P, T], F32, name="placed2", tag="slot1", align_bytes=64))
+        for c in range(1, OUT_TILES):
             for c0 in range(0, T, HALF):
                 nc.vector.memset(placed[c][:, c0 : c0 + HALF], 0.0)
-        gather_h(0, 0, QUARTER)
-        gather_h(0, QUARTER, J - QUARTER)
-        load_h(2)
+        gather_h(1, 0, J, "picked1")
         update(0, 0, QUARTER)
-        gather_h(1, 0, J)
-        update(1, 0, QUARTER)
+        load_h(2, "slot6")
         for a in range(PASSES):
             interleave(a, QUARTER)
             quantise(a, QUARTER, QUARTER)
-        for a in range(PASSES):
-            load_x(a, HALF, HALF)
-        load_h(3)
-        gather_h(2, 0, J)
+        update(1, 0, QUARTER)
+        load_x(0, HALF, HALF, "slot2")
+        load_x(1, HALF, HALF, "slot4")
+        gather_h(2, 0, J, "picked2")
+        load_h(3, "slot6")
         update(0, QUARTER, QUARTER)
         update(1, QUARTER, QUARTER)
-        update(2, 0, HALF)
         for a in range(PASSES):
             interleave(a, HALF)
             interleave(a, HALF + QUARTER)
             quantise(a, HALF, HALF)
-        gather_h(3, 0, J)
+        update(2, 0, HALF)
+        gather_h(3, 0, J, "picked3")
         for c in range(OUT_TILES):
             update(c, HALF, HALF)
             store(c)

@@ -15,6 +15,7 @@ U8 = mybir.dt.uint8
 FP8X4 = mybir.dt.float8_e4m3fn_x4
 FP4X4 = mybir.dt.float4_e2m1fn_x4
 ACT = mybir.ActivationFunctionType
+ALU = mybir.AluOpType
 
 P = 128
 PACK = 4
@@ -32,61 +33,74 @@ def tile_list_tgn_rnn_kernel(
     nc = tc.nc
     with ExitStack() as ctx:
         keep = ctx.enter_context(tc.tile_pool(name="keep", bufs=1))
+        staged = ctx.enter_context(tc.tile_pool(name="staged", bufs=1))
         ring = ctx.enter_context(tc.tile_pool(name="ring", bufs=3))
         psum = ctx.enter_context(tc.psum_pool(name="psum", bufs=2))
 
         offsets = keep.tile([P, J // 16], U16, name="offsets")
-        tab_w = keep.tile([P, T], I32, name="tab_w", tag="slot2", align_bytes=64)
-        tab_s = keep.tile([P, T // 4], I32, name="tab_s", tag="slot5", align_bytes=64)
+        tab_w = keep.tile([P, T], I32, name="tab_w", align_bytes=64)
+        tab_s = keep.tile([P, T // 4], I32, name="tab_s", align_bytes=64)
         v_w = keep.tile([P, J], U32, name="v_w", align_bytes=64)
         v_s = keep.tile([P, J], U8, name="v_s", align_bytes=64)
         wn_s = keep.tile([P, PASSES, N // 4], I32, name="wn_s", align_bytes=64)
-        un_s = keep.tile([P, N // 4], I32, name="un_s", align_bytes=64)
         x_raw = {}
-        x_bf = keep.tile([P, PASSES, J, PACK], BF16, name="x_bf", align_bytes=64)
+        x_bf = {}
         x_w = keep.tile([P, PASSES, J], U32, name="x_w", align_bytes=64)
         x_s = keep.tile([P, PASSES, J], U8, name="x_s", align_bytes=64)
         h_all = {}
         h_picked = {}
+        h_wide = {}
+        weight = {}
         placed = [keep.tile([P, T], F32, name="placed%d" % c) for c in range(OUT_TILES - 1)]
         ident = keep.tile([P, P], F32, name="ident")
-        vec_rows = keep.tile([P, P], F32, name="vec_rows")
+        vec_rows = keep.tile([P, P], F32, name="vec_rows", tag="slot7", align_bytes=64)
         vec_cols = keep.tile([P, 16], F32, name="vec_cols")
-        warm = keep.tile([P, 8], F32, name="warm", tag="slot1", align_bytes=64)
+        warm = staged.tile([P, 76 * 256], F32, name="warm", offset=0, align_bytes=64)
+        un_s = keep.tile([P, N // 4], I32, name="un_s", align_bytes=64)
 
         def listed(j0, width):
             return offsets[:, j0 // 16 : (j0 + width) // 16]
 
-        def load_x(a, j0, width, slot):
+        def load_x(a, j0, width, kib, span=0):
             rows = x[a * K_PASS : (a + 1) * K_PASS, j0 : j0 + width]
-            raw = keep.tile([P, PACK, width], F32, name="x_raw", tag=slot, align_bytes=64)
+            room = staged.tile(
+                [P, max(PACK * width, span * 256)], F32, name="x_raw%d_%d" % (a, j0), offset=kib * 1024, align_bytes=64
+            )
+            raw = room[:, : PACK * width].rearrange("p (i j) -> p i j", i=PACK)
             for q0 in range(0, width, QUARTER):
                 x_raw[a, j0 + q0] = raw[:, :, q0 : q0 + QUARTER]
-            nc.sync.dma_start(out=raw[:], in_=rows.rearrange("(p i) j -> p i j", i=PACK))
+            nc.sync.dma_start(out=raw, in_=rows.rearrange("(p i) j -> p i j", i=PACK))
 
-        def load_h(c, slot):
-            h_all[c] = keep.tile([P, T], F32, name="h_all", tag=slot, align_bytes=64)
+        def load_h(c, kib):
+            h_all[c] = staged.tile([P, T], F32, name="h_all%d" % c, offset=kib * 1024, align_bytes=64)
             nc.sync.dma_start(out=h_all[c][:], in_=hT[c * P : (c + 1) * P, :])
 
         def interleave(a, j0):
-            src = x_raw[a, j0].rearrange("p i (c e) -> p c i e", e=4)
-            dst = x_bf[:, a, j0 : j0 + QUARTER, :].rearrange("p (c e) i -> p c i e", e=4)
+            src = x_raw[a, j0].rearrange("p i j -> p j i")
+            span = j0 if j0 < HALF else HALF
+            if j0 == span:
+                x_bf[a, span] = keep.tile(
+                    [P, QUARTER if j0 < HALF else HALF, PACK], BF16, name="x_bf",
+                    tag="bf%d_%d" % (a, span), align_bytes=64,
+                )
+            dst = x_bf[a, span][:, j0 - span : j0 - span + QUARTER, :]
             nc.scalar.activation(out=dst, in_=src, func=ACT.Copy)
 
         def quantise(a, j0, width):
             nc.vector.quantize_mx(
                 out=x_w[:, a, j0 : j0 + width].bitcast(FP8X4),
                 scales=x_s[:, a, j0 : j0 + width],
-                in_=x_bf[:, a, j0 : j0 + width, :].rearrange("p j i -> p (j i)"),
+                in_=x_bf[a, j0][:].rearrange("p j i -> p (j i)"),
             )
 
         def gather_h(c, j0, width, slot):
             picked = keep.tile([P, width], F32, name="picked", tag=slot, align_bytes=64)
             for b0 in range(0, width, P):
                 h_picked[c, j0 + b0] = picked[:, b0 : b0 + P]
+                h_wide[c, j0 + b0] = picked[:, b0:]
             nc.vector.tensor_copy(out=picked[:], in_=h_all[c][:].indirect(listed(j0, width)))
 
-        def update(c, j0, width):
+        def update(c, j0, width, on_pe=True):
             cols = slice(c * P, (c + 1) * P)
             group = HALF if width == HALF else P
             sn = psum.tile([P, HALF], F32, name="sn")
@@ -112,10 +126,22 @@ def tile_list_tgn_rnn_kernel(
                     start=False,
                     stop=True,
                 )
-            step = ring.tile([P, HALF], F32, name="step")
+            step = ring.tile([P, HALF], F32, name="step", bufs=10)
             nc.scalar.activation(
                 out=step[:, :width], in_=sn[:, :width], func=ACT.Tanh, bias=vec_cols[:, 8 + c : 9 + c]
             )
+            if not on_pe:
+                result = ring.tile([P, HALF], F32, name="added")
+                nc.vector.tensor_tensor(
+                    out=result[:, :width], in0=step[:, :width], in1=h_wide[c, j0][:, :width], op=ALU.add
+                )
+                part = QUARTER if j0 == 0 else width
+                for s0 in range(0, width, part):
+                    nc.vector.tensor_tensor(
+                        out=placed[c % OUT_TILES][:].indirect(listed(j0 + s0, part)),
+                        in0=result[:, s0 : s0 + part], in1=weight[j0 + s0][:, :part], op=ALU.mult,
+                    )
+                return
             summed = psum.tile([P, HALF], F32, name="summed", bufs=3)
             for b0 in range(0, width, P):
                 blk = slice(b0, b0 + P)
@@ -137,93 +163,100 @@ def tile_list_tgn_rnn_kernel(
             back = psum.tile([P, HALF], F32, name="back", bufs=3)
             for b0 in range(0, width, P):
                 nc.tensor.transpose(back[:, b0 : b0 + P], weighted[:, b0 : b0 + P], ident[:])
-            result = ring.tile([P, HALF], F32, name="result")
+            result = ring.tile([P, HALF], F32, name="result", bufs=10)
             nc.scalar.copy(out=result[:, :width], in_=back[:, :width])
             nc.vector.tensor_copy(
                 out=placed[c % OUT_TILES][:].indirect(listed(j0, width)), in_=result[:, :width]
             )
 
+        def load_weight(j0, width, kib):
+            w = staged.tile([P, width], F32, name="w%d" % j0, offset=kib * 1024, align_bytes=64)
+            for q0 in range(0, width, QUARTER):
+                weight[j0 + q0] = w[:, q0:]
+            nc.sync.dma_start(out=w[:], in_=wgo[:, j0 : j0 + width])
+
         def store(c):
             nc.sync.dma_start(out=out[c * P : (c + 1) * P, :], in_=placed[c % OUT_TILES][:])
 
         nc.vector.memset(tab_s[:], 0)
-        nc.vector.memset(warm[:], 0.0)
-        nc.gpsimd.memset(vec_rows[:], 0.0)
-        nc.gpsimd.memset(un_s[:], 0)
+        nc.vector.memset(wn_s[:], 0)
+        nc.vector.memset(un_s[:], 0)
+        nc.vector.memset(vec_rows[:], 0.0)
 
         nc.sync.dma_start(offsets[:], offs)
         nc.sync.dma_start(out=tab_w[:], in_=tab_words[0].rearrange("p t i -> p (t i)").bitcast(I32))
-        load_x(0, 0, QUARTER, "slot3")
-        load_x(1, 0, QUARTER, "slot4")
         for q in range(4):
             nc.scalar.dma_start(
                 out=tab_s[32 * q : 32 * q + 4, :], in_=tab_scales[0, 4 * q : 4 * q + 4, :].bitcast(I32)
             )
-        nc.scalar.activation(out=warm[:, 4:5], in_=warm[:, 0:1], func=ACT.Tanh)
-        load_h(0, "slot1")
-        nc.gpsimd.dma_start(out=vec_rows[0:8, :], in_=wgo[0].rearrange("(c p) -> c p", p=P))
-        nc.gpsimd.dma_start(out=vec_rows[8:12, :], in_=bn.rearrange("(c p) -> c p", p=P))
-        make_identity(nc, ident[:])
-        for q in range(4):
-            nc.gpsimd.dma_start(
-                out=un_s[32 * q : 32 * q + 4, :], in_=un_scales[0, 4 * q : 4 * q + 4, :].bitcast(I32)
-            )
-
-        nc.vector.tensor_copy(out=v_s[:], in_=tab_s[:].bitcast(U8).indirect(offsets[:]))
-        nc.vector.tensor_copy(out=v_w[:], in_=tab_w[:].bitcast(U32).indirect(offsets[:]))
-        for c0 in range(0, T, HALF):
-            nc.vector.memset(placed[0][:, c0 : c0 + HALF], 0.0)
-        nc.vector.memset(wn_s[:], 0)
+        nc.scalar.activation(
+            out=warm[:, 0:1], in_=wn_s[:, 0, 0:1].bitcast(F32), func=ACT.Tanh, bias=un_s[:, 0:1].bitcast(F32)
+        )
+        load_x(0, 0, QUARTER, 18, span=58)
+        load_x(1, 0, QUARTER, 0)
         for q in range(4):
             nc.sync.dma_start(
                 out=wn_s[32 * q : 32 * q + 4, :, :],
                 in_=wn_scales[:, 4 * q : 4 * q + 4, :].bitcast(I32).rearrange("a r w -> r a w"),
             )
-        words = keep.tile([P, PASSES * N + N // 2], I32, name="words", tag="slot5", align_bytes=64)
+        load_h(0, 4)
+        for q in range(4):
+            nc.sync.dma_start(
+                out=un_s[32 * q : 32 * q + 4, :], in_=un_scales[0, 4 * q : 4 * q + 4, :].bitcast(I32)
+            )
+        words = staged.tile([P, PASSES * N + N // 2], I32, name="words", offset=12 * 1024, align_bytes=64)
         nc.sync.dma_start(
             out=words[:, : PASSES * N].rearrange("p (a n) -> p a n", a=PASSES),
             in_=wn_words.rearrange("a p n i -> p a (n i)").bitcast(I32),
         )
         nc.sync.dma_start(out=words[:, PASSES * N :], in_=un_words[0].bitcast(I32))
+        nc.gpsimd.dma_start(out=vec_rows[0:8, :], in_=wgo[0].rearrange("(c p) -> c p", p=P))
+        nc.gpsimd.dma_start(out=vec_rows[8:12, :], in_=bn.rearrange("(c p) -> c p", p=P))
 
-        turned = psum.tile([P, HALF], F32, name="back", bufs=3)
-        nc.tensor.transpose(turned[:, :P], vec_rows[:], ident[:])
-        nc.scalar.copy(out=vec_cols[:, :12], in_=turned[:, :12])
+        make_identity(nc, ident[:])
+        nc.vector.tensor_copy(out=v_s[:], in_=tab_s[:].bitcast(U8).indirect(offsets[:]))
+        nc.vector.tensor_copy(out=v_w[:], in_=tab_w[:].bitcast(U32).indirect(offsets[:]))
 
         for a in range(PASSES):
             interleave(a, 0)
             quantise(a, 0, QUARTER)
-        load_h(1, "slot3")
-        load_x(0, QUARTER, QUARTER, "slot2")
-        load_x(1, QUARTER, QUARTER, "slot4")
+        turned = psum.tile([P, HALF], F32, name="back", bufs=3)
+        nc.tensor.transpose(turned[:, :P], vec_rows[:], ident[:])
+        nc.scalar.copy(out=vec_cols[:, :12], in_=turned[:, :12])
+        load_h(1, 22)
+        load_x(0, QUARTER, QUARTER, 30)
+        load_x(1, QUARTER, QUARTER, 34)
+        load_h(2, 42)
+        load_x(0, HALF, HALF, 50)
+        load_x(1, HALF, HALF, 58)
+        load_h(3, 66)
         gather_h(0, 0, QUARTER, "slot6")
         gather_h(0, QUARTER, J - QUARTER, "picked0")
-        placed.append(keep.tile([P, T], F32, name="placed2", tag="slot1", align_bytes=64))
-        for c in range(1, OUT_TILES):
-            for c0 in range(0, T, HALF):
-                nc.vector.memset(placed[c][:, c0 : c0 + HALF], 0.0)
-        gather_h(1, 0, J, "picked1")
+        for c0 in range(0, T, HALF):
+            nc.vector.memset(placed[0][:, c0 : c0 + HALF].bitcast(I32), 0)
+        for c0 in range(0, T, QUARTER):
+            nc.gpsimd.memset(placed[1][:, c0 : c0 + QUARTER].bitcast(I32), 0)
         update(0, 0, QUARTER)
-        load_h(2, "slot6")
+        gather_h(1, 0, J, "picked1")
+        placed.append(keep.tile([P, T], F32, name="placed2"))
+        for c0 in range(0, T, QUARTER):
+            nc.gpsimd.memset(placed[2][:, c0 : c0 + QUARTER].bitcast(I32), 0)
         for a in range(PASSES):
             interleave(a, QUARTER)
             quantise(a, QUARTER, QUARTER)
-        update(1, 0, QUARTER)
-        load_x(0, HALF, HALF, "slot2")
-        load_x(1, HALF, HALF, "slot4")
-        gather_h(2, 0, J, "picked2")
-        load_h(3, "slot6")
+        update(1, 0, QUARTER, True)
         update(0, QUARTER, QUARTER)
-        update(1, QUARTER, QUARTER)
+        update(1, QUARTER, QUARTER, True)
+        gather_h(2, 0, J, "picked2")
         for a in range(PASSES):
             interleave(a, HALF)
             interleave(a, HALF + QUARTER)
             quantise(a, HALF, HALF)
-        update(2, 0, HALF)
+        update(2, 0, HALF, True)
         gather_h(3, 0, J, "picked3")
         for c in range(OUT_TILES):
-            update(c, HALF, HALF)
+            update(c, HALF, HALF, True)
             store(c)
-        update(3, 0, HALF)
+        update(3, 0, HALF, True)
         update(3, HALF, HALF)
         store(3)

@@ -25,6 +25,8 @@ N_TILES = N // P
 QUARTER = 256
 HALF = 512
 OUT_TILES = 3
+BANK_BYTES = 2048
+BANKS = {"sn": (0, 2), "summed": (2, 3), "back": (5, 3)}
 
 
 def tile_list_tgn_rnn_kernel(
@@ -34,146 +36,155 @@ def tile_list_tgn_rnn_kernel(
     with ExitStack() as ctx:
         keep = ctx.enter_context(tc.tile_pool(name="keep", bufs=1))
         staged = ctx.enter_context(tc.tile_pool(name="staged", bufs=1))
-        ring = ctx.enter_context(tc.tile_pool(name="ring", bufs=3))
-        psum = ctx.enter_context(tc.psum_pool(name="psum", bufs=2))
+        psum = ctx.enter_context(tc.psum_pool(name="psum", bufs=1))
+        banks_used = {"sn": 0, "summed": 0, "back": 0}
+
+        def bank(role):
+            first, count = BANKS[role]
+            n = banks_used[role]
+            banks_used[role] = n + 1
+            return psum.tile([P, HALF], F32, name="%s%d" % (role, n), offset=(first + n % count) * BANK_BYTES)
+
+        def stage(shape, dtype, name, kib):
+            return staged.tile(shape, dtype, name=name, offset=int(kib * 1024), align_bytes=64)
 
         offsets = keep.tile([P, J // 16], U16, name="offsets")
-        tab_w = keep.tile([P, T], I32, name="tab_w", align_bytes=64)
         tab_s = keep.tile([P, T // 4], I32, name="tab_s", align_bytes=64)
         v_w = keep.tile([P, J], U32, name="v_w", align_bytes=64)
         v_s = keep.tile([P, J], U8, name="v_s", align_bytes=64)
+        un_s = keep.tile([P, N // 4], I32, name="un_s", align_bytes=64)
+        x_w = {}
+        x_s = keep.tile([P, PASSES, J], U8, name="x_s", align_bytes=64)
+        placed = [keep.tile([P, T], F32, name="placed0")]
+        ident = keep.tile([P, P], F32, name="ident")
+        vec_rows = keep.tile([P, P], F32, name="vec_rows", align_bytes=64)
+        vec_cols = keep.tile([P, 16], F32, name="vec_cols")
         wn_s = keep.tile([P, PASSES, N // 4], I32, name="wn_s", align_bytes=64)
+        tab_w = keep.tile([P, T], I32, name="tab_w", align_bytes=64)
+        warm = stage([P, 70 * 256], F32, "warm", 4)
         x_raw = {}
         x_bf = {}
-        x_w = keep.tile([P, PASSES, J], U32, name="x_w", align_bytes=64)
-        x_s = keep.tile([P, PASSES, J], U8, name="x_s", align_bytes=64)
         h_all = {}
         h_picked = {}
         h_wide = {}
-        weight = {}
-        placed = [keep.tile([P, T], F32, name="placed%d" % c) for c in range(OUT_TILES - 1)]
-        ident = keep.tile([P, P], F32, name="ident")
-        vec_rows = keep.tile([P, P], F32, name="vec_rows", tag="slot7", align_bytes=64)
-        vec_cols = keep.tile([P, 16], F32, name="vec_cols")
-        warm = staged.tile([P, 76 * 256], F32, name="warm", offset=0, align_bytes=64)
-        un_s = keep.tile([P, N // 4], I32, name="un_s", align_bytes=64)
+        weight = keep.tile([P, HALF], F32, name="weight")
 
         def listed(j0, width):
             return offsets[:, j0 // 16 : (j0 + width) // 16]
 
-        def load_x(a, j0, width, kib, span=0):
+        def load_x(a, j0, width, kib):
             rows = x[a * K_PASS : (a + 1) * K_PASS, j0 : j0 + width]
-            room = staged.tile(
-                [P, max(PACK * width, span * 256)], F32, name="x_raw%d_%d" % (a, j0), offset=kib * 1024, align_bytes=64
-            )
-            raw = room[:, : PACK * width].rearrange("p (i j) -> p i j", i=PACK)
+            raw = stage([P, PACK, width], F32, "x_raw%d_%d" % (a, j0), kib)
             for q0 in range(0, width, QUARTER):
                 x_raw[a, j0 + q0] = raw[:, :, q0 : q0 + QUARTER]
-            nc.sync.dma_start(out=raw, in_=rows.rearrange("(p i) j -> p i j", i=PACK))
+            nc.sync.dma_start(out=raw[:], in_=rows.rearrange("(p i) j -> p i j", i=PACK))
 
         def load_h(c, kib):
-            h_all[c] = staged.tile([P, T], F32, name="h_all%d" % c, offset=kib * 1024, align_bytes=64)
+            h_all[c] = stage([P, T], F32, "h_all%d" % c, kib)
             nc.sync.dma_start(out=h_all[c][:], in_=hT[c * P : (c + 1) * P, :])
 
-        def interleave(a, j0):
-            src = x_raw[a, j0].rearrange("p i j -> p j i")
-            span = j0 if j0 < HALF else HALF
-            if j0 == span:
-                x_bf[a, span] = keep.tile(
-                    [P, QUARTER if j0 < HALF else HALF, PACK], BF16, name="x_bf",
-                    tag="bf%d_%d" % (a, span), align_bytes=64,
-                )
-            dst = x_bf[a, span][:, j0 - span : j0 - span + QUARTER, :]
-            nc.scalar.activation(out=dst, in_=src, func=ACT.Copy)
+        def own(shape, dtype, name, kib):
+            if kib is None:
+                return keep.tile(shape, dtype, name=name, align_bytes=64)
+            return stage(shape, dtype, name, kib)
 
-        def quantise(a, j0, width):
+        def interleave(a, j0, width, kib=None):
+            x_bf[a, j0] = own([P, width, PACK], BF16, "x_bf%d_%d" % (a, j0), kib)
+            for q0 in range(0, width, QUARTER):
+                nc.scalar.activation(
+                    out=x_bf[a, j0][:, q0 : q0 + QUARTER, :],
+                    in_=x_raw[a, j0 + q0].rearrange("p i j -> p j i"),
+                    func=ACT.Copy,
+                )
+
+        def quantise(a, j0, width, kib=None):
+            words = own([P, width], U32, "x_w%d_%d" % (a, j0), kib)
+            for b0 in range(0, width, P):
+                x_w[a, j0 + b0] = words[:, b0:]
             nc.vector.quantize_mx(
-                out=x_w[:, a, j0 : j0 + width].bitcast(FP8X4),
+                out=words[:].bitcast(FP8X4),
                 scales=x_s[:, a, j0 : j0 + width],
                 in_=x_bf[a, j0][:].rearrange("p j i -> p (j i)"),
             )
 
-        def gather_h(c, j0, width, slot):
-            picked = keep.tile([P, width], F32, name="picked", tag=slot, align_bytes=64)
+        def gather_h(c, j0, width, kib=None):
+            picked = own([P, width], F32, "picked%d_%d" % (c, j0), kib)
             for b0 in range(0, width, P):
                 h_picked[c, j0 + b0] = picked[:, b0 : b0 + P]
                 h_wide[c, j0 + b0] = picked[:, b0:]
             nc.vector.tensor_copy(out=picked[:], in_=h_all[c][:].indirect(listed(j0, width)))
 
-        def update(c, j0, width, on_pe=True):
+        steps = {}
+        weighteds = {}
+
+        def product(c, j0, width, kib=None):
             cols = slice(c * P, (c + 1) * P)
-            group = HALF if width == HALF else P
-            sn = psum.tile([P, HALF], F32, name="sn")
+            group = HALF if (j0, width) == (HALF, HALF) else P
+            sn = bank("sn")
             for g0 in range(0, width, group):
                 js = slice(j0 + g0, j0 + g0 + group)
                 acc = sn[:, g0 : g0 + group]
                 for a in range(PASSES):
                     nc.tensor.matmul_mx(
                         out=acc,
-                        lhsT=words[:, a * N + c * P : a * N + (c + 1) * P].bitcast(FP8X4),
+                        lhsT=wn_w[c][:, a, :].bitcast(FP8X4),
                         lhsT_scale=wn_s[:].bitcast(U8)[:, a, cols],
-                        rhs=x_w[:, a, js].bitcast(FP8X4),
+                        rhs=x_w[a, j0 + g0][:, :group].bitcast(FP8X4),
                         rhs_scale=x_s[:, a, js],
                         start=(a == 0),
                         stop=False,
                     )
                 nc.tensor.matmul_mx(
                     out=acc,
-                    lhsT=words[:, PASSES * N :].bitcast(U8)[:, 2 * c * P : 2 * (c + 1) * P].bitcast(FP4X4),
+                    lhsT=un_w[:].bitcast(U8)[:, 2 * c * P : 2 * (c + 1) * P].bitcast(FP4X4),
                     lhsT_scale=un_s[:].bitcast(U8)[:, cols],
                     rhs=v_w[:, js].bitcast(FP8X4),
                     rhs_scale=v_s[:, js],
                     start=False,
                     stop=True,
                 )
-            step = ring.tile([P, HALF], F32, name="step", bufs=10)
+            step = own([P, width], F32, "step%d_%d" % (c, j0), kib)
+            steps[c, j0] = step
             nc.scalar.activation(
-                out=step[:, :width], in_=sn[:, :width], func=ACT.Tanh, bias=vec_cols[:, 8 + c : 9 + c]
+                out=step[:], in_=sn[:, :width], func=ACT.Tanh, bias=vec_cols[:, 8 + c : 9 + c]
             )
-            if not on_pe:
-                result = ring.tile([P, HALF], F32, name="added")
-                nc.vector.tensor_tensor(
-                    out=result[:, :width], in0=step[:, :width], in1=h_wide[c, j0][:, :width], op=ALU.add
-                )
-                part = QUARTER if j0 == 0 else width
-                for s0 in range(0, width, part):
-                    nc.vector.tensor_tensor(
-                        out=placed[c % OUT_TILES][:].indirect(listed(j0 + s0, part)),
-                        in0=result[:, s0 : s0 + part], in1=weight[j0 + s0][:, :part], op=ALU.mult,
-                    )
-                return
-            summed = psum.tile([P, HALF], F32, name="summed", bufs=3)
+
+        def residual(c, j0, width, kib=None):
+            summed = bank("summed")
             for b0 in range(0, width, P):
                 blk = slice(b0, b0 + P)
                 nc.tensor.matmul(
-                    out=summed[:, blk], lhsT=h_picked[c, j0 + b0], rhs=ident[:],
+                    out=summed[:, blk], lhsT=steps[c, j0][:, blk], rhs=ident[:],
                     start=True, stop=False, is_transpose=True,
                 )
                 nc.tensor.matmul(
-                    out=summed[:, blk], lhsT=step[:, blk], rhs=ident[:],
+                    out=summed[:, blk], lhsT=h_picked[c, j0 + b0], rhs=ident[:],
                     start=False, stop=True, is_transpose=True,
                 )
-            weighted = ring.tile([P, HALF], F32, name="weighted")
+            weighted = own([P, width], F32, "weighted%d_%d" % (c, j0), kib)
+            weighteds[c, j0] = weighted
             for b0 in range(0, width, P):
                 jb = (j0 + b0) // P
                 nc.scalar.activation(
                     out=weighted[:, b0 : b0 + P], in_=summed[:, b0 : b0 + P], func=ACT.Copy,
                     scale=vec_cols[:, jb : jb + 1],
                 )
-            back = psum.tile([P, HALF], F32, name="back", bufs=3)
-            for b0 in range(0, width, P):
-                nc.tensor.transpose(back[:, b0 : b0 + P], weighted[:, b0 : b0 + P], ident[:])
-            result = ring.tile([P, HALF], F32, name="result", bufs=10)
-            nc.scalar.copy(out=result[:, :width], in_=back[:, :width])
-            nc.vector.tensor_copy(
-                out=placed[c % OUT_TILES][:].indirect(listed(j0, width)), in_=result[:, :width]
-            )
 
-        def load_weight(j0, width, kib):
-            w = staged.tile([P, width], F32, name="w%d" % j0, offset=kib * 1024, align_bytes=64)
-            for q0 in range(0, width, QUARTER):
-                weight[j0 + q0] = w[:, q0:]
-            nc.sync.dma_start(out=w[:], in_=wgo[:, j0 : j0 + width])
+        def place(c, j0, width, kib=None):
+            back = bank("back")
+            for b0 in range(0, width, P):
+                nc.tensor.transpose(back[:, b0 : b0 + P], weighteds[c, j0][:, b0 : b0 + P], ident[:])
+            result = own([P, width], F32, "result%d_%d" % (c, j0), kib)
+            nc.scalar.copy(out=result[:], in_=back[:, :width])
+            nc.vector.tensor_copy(out=placed[c % OUT_TILES][:].indirect(listed(j0, width)), in_=result[:])
+
+        def place_directly(c, j0, width, kib=None):
+            added = own([P, width], F32, "added%d_%d" % (c, j0), kib)
+            nc.vector.tensor_tensor(out=added[:], in0=steps[c, j0][:], in1=h_wide[c, j0][:, :width], op=ALU.add)
+            nc.vector.tensor_tensor(
+                out=placed[c % OUT_TILES][:].indirect(listed(j0, width)),
+                in0=added[:], in1=weight[:, j0 : j0 + width], op=ALU.mult,
+            )
 
         def store(c):
             nc.sync.dma_start(out=out[c * P : (c + 1) * P, :], in_=placed[c % OUT_TILES][:])
@@ -181,82 +192,112 @@ def tile_list_tgn_rnn_kernel(
         nc.vector.memset(tab_s[:], 0)
         nc.vector.memset(wn_s[:], 0)
         nc.vector.memset(un_s[:], 0)
-        nc.vector.memset(vec_rows[:], 0.0)
+        nc.gpsimd.memset(vec_rows[:], 0.0)
 
         nc.sync.dma_start(offsets[:], offs)
         nc.sync.dma_start(out=tab_w[:], in_=tab_words[0].rearrange("p t i -> p (t i)").bitcast(I32))
+        load_x(0, 0, QUARTER, 0)
         for q in range(4):
             nc.scalar.dma_start(
                 out=tab_s[32 * q : 32 * q + 4, :], in_=tab_scales[0, 4 * q : 4 * q + 4, :].bitcast(I32)
             )
+        nc.gpsimd.dma_start(out=vec_rows[8:12, :], in_=bn.rearrange("(c p) -> c p", p=P))
+        nc.gpsimd.dma_start(out=vec_rows[0:8, :], in_=wgo[0].rearrange("(c p) -> c p", p=P))
+        make_identity(nc, ident[:])
         nc.scalar.activation(
             out=warm[:, 0:1], in_=wn_s[:, 0, 0:1].bitcast(F32), func=ACT.Tanh, bias=un_s[:, 0:1].bitcast(F32)
         )
-        load_x(0, 0, QUARTER, 18, span=58)
-        load_x(1, 0, QUARTER, 0)
-        for q in range(4):
+
+        def load_un_scales(q):
+            nc.sync.dma_start(
+                out=un_s[32 * q : 32 * q + 4, :], in_=un_scales[0, 4 * q : 4 * q + 4, :].bitcast(I32)
+            )
+
+        def load_wn_scales(q):
             nc.sync.dma_start(
                 out=wn_s[32 * q : 32 * q + 4, :, :],
                 in_=wn_scales[:, 4 * q : 4 * q + 4, :].bitcast(I32).rearrange("a r w -> r a w"),
             )
-        load_h(0, 4)
+
+        wn_w = {}
+
+        def load_wn(c0, c1, kib):
+            words = stage([P, PASSES, (c1 - c0) * P], I32, "wn_w%d" % c0, kib)
+            for c in range(c0, c1):
+                wn_w[c] = words[:, :, (c - c0) * P : (c - c0 + 1) * P]
+            wn_all = wn_words.rearrange("a p n i -> p a (n i)").bitcast(I32)
+            nc.sync.dma_start(out=words[:], in_=wn_all[:, :, c0 * P : c1 * P])
+
+        load_x(1, 0, QUARTER, 4)
+        load_wn_scales(0)
+        load_h(0, 8)
+        load_wn(0, 2, 70)
+        un_w = stage([P, N // 2], I32, "un_w", 69)
+        nc.sync.dma_start(out=un_w[:], in_=un_words[0].bitcast(I32))
+        for q in range(1, 4):
+            load_wn_scales(q)
         for q in range(4):
-            nc.sync.dma_start(
-                out=un_s[32 * q : 32 * q + 4, :], in_=un_scales[0, 4 * q : 4 * q + 4, :].bitcast(I32)
-            )
-        words = staged.tile([P, PASSES * N + N // 2], I32, name="words", offset=12 * 1024, align_bytes=64)
-        nc.sync.dma_start(
-            out=words[:, : PASSES * N].rearrange("p (a n) -> p a n", a=PASSES),
-            in_=wn_words.rearrange("a p n i -> p a (n i)").bitcast(I32),
-        )
-        nc.sync.dma_start(out=words[:, PASSES * N :], in_=un_words[0].bitcast(I32))
-        nc.gpsimd.dma_start(out=vec_rows[0:8, :], in_=wgo[0].rearrange("(c p) -> c p", p=P))
-        nc.gpsimd.dma_start(out=vec_rows[8:12, :], in_=bn.rearrange("(c p) -> c p", p=P))
-
-        make_identity(nc, ident[:])
-        nc.vector.tensor_copy(out=v_s[:], in_=tab_s[:].bitcast(U8).indirect(offsets[:]))
-        nc.vector.tensor_copy(out=v_w[:], in_=tab_w[:].bitcast(U32).indirect(offsets[:]))
-
-        for a in range(PASSES):
-            interleave(a, 0)
-            quantise(a, 0, QUARTER)
-        turned = psum.tile([P, HALF], F32, name="back", bufs=3)
-        nc.tensor.transpose(turned[:, :P], vec_rows[:], ident[:])
-        nc.scalar.copy(out=vec_cols[:, :12], in_=turned[:, :12])
-        load_h(1, 22)
-        load_x(0, QUARTER, QUARTER, 30)
-        load_x(1, QUARTER, QUARTER, 34)
-        load_h(2, 42)
-        load_x(0, HALF, HALF, 50)
-        load_x(1, HALF, HALF, 58)
-        load_h(3, 66)
-        gather_h(0, 0, QUARTER, "slot6")
-        gather_h(0, QUARTER, J - QUARTER, "picked0")
+            load_un_scales(q)
+        load_h(1, 18)
+        load_x(0, QUARTER, QUARTER, 29)
+        load_x(1, QUARTER, QUARTER, 33)
+        load_x(0, HALF, HALF, 45)
+        load_x(1, HALF, HALF, 53)
+        load_wn(2, N_TILES, 72)
+        load_h(2, 37)
+        load_h(3, 61)
         for c0 in range(0, T, HALF):
             nc.vector.memset(placed[0][:, c0 : c0 + HALF].bitcast(I32), 0)
-        for c0 in range(0, T, QUARTER):
-            nc.gpsimd.memset(placed[1][:, c0 : c0 + QUARTER].bitcast(I32), 0)
-        update(0, 0, QUARTER)
-        gather_h(1, 0, J, "picked1")
-        placed.append(keep.tile([P, T], F32, name="placed2"))
-        for c0 in range(0, T, QUARTER):
-            nc.gpsimd.memset(placed[2][:, c0 : c0 + QUARTER].bitcast(I32), 0)
-        for a in range(PASSES):
-            interleave(a, QUARTER)
-            quantise(a, QUARTER, QUARTER)
-        update(1, 0, QUARTER, True)
-        update(0, QUARTER, QUARTER)
-        update(1, QUARTER, QUARTER, True)
-        gather_h(2, 0, J, "picked2")
-        for a in range(PASSES):
-            interleave(a, HALF)
-            interleave(a, HALF + QUARTER)
-            quantise(a, HALF, HALF)
-        update(2, 0, HALF, True)
-        gather_h(3, 0, J, "picked3")
-        for c in range(OUT_TILES):
-            update(c, HALF, HALF, True)
-            store(c)
-        update(3, 0, HALF, True)
-        update(3, HALF, HALF)
-        store(3)
+
+        nc.vector.tensor_copy(out=v_s[:], in_=tab_s[:].bitcast(U8).indirect(offsets[:]))
+        nc.vector.tensor_copy(out=v_w[:], in_=tab_w[:].bitcast(U32).indirect(offsets[:]))
+        turned = bank("back")
+        nc.tensor.transpose(turned[:, :P], vec_rows[:], ident[:])
+        nc.scalar.copy(out=vec_cols[:, :12], in_=turned[:, :12])
+        spread = bank("back")
+        for b in range(HALF // P):
+            nc.tensor.transpose(
+                spread[:, b * P : (b + 1) * P], vec_cols[:, b : b + 1].to_broadcast([P, P]), ident[:]
+            )
+        nc.scalar.copy(out=weight[:], in_=spread[:])
+        interleave(0, 0, QUARTER, 120)
+        quantise(0, 0, QUARTER)
+        interleave(1, 0, QUARTER, 90)
+        quantise(1, 0, QUARTER)
+        for c in range(1, OUT_TILES):
+            placed.append(stage([P, T], F32, "placed%d" % c, 105 + 8 * c))
+            for c0 in range(0, T, QUARTER):
+                nc.gpsimd.memset(placed[c][:, c0 : c0 + QUARTER].bitcast(I32), 0)
+        Q = QUARTER
+        gather_h(0, 0, Q, 90.5)
+        gather_h(0, Q, J - Q, 87.5)
+        product(0, 0, Q, 100)
+        product(1, 0, Q, 81)
+        place_directly(0, 0, Q, 96)
+        gather_h(1, 0, J, 92.5)
+        interleave(0, Q, Q, 98.5)
+        quantise(0, Q, Q, 18)
+        interleave(1, Q, Q, 100.5)
+        quantise(1, Q, Q, 19)
+        place_directly(1, 0, Q, 101)
+        product(0, Q, Q, 82)
+        product(1, Q, Q)
+        place_directly(0, Q, Q)
+        place_directly(1, Q, Q, 110)
+        interleave(0, HALF, HALF, 78)
+        quantise(0, HALF, HALF, 108.5)
+        interleave(1, HALF, HALF, 82)
+        quantise(1, HALF, HALF, 110.5)
+        gather_h(2, 0, J, 79.5)
+        gather_h(3, 0, J, 83.5)
+        late = [(0, HALF, Q), (0, HALF + Q, Q), (1, HALF, HALF)]
+        late = late + [(c, j0, HALF) for c in (2, 3) for j0 in (0, HALF)]
+        product(*late[0])
+        product(*late[1])
+        for n, piece in enumerate(late):
+            residual(*piece)
+            if n + 2 < len(late):
+                product(*late[n + 2])
+            place(*piece)
+            if piece[1] + piece[2] == J:
+                store(piece[0])

@@ -25,8 +25,9 @@ N_TILES = N // P
 QUARTER = 256
 HALF = 512
 OUT_TILES = 3
+DIRECT = HALF + QUARTER
 BANK_BYTES = 2048
-BANKS = {"sn": (0, 2), "summed": (2, 3), "back": (5, 3)}
+BANKS = {"summed": (4, 2), "back": (6, 2)}
 
 
 def tile_list_tgn_rnn_kernel(
@@ -37,7 +38,7 @@ def tile_list_tgn_rnn_kernel(
         keep = ctx.enter_context(tc.tile_pool(name="keep", bufs=1))
         staged = ctx.enter_context(tc.tile_pool(name="staged", bufs=1))
         psum = ctx.enter_context(tc.psum_pool(name="psum", bufs=1))
-        banks_used = {"sn": 0, "summed": 0, "back": 0}
+        banks_used = {"summed": 0, "back": 0}
 
         def bank(role):
             first, count = BANKS[role]
@@ -67,7 +68,7 @@ def tile_list_tgn_rnn_kernel(
         h_all = {}
         h_picked = {}
         h_wide = {}
-        weight = keep.tile([P, HALF], F32, name="weight")
+        weight = keep.tile([P, DIRECT], F32, name="weight")
 
         def listed(j0, width):
             return offsets[:, j0 // 16 : (j0 + width) // 16]
@@ -117,10 +118,10 @@ def tile_list_tgn_rnn_kernel(
         steps = {}
         weighteds = {}
 
-        def product(c, j0, width, kib=None):
+        def product(c, j0, width, sn_bank, kib=None):
             cols = slice(c * P, (c + 1) * P)
             group = HALF if (j0, width) == (HALF, HALF) else P
-            sn = bank("sn")
+            sn = psum.tile([P, HALF], F32, name="sn%d_%d" % (c, j0), offset=sn_bank * BANK_BYTES)
             for g0 in range(0, width, group):
                 js = slice(j0 + g0, j0 + g0 + group)
                 acc = sn[:, g0 : g0 + group]
@@ -254,12 +255,13 @@ def tile_list_tgn_rnn_kernel(
         turned = bank("back")
         nc.tensor.transpose(turned[:, :P], vec_rows[:], ident[:])
         nc.scalar.copy(out=vec_cols[:, :12], in_=turned[:, :12])
-        spread = bank("back")
-        for b in range(HALF // P):
-            nc.tensor.transpose(
-                spread[:, b * P : (b + 1) * P], vec_cols[:, b : b + 1].to_broadcast([P, P]), ident[:]
-            )
-        nc.scalar.copy(out=weight[:], in_=spread[:])
+        for j0 in range(0, DIRECT, HALF):
+            width = min(HALF, DIRECT - j0)
+            spread = bank("back")
+            for b0 in range(0, width, P):
+                b = (j0 + b0) // P
+                nc.tensor.transpose(spread[:, b0 : b0 + P], vec_cols[:, b : b + 1].to_broadcast([P, P]), ident[:])
+            nc.scalar.copy(out=weight[:, j0 : j0 + width], in_=spread[:, :width])
         interleave(0, 0, QUARTER, 120)
         quantise(0, 0, QUARTER)
         interleave(1, 0, QUARTER, 90)
@@ -271,8 +273,8 @@ def tile_list_tgn_rnn_kernel(
         Q = QUARTER
         gather_h(0, 0, Q, 90.5)
         gather_h(0, Q, J - Q, 87.5)
-        product(0, 0, Q, 100)
-        product(1, 0, Q, 81)
+        product(0, 0, Q, 0, 100)
+        product(1, 0, Q, 1, 81)
         place_directly(0, 0, Q, 96)
         gather_h(1, 0, J, 92.5)
         interleave(0, Q, Q, 98.5)
@@ -280,24 +282,32 @@ def tile_list_tgn_rnn_kernel(
         interleave(1, Q, Q, 100.5)
         quantise(1, Q, Q, 19)
         place_directly(1, 0, Q, 101)
-        product(0, Q, Q, 82)
-        product(1, Q, Q)
+        product(0, Q, Q, 0, 82)
+        product(1, Q, Q, 1)
         place_directly(0, Q, Q)
         place_directly(1, Q, Q, 110)
         interleave(0, HALF, HALF, 78)
         quantise(0, HALF, HALF, 108.5)
         interleave(1, HALF, HALF, 82)
         quantise(1, HALF, HALF, 110.5)
+        product(2, 0, HALF, 0, 53)
+        product(3, 0, HALF, 1, 55)
         gather_h(2, 0, J, 79.5)
         gather_h(3, 0, J, 83.5)
-        late = [(0, HALF, Q), (0, HALF + Q, Q), (1, HALF, HALF)]
-        late = late + [(c, j0, HALF) for c in (2, 3) for j0 in (0, HALF)]
-        product(*late[0])
-        product(*late[1])
+        product(0, HALF, Q, 2)
+        product(0, HALF + Q, Q, 3)
+        place_directly(0, HALF, Q)
+        residual(0, HALF + Q, Q)
+        product(1, HALF, HALF, 0)
+        place(0, HALF + Q, Q)
+        store(0)
+        residual(1, HALF, HALF)
+        product(2, HALF, HALF, 1)
+        product(3, HALF, HALF, 2)
+        late = [(1, HALF, HALF)] + [(c, j0, HALF) for c in (2, 3) for j0 in (0, HALF)]
         for n, piece in enumerate(late):
-            residual(*piece)
-            if n + 2 < len(late):
-                product(*late[n + 2])
+            if n + 1 < len(late):
+                residual(*late[n + 1])
             place(*piece)
             if piece[1] + piece[2] == J:
                 store(piece[0])

@@ -26,6 +26,7 @@ QUARTER = 256
 HALF = 512
 OUT_TILES = 3
 DIRECT = HALF + QUARTER
+LINE = 4
 BANK_BYTES = 2048
 BANKS = {"summed": (4, 2), "back": (6, 2)}
 
@@ -55,19 +56,16 @@ def tile_list_tgn_rnn_kernel(
         v_s = keep.tile([P, J], U8, name="v_s", align_bytes=64)
         un_s = keep.tile([P, N // 4], I32, name="un_s", align_bytes=64)
         x_w = {}
-        x_s = keep.tile([P, PASSES, J], U8, name="x_s", align_bytes=64)
+        x_s = {}
         placed = [keep.tile([P, T], F32, name="placed0")]
         ident = keep.tile([P, P], F32, name="ident")
         vec_rows = keep.tile([P, P], F32, name="vec_rows", align_bytes=64)
-        vec_cols = keep.tile([P, 16], F32, name="vec_cols")
         wn_s = keep.tile([P, PASSES, N // 4], I32, name="wn_s", align_bytes=64)
         tab_w = keep.tile([P, T], I32, name="tab_w", align_bytes=64)
         warm = stage([P, 70 * 256], F32, "warm", 4)
         x_raw = {}
-        x_bf = {}
         h_all = {}
         h_picked = {}
-        h_wide = {}
         weight = keep.tile([P, DIRECT], F32, name="weight")
 
         def listed(j0, width):
@@ -89,36 +87,36 @@ def tile_list_tgn_rnn_kernel(
                 return keep.tile(shape, dtype, name=name, align_bytes=64)
             return stage(shape, dtype, name, kib)
 
-        def interleave(a, j0, width, kib=None):
-            x_bf[a, j0] = own([P, width, PACK], BF16, "x_bf%d_%d" % (a, j0), kib)
-            for q0 in range(0, width, QUARTER):
+        def interleave(a, j0, grouped):
+            for q0 in range(0, grouped.shape[1], QUARTER):
                 nc.scalar.activation(
-                    out=x_bf[a, j0][:, q0 : q0 + QUARTER, :],
-                    in_=x_raw[a, j0 + q0].rearrange("p i j -> p j i"),
+                    out=grouped[:, q0 : q0 + QUARTER, :].rearrange("p (g j) i -> p g i j", j=LINE),
+                    in_=x_raw[a, j0 + q0].rearrange("p i (g j) -> p g i j", j=LINE),
                     func=ACT.Copy,
                 )
 
-        def quantise(a, j0, width, kib=None):
-            words = own([P, width], U32, "x_w%d_%d" % (a, j0), kib)
-            for b0 in range(0, width, P):
-                x_w[a, j0 + b0] = words[:, b0:]
+        def quantise(passes, j0, width, kib):
+            name = "%d_%d" % (passes[0], j0)
+            grouped = stage([P, len(passes) * width, PACK], BF16, "x_bf" + name, kib)
+            words = keep.tile([P, len(passes) * width], U32, name="x_w" + name, align_bytes=64)
+            scales = keep.tile([P, len(passes) * width], U8, name="x_s" + name, align_bytes=64)
+            for n, a in enumerate(passes):
+                interleave(a, j0, grouped[:, n * width : (n + 1) * width, :])
+                for b0 in range(0, width, P):
+                    x_w[a, j0 + b0] = words[:, n * width + b0 :]
+                    x_s[a, j0 + b0] = scales[:, n * width + b0 :]
             nc.vector.quantize_mx(
-                out=words[:].bitcast(FP8X4),
-                scales=x_s[:, a, j0 : j0 + width],
-                in_=x_bf[a, j0][:].rearrange("p j i -> p (j i)"),
+                out=words[:].bitcast(FP8X4), scales=scales[:], in_=grouped[:].rearrange("p j i -> p (j i)")
             )
 
-        def gather_h(c, j0, width, kib=None):
-            picked = own([P, width], F32, "picked%d_%d" % (c, j0), kib)
-            for b0 in range(0, width, P):
-                h_picked[c, j0 + b0] = picked[:, b0 : b0 + P]
-                h_wide[c, j0 + b0] = picked[:, b0:]
-            nc.vector.tensor_copy(out=picked[:], in_=h_all[c][:].indirect(listed(j0, width)))
+        def gather_h(c, picked):
+            h_picked[c] = picked
+            nc.vector.tensor_copy(out=picked, in_=h_all[c][:].indirect(offsets[:]))
 
         steps = {}
         weighteds = {}
 
-        def product(c, j0, width, sn_bank, kib=None):
+        def product(c, j0, width, sn_bank, step):
             cols = slice(c * P, (c + 1) * P)
             group = HALF if (j0, width) == (HALF, HALF) else P
             sn = psum.tile([P, HALF], F32, name="sn%d_%d" % (c, j0), offset=sn_bank * BANK_BYTES)
@@ -131,7 +129,7 @@ def tile_list_tgn_rnn_kernel(
                         lhsT=wn_w[c][:, a, :].bitcast(FP8X4),
                         lhsT_scale=wn_s[:].bitcast(U8)[:, a, cols],
                         rhs=x_w[a, j0 + g0][:, :group].bitcast(FP8X4),
-                        rhs_scale=x_s[:, a, js],
+                        rhs_scale=x_s[a, j0 + g0][:, :group],
                         start=(a == 0),
                         stop=False,
                     )
@@ -144,10 +142,9 @@ def tile_list_tgn_rnn_kernel(
                     start=False,
                     stop=True,
                 )
-            step = own([P, width], F32, "step%d_%d" % (c, j0), kib)
             steps[c, j0] = step
             nc.scalar.activation(
-                out=step[:], in_=sn[:, :width], func=ACT.Tanh, bias=vec_cols[:, 8 + c : 9 + c]
+                out=step, in_=sn[:, :width], func=ACT.Tanh, bias=vec_cols[:, 8 + c : 9 + c]
             )
 
         def residual(c, j0, width, kib=None):
@@ -159,7 +156,7 @@ def tile_list_tgn_rnn_kernel(
                     start=True, stop=False, is_transpose=True,
                 )
                 nc.tensor.matmul(
-                    out=summed[:, blk], lhsT=h_picked[c, j0 + b0], rhs=ident[:],
+                    out=summed[:, blk], lhsT=h_picked[c][:, j0 + b0 : j0 + b0 + P], rhs=ident[:],
                     start=False, stop=True, is_transpose=True,
                 )
             weighted = own([P, width], F32, "weighted%d_%d" % (c, j0), kib)
@@ -179,16 +176,30 @@ def tile_list_tgn_rnn_kernel(
             nc.scalar.copy(out=result[:], in_=back[:, :width])
             nc.vector.tensor_copy(out=placed[c % OUT_TILES][:].indirect(listed(j0, width)), in_=result[:])
 
-        def place_directly(c, j0, width, kib=None):
-            added = own([P, width], F32, "added%d_%d" % (c, j0), kib)
-            nc.vector.tensor_tensor(out=added[:], in0=steps[c, j0][:], in1=h_wide[c, j0][:, :width], op=ALU.add)
+        def scatter_weighted(c, j0, added):
             nc.vector.tensor_tensor(
-                out=placed[c % OUT_TILES][:].indirect(listed(j0, width)),
-                in0=added[:], in1=weight[:, j0 : j0 + width], op=ALU.mult,
+                out=placed[c][:].indirect(listed(j0, QUARTER)),
+                in0=added, in1=weight[:, j0 : j0 + QUARTER], op=ALU.mult,
             )
 
+        def add_residual(c, j0, kib=None):
+            added = own([P, QUARTER], F32, "added%d_%d" % (c, j0), kib)
+            nc.vector.tensor_tensor(
+                out=added[:], in0=steps[c, j0], in1=h_picked[c][:, j0 : j0 + QUARTER], op=ALU.add
+            )
+            return added[:]
+
+        def tile_f32(name, width, kib=None):
+            return own([P, width], F32, name, kib)[:]
+
         def store(c):
-            nc.sync.dma_start(out=out[c * P : (c + 1) * P, :], in_=placed[c % OUT_TILES][:])
+            rows = out[c * P : (c + 1) * P, :]
+            window = placed[c % OUT_TILES]
+            if c + 1 < N_TILES:
+                nc.sync.dma_start(out=rows, in_=window[:])
+            else:
+                nc.sync.dma_start(out=rows[:, : T // 2], in_=window[:, : T // 2])
+                nc.scalar.dma_start(out=rows[:, T // 2 :], in_=window[:, T // 2 :])
 
         nc.vector.memset(tab_s[:], 0)
         nc.vector.memset(wn_s[:], 0)
@@ -230,13 +241,13 @@ def tile_list_tgn_rnn_kernel(
             nc.sync.dma_start(out=words[:], in_=wn_all[:, :, c0 * P : c1 * P])
 
         load_x(1, 0, QUARTER, 4)
-        load_wn_scales(0)
-        load_h(0, 8)
+        for q in range(3):
+            load_wn_scales(q)
         load_wn(0, 2, 70)
         un_w = stage([P, N // 2], I32, "un_w", 69)
         nc.sync.dma_start(out=un_w[:], in_=un_words[0].bitcast(I32))
-        for q in range(1, 4):
-            load_wn_scales(q)
+        load_wn_scales(3)
+        load_h(0, 8)
         for q in range(4):
             load_un_scales(q)
         load_h(1, 18)
@@ -252,6 +263,9 @@ def tile_list_tgn_rnn_kernel(
 
         nc.vector.tensor_copy(out=v_s[:], in_=tab_s[:].bitcast(U8).indirect(offsets[:]))
         nc.vector.tensor_copy(out=v_w[:], in_=tab_w[:].bitcast(U32).indirect(offsets[:]))
+        quantise([0], 0, QUARTER, 120)
+        quantise([1], 0, QUARTER, 90)
+        vec_cols = stage([P, 16], F32, "vec_cols", 4)
         turned = bank("back")
         nc.tensor.transpose(turned[:, :P], vec_rows[:], ident[:])
         nc.scalar.copy(out=vec_cols[:, :12], in_=turned[:, :12])
@@ -262,49 +276,41 @@ def tile_list_tgn_rnn_kernel(
                 b = (j0 + b0) // P
                 nc.tensor.transpose(spread[:, b0 : b0 + P], vec_cols[:, b : b + 1].to_broadcast([P, P]), ident[:])
             nc.scalar.copy(out=weight[:, j0 : j0 + width], in_=spread[:, :width])
-        interleave(0, 0, QUARTER, 120)
-        quantise(0, 0, QUARTER)
-        interleave(1, 0, QUARTER, 90)
-        quantise(1, 0, QUARTER)
         for c in range(1, OUT_TILES):
             placed.append(stage([P, T], F32, "placed%d" % c, 105 + 8 * c))
             for c0 in range(0, T, QUARTER):
                 nc.gpsimd.memset(placed[c][:, c0 : c0 + QUARTER].bitcast(I32), 0)
         Q = QUARTER
-        gather_h(0, 0, Q, 90.5)
-        gather_h(0, Q, J - Q, 87.5)
-        product(0, 0, Q, 0, 100)
-        product(1, 0, Q, 1, 81)
-        place_directly(0, 0, Q, 96)
-        gather_h(1, 0, J, 92.5)
-        interleave(0, Q, Q, 98.5)
-        quantise(0, Q, Q, 18)
-        interleave(1, Q, Q, 100.5)
-        quantise(1, Q, Q, 19)
-        place_directly(1, 0, Q, 101)
-        product(0, Q, Q, 0, 82)
-        product(1, Q, Q, 1)
-        place_directly(0, Q, Q)
-        place_directly(1, Q, Q, 110)
-        interleave(0, HALF, HALF, 78)
-        quantise(0, HALF, HALF, 108.5)
-        interleave(1, HALF, HALF, 82)
-        quantise(1, HALF, HALF, 110.5)
-        product(2, 0, HALF, 0, 53)
-        product(3, 0, HALF, 1, 55)
-        gather_h(2, 0, J, 79.5)
-        gather_h(3, 0, J, 83.5)
-        product(0, HALF, Q, 2)
-        product(0, HALF + Q, Q, 3)
-        place_directly(0, HALF, Q)
+        gather_h(0, tile_f32("picked0", J, 88))
+        product(0, 0, Q, 0, tile_f32("step0_0", Q, 97.5))
+        product(1, 0, Q, 1, tile_f32("step1_0", Q, 79))
+        added = add_residual(0, 0)
+        gather_h(1, tile_f32("picked1", J, 94))
+        scatter_weighted(0, 0, added)
+        quantise([0, 1], Q, Q, 98)
+        scatter_weighted(1, 0, add_residual(1, 0, 98))
+        product(0, Q, Q, 0, tile_f32("step0_1", Q, 82))
+        product(1, Q, Q, 1, tile_f32("step1_1", Q))
+        added = [add_residual(c, Q) for c in range(2)]
+        for c in range(2):
+            scatter_weighted(c, Q, added[c])
+        quantise([0], HALF, HALF, 76)
+        quantise([1], HALF, HALF, 82)
+        product(2, 0, HALF, 0, tile_f32("step2_0", HALF, 53))
+        product(3, 0, HALF, 1, tile_f32("step3_0", HALF, 55))
+        gather_h(2, tile_f32("picked2", J, 82))
+        product(0, HALF, Q, 2, tile_f32("step0_2", Q, 106))
+        product(0, HALF + Q, Q, 3, tile_f32("step0_3", Q))
+        scatter_weighted(0, HALF, add_residual(0, HALF))
+        gather_h(3, tile_f32("picked3", J, 104))
         residual(0, HALF + Q, Q)
-        product(1, HALF, HALF, 0)
+        product(1, HALF, HALF, 0, tile_f32("step1_2", HALF))
         place(0, HALF + Q, Q)
         store(0)
         residual(1, HALF, HALF)
-        product(2, HALF, HALF, 1)
-        product(3, HALF, HALF, 2)
-        late = [(1, HALF, HALF)] + [(c, j0, HALF) for c in (2, 3) for j0 in (0, HALF)]
+        product(2, HALF, HALF, 1, tile_f32("step2_2", HALF))
+        product(3, HALF, HALF, 2, tile_f32("step3_2", HALF))
+        late = [(1, HALF, HALF)] + [(c, j0, HALF) for j0 in (0, HALF) for c in (2, 3)]
         for n, piece in enumerate(late):
             if n + 1 < len(late):
                 residual(*late[n + 1])

@@ -62,7 +62,7 @@ def tile_list_tgn_rnn_kernel(
         vec_rows = keep.tile([P, P], F32, name="vec_rows", align_bytes=64)
         wn_s = keep.tile([P, PASSES, N // 4], I32, name="wn_s", align_bytes=64)
         tab_w = keep.tile([P, T], I32, name="tab_w", align_bytes=64)
-        warm = stage([P, 70 * 256], F32, "warm", 4)
+        warm = stage([P, 74 * 256], F32, "warm", 0)
         x_raw = {}
         h_all = {}
         h_picked = {}
@@ -208,9 +208,8 @@ def tile_list_tgn_rnn_kernel(
 
         nc.sync.dma_start(offsets[:], offs)
         nc.sync.dma_start(out=tab_w[:], in_=tab_words[0].rearrange("p t i -> p (t i)").bitcast(I32))
-        load_x(0, 0, QUARTER, 0)
         for q in range(4):
-            nc.scalar.dma_start(
+            nc.sync.dma_start(
                 out=tab_s[32 * q : 32 * q + 4, :], in_=tab_scales[0, 4 * q : 4 * q + 4, :].bitcast(I32)
             )
         nc.gpsimd.dma_start(out=vec_rows[8:12, :], in_=bn.rearrange("(c p) -> c p", p=P))
@@ -240,16 +239,18 @@ def tile_list_tgn_rnn_kernel(
             wn_all = wn_words.rearrange("a p n i -> p a (n i)").bitcast(I32)
             nc.sync.dma_start(out=words[:], in_=wn_all[:, :, c0 * P : c1 * P])
 
-        load_x(1, 0, QUARTER, 4)
-        for q in range(3):
+        for q in range(2):
             load_wn_scales(q)
+        load_x(0, 0, QUARTER, 0)
+        load_x(1, 0, QUARTER, 4)
+        for q in range(2, 4):
+            load_wn_scales(q)
+        for q in range(4):
+            load_un_scales(q)
+        load_h(0, 8)
         load_wn(0, 2, 70)
         un_w = stage([P, N // 2], I32, "un_w", 69)
         nc.sync.dma_start(out=un_w[:], in_=un_words[0].bitcast(I32))
-        load_wn_scales(3)
-        load_h(0, 8)
-        for q in range(4):
-            load_un_scales(q)
         load_h(1, 18)
         load_x(0, QUARTER, QUARTER, 29)
         load_x(1, QUARTER, QUARTER, 33)
@@ -285,8 +286,8 @@ def tile_list_tgn_rnn_kernel(
         product(0, 0, Q, 0, tile_f32("step0_0", Q, 97.5))
         product(1, 0, Q, 1, tile_f32("step1_0", Q, 79))
         added = add_residual(0, 0)
-        gather_h(1, tile_f32("picked1", J, 94))
         scatter_weighted(0, 0, added)
+        gather_h(1, tile_f32("picked1", J, 94))
         quantise([0, 1], Q, Q, 98)
         scatter_weighted(1, 0, add_residual(1, 0, 98))
         product(0, Q, Q, 0, tile_f32("step0_1", Q, 82))

@@ -25,10 +25,8 @@ N_TILES = N // P
 QUARTER = 256
 HALF = 512
 OUT_TILES = 3
-DIRECT = HALF + QUARTER
 LINE = 4
 BANK_BYTES = 2048
-BANKS = {"summed": (4, 2), "back": (6, 2)}
 
 
 def tile_list_tgn_rnn_kernel(
@@ -39,185 +37,52 @@ def tile_list_tgn_rnn_kernel(
         keep = ctx.enter_context(tc.tile_pool(name="keep", bufs=1))
         staged = ctx.enter_context(tc.tile_pool(name="staged", bufs=1))
         psum = ctx.enter_context(tc.psum_pool(name="psum", bufs=1))
-        banks_used = {"summed": 0, "back": 0}
 
-        def bank(role):
-            first, count = BANKS[role]
-            n = banks_used[role]
-            banks_used[role] = n + 1
-            return psum.tile([P, HALF], F32, name="%s%d" % (role, n), offset=(first + n % count) * BANK_BYTES)
+        def bank(name, n):
+            return psum.tile([P, HALF], F32, name=name, offset=n * BANK_BYTES)
 
         def stage(shape, dtype, name, kib):
             return staged.tile(shape, dtype, name=name, offset=int(kib * 1024), align_bytes=64)
 
+        def own(shape, dtype, name):
+            return keep.tile(shape, dtype, name=name, align_bytes=64)
+
         offsets = keep.tile([P, J // 16], U16, name="offsets")
-        tab_s = keep.tile([P, T // 4], I32, name="tab_s", align_bytes=64)
-        v_w = keep.tile([P, J], U32, name="v_w", align_bytes=64)
-        v_s = keep.tile([P, J], U8, name="v_s", align_bytes=64)
-        un_s = keep.tile([P, N // 4], I32, name="un_s", align_bytes=64)
+        tab_s = own([P, T // 4], I32, "tab_s")
+        wn_s = own([P, PASSES, N // 4], I32, "wn_s")
+        un_s = own([P, N // 4], I32, "un_s")
+        v_s = own([P, J], U8, "v_s")
+        placed = [own([P, T], F32, "placed%d" % c) for c in range(OUT_TILES)]
+        ident = own([P, P], F32, "ident")
+        vec_rows = own([P, P], F32, "vec_rows")
+        vec_cols = own([P, 16], F32, "vec_cols")
+        weight = own([P, J], F32, "weight")
+        steps = [own([P, J], F32, "step%d" % c) for c in range(N_TILES)]
+        warm = stage([P, 69 * 256], F32, "warm", 0)
+        x_raw = {}
         x_w = {}
         x_s = {}
-        placed = [keep.tile([P, T], F32, name="placed0")]
-        ident = keep.tile([P, P], F32, name="ident")
-        vec_rows = keep.tile([P, P], F32, name="vec_rows", align_bytes=64)
-        wn_s = keep.tile([P, PASSES, N // 4], I32, name="wn_s", align_bytes=64)
-        tab_w = keep.tile([P, T], I32, name="tab_w", align_bytes=64)
-        warm = stage([P, 74 * 256], F32, "warm", 0)
-        x_raw = {}
+        v_w = {}
         h_all = {}
-        h_picked = {}
-        weight = keep.tile([P, DIRECT], F32, name="weight")
+        wn_w = {}
+        sums = {}
 
         def listed(j0, width):
             return offsets[:, j0 // 16 : (j0 + width) // 16]
 
-        def load_x(a, j0, width, kib):
-            rows = x[a * K_PASS : (a + 1) * K_PASS, j0 : j0 + width]
-            raw = stage([P, PACK, width], F32, "x_raw%d_%d" % (a, j0), kib)
-            for q0 in range(0, width, QUARTER):
-                x_raw[a, j0 + q0] = raw[:, :, q0 : q0 + QUARTER]
+        def load_x(a, j0, raw):
+            rows = x[a * K_PASS : (a + 1) * K_PASS, j0 : j0 + HALF]
+            x_raw[a, j0] = raw
             nc.sync.dma_start(out=raw[:], in_=rows.rearrange("(p i) j -> p i j", i=PACK))
 
         def load_h(c, kib):
             h_all[c] = stage([P, T], F32, "h_all%d" % c, kib)
             nc.sync.dma_start(out=h_all[c][:], in_=hT[c * P : (c + 1) * P, :])
 
-        def own(shape, dtype, name, kib):
-            if kib is None:
-                return keep.tile(shape, dtype, name=name, align_bytes=64)
-            return stage(shape, dtype, name, kib)
-
-        def interleave(a, j0, grouped):
-            for q0 in range(0, grouped.shape[1], QUARTER):
-                nc.scalar.activation(
-                    out=grouped[:, q0 : q0 + QUARTER, :].rearrange("p (g j) i -> p g i j", j=LINE),
-                    in_=x_raw[a, j0 + q0].rearrange("p i (g j) -> p g i j", j=LINE),
-                    func=ACT.Copy,
-                )
-
-        def quantise(passes, j0, width, kib):
-            name = "%d_%d" % (passes[0], j0)
-            grouped = stage([P, len(passes) * width, PACK], BF16, "x_bf" + name, kib)
-            words = keep.tile([P, len(passes) * width], U32, name="x_w" + name, align_bytes=64)
-            scales = keep.tile([P, len(passes) * width], U8, name="x_s" + name, align_bytes=64)
-            for n, a in enumerate(passes):
-                interleave(a, j0, grouped[:, n * width : (n + 1) * width, :])
-                for b0 in range(0, width, P):
-                    x_w[a, j0 + b0] = words[:, n * width + b0 :]
-                    x_s[a, j0 + b0] = scales[:, n * width + b0 :]
-            nc.vector.quantize_mx(
-                out=words[:].bitcast(FP8X4), scales=scales[:], in_=grouped[:].rearrange("p j i -> p (j i)")
-            )
-
-        def gather_h(c, picked):
-            h_picked[c] = picked
-            nc.vector.tensor_copy(out=picked, in_=h_all[c][:].indirect(offsets[:]))
-
-        steps = {}
-        weighteds = {}
-
-        def product(c, j0, width, sn_bank, step):
-            cols = slice(c * P, (c + 1) * P)
-            group = HALF if (j0, width) == (HALF, HALF) else P
-            sn = psum.tile([P, HALF], F32, name="sn%d_%d" % (c, j0), offset=sn_bank * BANK_BYTES)
-            for g0 in range(0, width, group):
-                js = slice(j0 + g0, j0 + g0 + group)
-                acc = sn[:, g0 : g0 + group]
-                for a in range(PASSES):
-                    nc.tensor.matmul_mx(
-                        out=acc,
-                        lhsT=wn_w[c][:, a, :].bitcast(FP8X4),
-                        lhsT_scale=wn_s[:].bitcast(U8)[:, a, cols],
-                        rhs=x_w[a, j0 + g0][:, :group].bitcast(FP8X4),
-                        rhs_scale=x_s[a, j0 + g0][:, :group],
-                        start=(a == 0),
-                        stop=False,
-                    )
-                nc.tensor.matmul_mx(
-                    out=acc,
-                    lhsT=un_w[:].bitcast(U8)[:, 2 * c * P : 2 * (c + 1) * P].bitcast(FP4X4),
-                    lhsT_scale=un_s[:].bitcast(U8)[:, cols],
-                    rhs=v_w[:, js].bitcast(FP8X4),
-                    rhs_scale=v_s[:, js],
-                    start=False,
-                    stop=True,
-                )
-            steps[c, j0] = step
-            nc.scalar.activation(
-                out=step, in_=sn[:, :width], func=ACT.Tanh, bias=vec_cols[:, 8 + c : 9 + c]
-            )
-
-        def residual(c, j0, width, kib=None):
-            summed = bank("summed")
-            for b0 in range(0, width, P):
-                blk = slice(b0, b0 + P)
-                nc.tensor.matmul(
-                    out=summed[:, blk], lhsT=steps[c, j0][:, blk], rhs=ident[:],
-                    start=True, stop=False, is_transpose=True,
-                )
-                nc.tensor.matmul(
-                    out=summed[:, blk], lhsT=h_picked[c][:, j0 + b0 : j0 + b0 + P], rhs=ident[:],
-                    start=False, stop=True, is_transpose=True,
-                )
-            weighted = own([P, width], F32, "weighted%d_%d" % (c, j0), kib)
-            weighteds[c, j0] = weighted
-            for b0 in range(0, width, P):
-                jb = (j0 + b0) // P
-                nc.scalar.activation(
-                    out=weighted[:, b0 : b0 + P], in_=summed[:, b0 : b0 + P], func=ACT.Copy,
-                    scale=vec_cols[:, jb : jb + 1],
-                )
-
-        def place(c, j0, width, kib=None):
-            back = bank("back")
-            for b0 in range(0, width, P):
-                nc.tensor.transpose(back[:, b0 : b0 + P], weighteds[c, j0][:, b0 : b0 + P], ident[:])
-            result = own([P, width], F32, "result%d_%d" % (c, j0), kib)
-            nc.scalar.copy(out=result[:], in_=back[:, :width])
-            nc.vector.tensor_copy(out=placed[c % OUT_TILES][:].indirect(listed(j0, width)), in_=result[:])
-
-        def scatter_weighted(c, j0, added):
-            nc.vector.tensor_tensor(
-                out=placed[c][:].indirect(listed(j0, QUARTER)),
-                in0=added, in1=weight[:, j0 : j0 + QUARTER], op=ALU.mult,
-            )
-
-        def add_residual(c, j0, kib=None):
-            added = own([P, QUARTER], F32, "added%d_%d" % (c, j0), kib)
-            nc.vector.tensor_tensor(
-                out=added[:], in0=steps[c, j0], in1=h_picked[c][:, j0 : j0 + QUARTER], op=ALU.add
-            )
-            return added[:]
-
-        def tile_f32(name, width, kib=None):
-            return own([P, width], F32, name, kib)[:]
-
-        def store(c):
-            rows = out[c * P : (c + 1) * P, :]
-            window = placed[c % OUT_TILES]
-            if c + 1 < N_TILES:
-                nc.sync.dma_start(out=rows, in_=window[:])
-            else:
-                nc.sync.dma_start(out=rows[:, : T // 2], in_=window[:, : T // 2])
-                nc.scalar.dma_start(out=rows[:, T // 2 :], in_=window[:, T // 2 :])
-
-        nc.vector.memset(tab_s[:], 0)
-        nc.vector.memset(wn_s[:], 0)
-        nc.vector.memset(un_s[:], 0)
-        nc.gpsimd.memset(vec_rows[:], 0.0)
-
-        nc.sync.dma_start(offsets[:], offs)
-        nc.sync.dma_start(out=tab_w[:], in_=tab_words[0].rearrange("p t i -> p (t i)").bitcast(I32))
-        for q in range(4):
+        def load_tab_scales(q):
             nc.sync.dma_start(
                 out=tab_s[32 * q : 32 * q + 4, :], in_=tab_scales[0, 4 * q : 4 * q + 4, :].bitcast(I32)
             )
-        nc.gpsimd.dma_start(out=vec_rows[8:12, :], in_=bn.rearrange("(c p) -> c p", p=P))
-        nc.gpsimd.dma_start(out=vec_rows[0:8, :], in_=wgo[0].rearrange("(c p) -> c p", p=P))
-        make_identity(nc, ident[:])
-        nc.scalar.activation(
-            out=warm[:, 0:1], in_=wn_s[:, 0, 0:1].bitcast(F32), func=ACT.Tanh, bias=un_s[:, 0:1].bitcast(F32)
-        )
 
         def load_un_scales(q):
             nc.sync.dma_start(
@@ -230,8 +95,6 @@ def tile_list_tgn_rnn_kernel(
                 in_=wn_scales[:, 4 * q : 4 * q + 4, :].bitcast(I32).rearrange("a r w -> r a w"),
             )
 
-        wn_w = {}
-
         def load_wn(c0, c1, kib):
             words = stage([P, PASSES, (c1 - c0) * P], I32, "wn_w%d" % c0, kib)
             for c in range(c0, c1):
@@ -239,82 +102,148 @@ def tile_list_tgn_rnn_kernel(
             wn_all = wn_words.rearrange("a p n i -> p a (n i)").bitcast(I32)
             nc.sync.dma_start(out=words[:], in_=wn_all[:, :, c0 * P : c1 * P])
 
-        for q in range(2):
-            load_wn_scales(q)
-        load_x(0, 0, QUARTER, 0)
-        load_x(1, 0, QUARTER, 4)
-        for q in range(2, 4):
-            load_wn_scales(q)
+        def quantise(a, j0):
+            name = "%d_%d" % (a, j0)
+            grouped = own([P, HALF, PACK], BF16, "x_bf" + name)
+            x_w[a, j0] = own([P, HALF], U32, "x_w" + name)
+            x_s[a, j0] = own([P, HALF], U8, "x_s" + name)
+            nc.scalar.activation(
+                out=grouped[:].rearrange("p (g j) i -> p g i j", j=LINE),
+                in_=x_raw[a, j0][:].rearrange("p i (g j) -> p g i j", j=LINE),
+                func=ACT.Copy,
+            )
+            nc.vector.quantize_mx(
+                out=x_w[a, j0][:].bitcast(FP8X4),
+                scales=x_s[a, j0][:],
+                in_=grouped[:].rearrange("p j i -> p (j i)"),
+            )
+
+        def gather_words(j0):
+            v_w[j0] = own([P, HALF], U32, "v_w%d" % j0)
+            nc.vector.tensor_copy(out=v_w[j0][:], in_=tab_w[:].bitcast(U32).indirect(listed(j0, HALF)))
+
+        def product(c, j0):
+            cols = slice(c * P, (c + 1) * P)
+            sn = bank("sn%d_%d" % (c, j0), c + N_TILES * (j0 // HALF))
+            for a in range(PASSES):
+                nc.tensor.matmul_mx(
+                    out=sn[:],
+                    lhsT=wn_w[c][:, a, :].bitcast(FP8X4),
+                    lhsT_scale=wn_s[:].bitcast(U8)[:, a, cols],
+                    rhs=x_w[a, j0][:].bitcast(FP8X4),
+                    rhs_scale=x_s[a, j0][:],
+                    start=(a == 0),
+                    stop=False,
+                )
+            nc.tensor.matmul_mx(
+                out=sn[:],
+                lhsT=un_w[:].bitcast(U8)[:, 2 * c * P : 2 * (c + 1) * P].bitcast(FP4X4),
+                lhsT_scale=un_s[:].bitcast(U8)[:, cols],
+                rhs=v_w[j0][:].bitcast(FP8X4),
+                rhs_scale=v_s[:, j0 : j0 + HALF],
+                start=False,
+                stop=True,
+            )
+            nc.scalar.activation(
+                out=steps[c][:, j0 : j0 + HALF], in_=sn[:], func=ACT.Tanh, bias=vec_cols[:, 8 + c : 9 + c]
+            )
+
+        def add_state(c, j0, width):
+            sums[c, j0] = own([P, width], F32, "sum%d_%d" % (c, j0))
+            nc.vector.tensor_tensor(
+                out=sums[c, j0][:],
+                in0=h_all[c][:].indirect(listed(j0, width)),
+                in1=steps[c][:, j0 : j0 + width],
+                op=ALU.add,
+            )
+
+        def place(c, j0, width):
+            window = placed[c % OUT_TILES]
+            nc.vector.tensor_tensor(
+                out=window[:].indirect(listed(j0, width)),
+                in0=sums[c, j0][:],
+                in1=weight[:, j0 : j0 + width],
+                op=ALU.mult,
+            )
+            if j0 + width == J:
+                rows = out[c * P : (c + 1) * P, :]
+                if c + 1 < N_TILES:
+                    nc.sync.dma_start(out=rows, in_=window[:])
+                else:
+                    nc.sync.dma_start(out=rows[:, : T // 2], in_=window[:, : T // 2])
+                    nc.scalar.dma_start(out=rows[:, T // 2 :], in_=window[:, T // 2 :])
+
+        nc.vector.memset(tab_s[:], 0)
+        nc.vector.memset(wn_s[:], 0)
+        nc.vector.memset(un_s[:], 0)
+        nc.gpsimd.memset(vec_rows[:], 0.0)
+
+        nc.sync.dma_start(offsets[:], offs)
+        load_x(0, 0, own([P, PACK, HALF], F32, "x_raw0_0"))
+        nc.gpsimd.dma_start(out=vec_rows[8:12, :], in_=bn.rearrange("(c p) -> c p", p=P))
+        nc.gpsimd.dma_start(out=vec_rows[0:8, :], in_=wgo[0].rearrange("(c p) -> c p", p=P))
+        make_identity(nc, ident[:])
+        nc.scalar.activation(
+            out=warm[:, 0:1],
+            in_=wn_s[:, 0, 0:1].bitcast(F32),
+            func=ACT.Tanh,
+            bias=un_s[:, 0:1].bitcast(F32),
+        )
+
+        for q in range(4):
+            load_tab_scales(q)
+        load_x(1, 0, stage([P, PACK, HALF], F32, "x_raw1_0", 0))
+        load_wn_scales(0)
+        load_wn(0, 2, 8)
+        load_wn_scales(1)
+        un_w = stage([P, N // 2], I32, "un_w", 12)
+        nc.sync.dma_start(out=un_w[:], in_=un_words[0].bitcast(I32))
+        load_wn_scales(2)
+        load_wn_scales(3)
+        tab_w = stage([P, T], I32, "tab_w", 13)
+        nc.sync.dma_start(out=tab_w[:], in_=tab_words[0].rearrange("p t i -> p (t i)").bitcast(I32))
         for q in range(4):
             load_un_scales(q)
-        load_h(0, 8)
-        load_wn(0, 2, 70)
-        un_w = stage([P, N // 2], I32, "un_w", 69)
-        nc.sync.dma_start(out=un_w[:], in_=un_words[0].bitcast(I32))
-        load_h(1, 18)
-        load_x(0, QUARTER, QUARTER, 29)
-        load_x(1, QUARTER, QUARTER, 33)
-        load_x(0, HALF, HALF, 45)
-        load_x(1, HALF, HALF, 53)
-        load_wn(2, N_TILES, 72)
-        load_h(2, 37)
+        load_h(0, 21)
+        load_wn(2, N_TILES, 10)
+        load_h(1, 29)
+        load_x(0, HALF, stage([P, PACK, HALF], F32, "x_raw0_1", 37))
+        load_x(1, HALF, stage([P, PACK, HALF], F32, "x_raw1_1", 45))
+        load_h(2, 53)
         load_h(3, 61)
-        for c0 in range(0, T, HALF):
-            nc.vector.memset(placed[0][:, c0 : c0 + HALF].bitcast(I32), 0)
 
+        for window in placed:
+            nc.vector.memset(window[:].bitcast(I32), 0)
         nc.vector.tensor_copy(out=v_s[:], in_=tab_s[:].bitcast(U8).indirect(offsets[:]))
-        nc.vector.tensor_copy(out=v_w[:], in_=tab_w[:].bitcast(U32).indirect(offsets[:]))
-        quantise([0], 0, QUARTER, 120)
-        quantise([1], 0, QUARTER, 90)
-        vec_cols = stage([P, 16], F32, "vec_cols", 4)
-        turned = bank("back")
+        quantise(0, 0)
+        quantise(1, 0)
+        turned = bank("turned", 6)
         nc.tensor.transpose(turned[:, :P], vec_rows[:], ident[:])
         nc.scalar.copy(out=vec_cols[:, :12], in_=turned[:, :12])
-        for j0 in range(0, DIRECT, HALF):
-            width = min(HALF, DIRECT - j0)
-            spread = bank("back")
-            for b0 in range(0, width, P):
+        for j0 in range(0, J, HALF):
+            spread = bank("spread%d" % j0, 4 + j0 // HALF)
+            for b0 in range(0, HALF, P):
                 b = (j0 + b0) // P
                 nc.tensor.transpose(spread[:, b0 : b0 + P], vec_cols[:, b : b + 1].to_broadcast([P, P]), ident[:])
-            nc.scalar.copy(out=weight[:, j0 : j0 + width], in_=spread[:, :width])
-        for c in range(1, OUT_TILES):
-            placed.append(stage([P, T], F32, "placed%d" % c, 105 + 8 * c))
-            for c0 in range(0, T, QUARTER):
-                nc.gpsimd.memset(placed[c][:, c0 : c0 + QUARTER].bitcast(I32), 0)
-        Q = QUARTER
-        gather_h(0, tile_f32("picked0", J, 88))
-        product(0, 0, Q, 0, tile_f32("step0_0", Q, 97.5))
-        product(1, 0, Q, 1, tile_f32("step1_0", Q, 79))
-        added = add_residual(0, 0)
-        scatter_weighted(0, 0, added)
-        gather_h(1, tile_f32("picked1", J, 94))
-        quantise([0, 1], Q, Q, 98)
-        scatter_weighted(1, 0, add_residual(1, 0, 98))
-        product(0, Q, Q, 0, tile_f32("step0_1", Q, 82))
-        product(1, Q, Q, 1, tile_f32("step1_1", Q))
-        added = [add_residual(c, Q) for c in range(2)]
+            nc.scalar.copy(out=weight[:, j0 : j0 + HALF], in_=spread[:])
+        gather_words(0)
+        gather_words(HALF)
+        for c in range(N_TILES):
+            product(c, 0)
         for c in range(2):
-            scatter_weighted(c, Q, added[c])
-        quantise([0], HALF, HALF, 76)
-        quantise([1], HALF, HALF, 82)
-        product(2, 0, HALF, 0, tile_f32("step2_0", HALF, 53))
-        product(3, 0, HALF, 1, tile_f32("step3_0", HALF, 55))
-        gather_h(2, tile_f32("picked2", J, 82))
-        product(0, HALF, Q, 2, tile_f32("step0_2", Q, 106))
-        product(0, HALF + Q, Q, 3, tile_f32("step0_3", Q))
-        scatter_weighted(0, HALF, add_residual(0, HALF))
-        gather_h(3, tile_f32("picked3", J, 104))
-        residual(0, HALF + Q, Q)
-        product(1, HALF, HALF, 0, tile_f32("step1_2", HALF))
-        place(0, HALF + Q, Q)
-        store(0)
-        residual(1, HALF, HALF)
-        product(2, HALF, HALF, 1, tile_f32("step2_2", HALF))
-        product(3, HALF, HALF, 2, tile_f32("step3_2", HALF))
-        late = [(1, HALF, HALF)] + [(c, j0, HALF) for j0 in (0, HALF) for c in (2, 3)]
-        for n, piece in enumerate(late):
-            if n + 1 < len(late):
-                residual(*late[n + 1])
-            place(*piece)
-            if piece[1] + piece[2] == J:
-                store(piece[0])
+            add_state(c, 0, HALF)
+            place(c, 0, HALF)
+        quantise(0, HALF)
+        add_state(2, 0, HALF)
+        quantise(1, HALF)
+        place(2, 0, HALF)
+        for c in range(N_TILES):
+            product(c, HALF)
+        add_state(0, HALF, HALF)
+        add_state(1, HALF, HALF)
+        place(0, HALF, HALF)
+        add_state(2, HALF, HALF)
+        place(1, HALF, HALF)
+        add_state(3, 0, J)
+        place(2, HALF, HALF)
+        place(3, 0, J)

@@ -44,21 +44,21 @@ def tile_list_tgn_rnn_kernel(
         def stage(shape, dtype, name, kib):
             return staged.tile(shape, dtype, name=name, offset=int(kib * 1024), align_bytes=64)
 
-        def own(shape, dtype, name):
-            return keep.tile(shape, dtype, name=name, align_bytes=64)
+        def own(shape, dtype, name, kib=None):
+            if kib is None:
+                return keep.tile(shape, dtype, name=name, align_bytes=64)
+            return stage(shape, dtype, name, kib)
 
         offsets = keep.tile([P, J // 16], U16, name="offsets")
-        tab_s = own([P, T // 4], I32, "tab_s")
-        wn_s = own([P, PASSES, N // 4], I32, "wn_s")
-        un_s = own([P, N // 4], I32, "un_s")
+        tab_s = stage([P, T // 4], I32, "tab_s", 78)
+        w_s = own([P, N // 4], I32, "w_s")
         v_s = own([P, J], U8, "v_s")
-        placed = [own([P, T], F32, "placed%d" % c) for c in range(OUT_TILES)]
+        placed = [own([P, T], F32, "placed0")]
         ident = own([P, P], F32, "ident")
         vec_rows = own([P, P], F32, "vec_rows")
-        vec_cols = own([P, 16], F32, "vec_cols")
-        weight = own([P, J], F32, "weight")
-        steps = [own([P, J], F32, "step%d" % c) for c in range(N_TILES)]
-        warm = stage([P, 69 * 256], F32, "warm", 0)
+        vec_cols = own([P, 16], F32, "vec_cols", 94)
+        steps = {}
+        warm = stage([P, 77 * 256], F32, "warm", 0)
         x_raw = {}
         x_w = {}
         x_s = {}
@@ -79,20 +79,15 @@ def tile_list_tgn_rnn_kernel(
             h_all[c] = stage([P, T], F32, "h_all%d" % c, kib)
             nc.sync.dma_start(out=h_all[c][:], in_=hT[c * P : (c + 1) * P, :])
 
-        def load_tab_scales(q):
-            nc.sync.dma_start(
-                out=tab_s[32 * q : 32 * q + 4, :], in_=tab_scales[0, 4 * q : 4 * q + 4, :].bitcast(I32)
-            )
+        def load_tab_scales(r):
+            nc.sync.dma_start(out=tab_s[r:P:32, :], in_=tab_scales[0, r:16:4, :].bitcast(I32))
 
-        def load_un_scales(q):
-            nc.sync.dma_start(
-                out=un_s[32 * q : 32 * q + 4, :], in_=un_scales[0, 4 * q : 4 * q + 4, :].bitcast(I32)
-            )
+        def load_un_scales(r):
+            nc.sync.dma_start(out=w_s[r:P:32, :], in_=un_scales[0, r:16:4, :].bitcast(I32))
 
         def load_wn_scales(q):
             nc.sync.dma_start(
-                out=wn_s[32 * q : 32 * q + 4, :, :],
-                in_=wn_scales[:, 4 * q : 4 * q + 4, :].bitcast(I32).rearrange("a r w -> r a w"),
+                out=w_s[32 * q + 4 : 32 * q + 12, :], in_=wn_scales[:, 4 * q : 4 * q + 4, :].bitcast(I32)
             )
 
         def load_wn(c0, c1, kib):
@@ -102,16 +97,22 @@ def tile_list_tgn_rnn_kernel(
             wn_all = wn_words.rearrange("a p n i -> p a (n i)").bitcast(I32)
             nc.sync.dma_start(out=words[:], in_=wn_all[:, :, c0 * P : c1 * P])
 
-        def quantise(a, j0):
+        def quantise(a, j0, kib=None, shared=False, bf_kib=None):
             name = "%d_%d" % (a, j0)
-            grouped = own([P, HALF, PACK], BF16, "x_bf" + name)
-            x_w[a, j0] = own([P, HALF], U32, "x_w" + name)
+            grouped = own([P, HALF, PACK], BF16, "x_bf" + name, bf_kib)
+            x_w[a, j0] = own([P, HALF], U32, "x_w" + name, kib)
             x_s[a, j0] = own([P, HALF], U8, "x_s" + name)
+            on_scalar = QUARTER if shared else HALF
             nc.scalar.activation(
-                out=grouped[:].rearrange("p (g j) i -> p g i j", j=LINE),
-                in_=x_raw[a, j0][:].rearrange("p i (g j) -> p g i j", j=LINE),
+                out=grouped[:, :on_scalar, :].rearrange("p (g j) i -> p g i j", j=LINE),
+                in_=x_raw[a, j0][:, :, :on_scalar].rearrange("p i (g j) -> p g i j", j=LINE),
                 func=ACT.Copy,
             )
+            if shared:
+                nc.vector.tensor_copy(
+                    out=grouped[:, on_scalar:, :].rearrange("p (g j) i -> p g i j", j=LINE),
+                    in_=x_raw[a, j0][:, :, on_scalar:].rearrange("p i (g j) -> p g i j", j=LINE),
+                )
             nc.vector.quantize_mx(
                 out=x_w[a, j0][:].bitcast(FP8X4),
                 scales=x_s[a, j0][:],
@@ -122,47 +123,48 @@ def tile_list_tgn_rnn_kernel(
             v_w[j0] = own([P, HALF], U32, "v_w%d" % j0)
             nc.vector.tensor_copy(out=v_w[j0][:], in_=tab_w[:].bitcast(U32).indirect(listed(j0, HALF)))
 
-        def product(c, j0):
+        def product(c, j0, sn_bank, step, bias):
             cols = slice(c * P, (c + 1) * P)
-            sn = bank("sn%d_%d" % (c, j0), c + N_TILES * (j0 // HALF))
-            for a in range(PASSES):
-                nc.tensor.matmul_mx(
-                    out=sn[:],
-                    lhsT=wn_w[c][:, a, :].bitcast(FP8X4),
-                    lhsT_scale=wn_s[:].bitcast(U8)[:, a, cols],
-                    rhs=x_w[a, j0][:].bitcast(FP8X4),
-                    rhs_scale=x_s[a, j0][:],
-                    start=(a == 0),
-                    stop=False,
+            sn = bank("sn%d_%d" % (c, j0), sn_bank)
+            state_pass = (
+                un_w[:].bitcast(U8)[:, 2 * c * P : 2 * (c + 1) * P].bitcast(FP4X4),
+                w_s[:].bitcast(U8)[:, cols],
+                v_w[j0][:].bitcast(FP8X4),
+                v_s[:, j0 : j0 + HALF],
+            )
+            message_passes = [
+                (
+                    wn_w[c][:, a, :].bitcast(FP8X4),
+                    w_s[:].bitcast(U8)[4 + 4 * a :, cols],
+                    x_w[a, j0][:].bitcast(FP8X4),
+                    x_s[a, j0][:],
                 )
-            nc.tensor.matmul_mx(
-                out=sn[:],
-                lhsT=un_w[:].bitcast(U8)[:, 2 * c * P : 2 * (c + 1) * P].bitcast(FP4X4),
-                lhsT_scale=un_s[:].bitcast(U8)[:, cols],
-                rhs=v_w[j0][:].bitcast(FP8X4),
-                rhs_scale=v_s[:, j0 : j0 + HALF],
-                start=False,
-                stop=True,
-            )
-            nc.scalar.activation(
-                out=steps[c][:, j0 : j0 + HALF], in_=sn[:], func=ACT.Tanh, bias=vec_cols[:, 8 + c : 9 + c]
-            )
+                for a in range(PASSES)
+            ]
+            passes = message_passes + [state_pass] if j0 == 0 else [state_pass] + message_passes
+            for n, (w_codes, w_scales, codes, scales) in enumerate(passes):
+                nc.tensor.matmul_mx(
+                    out=sn[:], lhsT=w_codes, lhsT_scale=w_scales, rhs=codes, rhs_scale=scales,
+                    start=(n == 0), stop=(n == PASSES),
+                )
+            steps[c, j0] = step
+            nc.scalar.activation(out=step, in_=sn[:], func=ACT.Tanh, bias=bias[:, c : c + 1])
 
-        def add_state(c, j0, width):
-            sums[c, j0] = own([P, width], F32, "sum%d_%d" % (c, j0))
+        def add_state(c, j0, width, step, kib=None):
+            sums[c, j0] = own([P, width], F32, "sum%d_%d" % (c, j0), kib)
             nc.vector.tensor_tensor(
                 out=sums[c, j0][:],
                 in0=h_all[c][:].indirect(listed(j0, width)),
-                in1=steps[c][:, j0 : j0 + width],
+                in1=step,
                 op=ALU.add,
             )
 
-        def place(c, j0, width):
+        def place(c, j0, width, factor=None):
             window = placed[c % OUT_TILES]
             nc.vector.tensor_tensor(
                 out=window[:].indirect(listed(j0, width)),
                 in0=sums[c, j0][:],
-                in1=weight[:, j0 : j0 + width],
+                in1=weight[:, j0 : j0 + width] if factor is None else factor,
                 op=ALU.mult,
             )
             if j0 + width == J:
@@ -174,8 +176,7 @@ def tile_list_tgn_rnn_kernel(
                     nc.scalar.dma_start(out=rows[:, T // 2 :], in_=window[:, T // 2 :])
 
         nc.vector.memset(tab_s[:], 0)
-        nc.vector.memset(wn_s[:], 0)
-        nc.vector.memset(un_s[:], 0)
+        nc.vector.memset(w_s[:], 0)
         nc.gpsimd.memset(vec_rows[:], 0.0)
 
         nc.sync.dma_start(offsets[:], offs)
@@ -185,65 +186,94 @@ def tile_list_tgn_rnn_kernel(
         make_identity(nc, ident[:])
         nc.scalar.activation(
             out=warm[:, 0:1],
-            in_=wn_s[:, 0, 0:1].bitcast(F32),
+            in_=w_s[:, 0:1].bitcast(F32),
             func=ACT.Tanh,
-            bias=un_s[:, 0:1].bitcast(F32),
         )
 
         for q in range(4):
             load_tab_scales(q)
-        load_x(1, 0, stage([P, PACK, HALF], F32, "x_raw1_0", 0))
         load_wn_scales(0)
-        load_wn(0, 2, 8)
         load_wn_scales(1)
-        un_w = stage([P, N // 2], I32, "un_w", 12)
-        nc.sync.dma_start(out=un_w[:], in_=un_words[0].bitcast(I32))
+        load_x(1, 0, stage([P, PACK, HALF], F32, "x_raw1_0", 0))
         load_wn_scales(2)
         load_wn_scales(3)
-        tab_w = stage([P, T], I32, "tab_w", 13)
+        tab_w = stage([P, T], I32, "tab_w", 17)
         nc.sync.dma_start(out=tab_w[:], in_=tab_words[0].rearrange("p t i -> p (t i)").bitcast(I32))
         for q in range(4):
             load_un_scales(q)
-        load_h(0, 21)
+        load_wn(0, 2, 8)
+        un_w = stage([P, N // 2], I32, "un_w", 12)
+        nc.sync.dma_start(out=un_w[:], in_=un_words[0].bitcast(I32))
+        load_h(0, 29)
+        load_h(1, 37)
+        load_x(0, HALF, stage([P, PACK, HALF], F32, "x_raw0_1", 45))
+        load_x(1, HALF, stage([P, PACK, HALF], F32, "x_raw1_1", 53))
         load_wn(2, N_TILES, 10)
-        load_h(1, 29)
-        load_x(0, HALF, stage([P, PACK, HALF], F32, "x_raw0_1", 37))
-        load_x(1, HALF, stage([P, PACK, HALF], F32, "x_raw1_1", 45))
-        load_h(2, 53)
-        load_h(3, 61)
+        load_h(2, 61)
+        load_h(3, 69)
 
-        for window in placed:
-            nc.vector.memset(window[:].bitcast(I32), 0)
+        nc.vector.memset(placed[0][:].bitcast(I32), 0)
         nc.vector.tensor_copy(out=v_s[:], in_=tab_s[:].bitcast(U8).indirect(offsets[:]))
-        quantise(0, 0)
-        quantise(1, 0)
-        turned = bank("turned", 6)
+        quantise(0, 0, 78)
+        quantise(1, 0, shared=True)
+        turned = bank("turned", 1)
         nc.tensor.transpose(turned[:, :P], vec_rows[:], ident[:])
         nc.scalar.copy(out=vec_cols[:, :12], in_=turned[:, :12])
+        early_bias = stage([P, 32], F32, "early_bias", 84 - 1 / 16)
+        nc.scalar.copy(out=early_bias[:, :4], in_=turned[:, 8:12])
+        weight = stage([P, J], F32, "weight", 0)
+        spreads = []
         for j0 in range(0, J, HALF):
             spread = bank("spread%d" % j0, 4 + j0 // HALF)
+            spreads.append(spread)
             for b0 in range(0, HALF, P):
                 b = (j0 + b0) // P
                 nc.tensor.transpose(spread[:, b0 : b0 + P], vec_cols[:, b : b + 1].to_broadcast([P, P]), ident[:])
             nc.scalar.copy(out=weight[:, j0 : j0 + HALF], in_=spread[:])
         gather_words(0)
         gather_words(HALF)
-        for c in range(N_TILES):
-            product(c, 0)
-        for c in range(2):
-            add_state(c, 0, HALF)
-            place(c, 0, HALF)
-        quantise(0, HALF)
-        add_state(2, 0, HALF)
+        for c in range(1, OUT_TILES):
+            placed.append(own([P, T], F32, "placed%d" % c, 5 + 8 * c))
+            nc.gpsimd.memset(placed[c][:].bitcast(I32), 0)
+        Q = QUARTER
+
+        def second_quarter_weight(name, kib):
+            factor = own([P, Q], F32, name, kib)
+            nc.scalar.copy(out=factor[:], in_=spreads[0][:, Q:])
+            return factor[:]
+
+        product(0, 0, 0, own([P, HALF], F32, "step0_0", 86)[:], early_bias)
+        product(1, 0, 0, own([P, HALF], F32, "step1_0", 88)[:], early_bias)
+        factor = second_quarter_weight("factor0", 84)
+        add_state(0, 0, Q, steps[0, 0][:, :Q])
+        add_state(0, Q, Q, steps[0, 0][:, Q:])
+        place(0, 0, Q)
+        add_state(1, 0, HALF, steps[1, 0], 86)
+        place(0, Q, Q, factor)
+        place(1, 0, HALF)
+        quantise(0, HALF, 88, bf_kib=80)
         quantise(1, HALF)
-        place(2, 0, HALF)
-        for c in range(N_TILES):
-            product(c, HALF)
-        add_state(0, HALF, HALF)
-        add_state(1, HALF, HALF)
+        step3 = own([P, J], F32, "step3", 55)
+        product(2, 0, 0, own([P, HALF], F32, "step2_0", 53)[:], vec_cols[:, 8:12])
+        product(3, 0, 2, step3[:, :HALF], vec_cols[:, 8:12])
+        late_bias = own([P, 32], F32, "late_bias", 94)
+        last_bias = own([P, 8], F32, "last_bias")
+        nc.scalar.copy(out=late_bias[:, :4], in_=turned[:, 8:12])
+        nc.scalar.copy(out=last_bias[:, :4], in_=turned[:, 8:12])
+        add_state(2, 0, Q, steps[2, 0][:, :Q])
+        add_state(2, Q, Q, steps[2, 0][:, Q:])
+        place(2, 0, Q)
+        for c in range(2):
+            product(c, HALF, c, own([P, HALF], F32, "step%d_1" % c)[:], late_bias)
+        factor = second_quarter_weight("factor2", 94 + 1 / 16)
+        product(2, HALF, 2, own([P, HALF], F32, "step2_1")[:], last_bias)
+        product(3, HALF, 0, step3[:, HALF:], last_bias)
+        add_state(0, HALF, HALF, steps[0, HALF], 92 + 1 / 16)
+        place(2, Q, Q, factor)
+        add_state(1, HALF, HALF, steps[1, HALF])
         place(0, HALF, HALF)
-        add_state(2, HALF, HALF)
+        add_state(2, HALF, HALF, steps[2, HALF])
         place(1, HALF, HALF)
-        add_state(3, 0, J)
+        add_state(3, 0, J, step3[:])
         place(2, HALF, HALF)
         place(3, 0, J)

@@ -24,7 +24,6 @@ PASSES = K // K_PASS
 N_TILES = N // P
 QUARTER = 256
 HALF = 512
-OUT_TILES = 3
 LINE = 4
 BANK_BYTES = 2048
 
@@ -56,15 +55,16 @@ def tile_list_tgn_rnn_kernel(
         placed = [own([P, T], F32, "placed0")]
         ident = own([P, P], F32, "ident")
         vec_rows = own([P, P], F32, "vec_rows")
-        vec_cols = own([P, 16], F32, "vec_cols", 94)
+        vec_cols = own([P, 32], F32, "vec_cols", 94)
         steps = {}
-        warm = stage([P, 77 * 256], F32, "warm", 0)
+        warm = stage([P, 78 * 256], F32, "warm", 0)
         x_raw = {}
         x_w = {}
         x_s = {}
         v_w = {}
         h_all = {}
         wn_w = {}
+        un_w = {}
         sums = {}
 
         def listed(j0, width):
@@ -97,6 +97,12 @@ def tile_list_tgn_rnn_kernel(
             wn_all = wn_words.rearrange("a p n i -> p a (n i)").bitcast(I32)
             nc.sync.dma_start(out=words[:], in_=wn_all[:, :, c0 * P : c1 * P])
 
+        def load_un(c0, kib):
+            words = stage([P, P], I32, "un_w%d" % c0, kib)
+            for c in range(c0, c0 + 2):
+                un_w[c] = words[:].bitcast(U8)[:, 2 * (c - c0) * P : 2 * (c - c0 + 1) * P]
+            nc.sync.dma_start(out=words[:], in_=un_words[0].bitcast(I32)[:, c0 * P // 2 : (c0 + 2) * P // 2])
+
         def quantise(a, j0, kib=None, shared=False, bf_kib=None):
             name = "%d_%d" % (a, j0)
             grouped = own([P, HALF, PACK], BF16, "x_bf" + name, bf_kib)
@@ -119,36 +125,46 @@ def tile_list_tgn_rnn_kernel(
                 in_=grouped[:].rearrange("p j i -> p (j i)"),
             )
 
-        def gather_words(j0):
+        def gather_words(j0, width):
             v_w[j0] = own([P, HALF], U32, "v_w%d" % j0)
-            nc.vector.tensor_copy(out=v_w[j0][:], in_=tab_w[:].bitcast(U32).indirect(listed(j0, HALF)))
+            for b0 in range(0, HALF, width):
+                nc.vector.tensor_copy(
+                    out=v_w[j0][:, b0 : b0 + width], in_=tab_w[:].bitcast(U32).indirect(listed(j0 + b0, width))
+                )
 
-        def product(c, j0, sn_bank, step, bias):
+        def product(c, j0, width, sn_bank, step, bias, state_first=True, pass_order=(0, 1)):
             cols = slice(c * P, (c + 1) * P)
+            half, b0 = j0 - j0 % HALF, j0 % HALF
             sn = bank("sn%d_%d" % (c, j0), sn_bank)
-            state_pass = (
-                un_w[:].bitcast(U8)[:, 2 * c * P : 2 * (c + 1) * P].bitcast(FP4X4),
-                w_s[:].bitcast(U8)[:, cols],
-                v_w[j0][:].bitcast(FP8X4),
-                v_s[:, j0 : j0 + HALF],
-            )
+            group = HALF if width == HALF else P
+            state_passes = [
+                (
+                    slice(g0, g0 + group),
+                    un_w[c].bitcast(FP4X4),
+                    w_s[:].bitcast(U8)[:, cols],
+                    v_w[half][:, b0 + g0 : b0 + g0 + group],
+                    v_s[:, j0 + g0 : j0 + g0 + group],
+                )
+                for g0 in range(0, width, group)
+            ]
             message_passes = [
                 (
+                    slice(0, width),
                     wn_w[c][:, a, :].bitcast(FP8X4),
                     w_s[:].bitcast(U8)[4 + 4 * a :, cols],
-                    x_w[a, j0][:].bitcast(FP8X4),
-                    x_s[a, j0][:],
+                    x_w[a, half][:, b0 : b0 + width],
+                    x_s[a, half][:, b0 : b0 + width],
                 )
-                for a in range(PASSES)
+                for a in pass_order
             ]
-            passes = message_passes + [state_pass] if j0 == 0 else [state_pass] + message_passes
-            for n, (w_codes, w_scales, codes, scales) in enumerate(passes):
+            passes = state_passes + message_passes if state_first else message_passes + state_passes
+            for n, (span, w_codes, w_scales, codes, scales) in enumerate(passes):
                 nc.tensor.matmul_mx(
-                    out=sn[:], lhsT=w_codes, lhsT_scale=w_scales, rhs=codes, rhs_scale=scales,
-                    start=(n == 0), stop=(n == PASSES),
+                    out=sn[:, span], lhsT=w_codes, lhsT_scale=w_scales, rhs=codes.bitcast(FP8X4), rhs_scale=scales,
+                    start=(n == 0), stop=(n == len(passes) - 1),
                 )
             steps[c, j0] = step
-            nc.scalar.activation(out=step, in_=sn[:], func=ACT.Tanh, bias=bias[:, c : c + 1])
+            nc.scalar.activation(out=step, in_=sn[:, :width], func=ACT.Tanh, bias=bias[:, c : c + 1])
 
         def add_state(c, j0, width, step, kib=None):
             sums[c, j0] = own([P, width], F32, "sum%d_%d" % (c, j0), kib)
@@ -160,7 +176,7 @@ def tile_list_tgn_rnn_kernel(
             )
 
         def place(c, j0, width, factor=None):
-            window = placed[c % OUT_TILES]
+            window = placed[c]
             nc.vector.tensor_tensor(
                 out=window[:].indirect(listed(j0, width)),
                 in0=sums[c, j0][:],
@@ -201,15 +217,18 @@ def tile_list_tgn_rnn_kernel(
         nc.sync.dma_start(out=tab_w[:], in_=tab_words[0].rearrange("p t i -> p (t i)").bitcast(I32))
         for q in range(4):
             load_un_scales(q)
-        load_wn(0, 2, 8)
-        un_w = stage([P, N // 2], I32, "un_w", 12)
-        nc.sync.dma_start(out=un_w[:], in_=un_words[0].bitcast(I32))
+        load_wn(0, 1, 8)
+        load_un(0, 12)
         load_h(0, 29)
+        load_wn(1, 2, 9)
         load_h(1, 37)
+        early_factor = stage([P, QUARTER], F32, "early_factor", 77)
+        nc.sync.dma_start(out=early_factor[:], in_=wgo[:, QUARTER:HALF])
+        load_wn(2, N_TILES, 10)
+        load_un(2, 12.5)
+        load_h(2, 61)
         load_x(0, HALF, stage([P, PACK, HALF], F32, "x_raw0_1", 45))
         load_x(1, HALF, stage([P, PACK, HALF], F32, "x_raw1_1", 53))
-        load_wn(2, N_TILES, 10)
-        load_h(2, 61)
         load_h(3, 69)
 
         nc.vector.memset(placed[0][:].bitcast(I32), 0)
@@ -219,7 +238,7 @@ def tile_list_tgn_rnn_kernel(
         turned = bank("turned", 1)
         nc.tensor.transpose(turned[:, :P], vec_rows[:], ident[:])
         nc.scalar.copy(out=vec_cols[:, :12], in_=turned[:, :12])
-        early_bias = stage([P, 32], F32, "early_bias", 84 - 1 / 16)
+        early_bias = stage([P, 8], F32, "early_bias", 80)
         nc.scalar.copy(out=early_bias[:, :4], in_=turned[:, 8:12])
         weight = stage([P, J], F32, "weight", 0)
         spreads = []
@@ -230,9 +249,9 @@ def tile_list_tgn_rnn_kernel(
                 b = (j0 + b0) // P
                 nc.tensor.transpose(spread[:, b0 : b0 + P], vec_cols[:, b : b + 1].to_broadcast([P, P]), ident[:])
             nc.scalar.copy(out=weight[:, j0 : j0 + HALF], in_=spread[:])
-        gather_words(0)
-        gather_words(HALF)
-        for c in range(1, OUT_TILES):
+        gather_words(0, QUARTER)
+        gather_words(HALF, HALF)
+        for c in range(1, 3):
             placed.append(own([P, T], F32, "placed%d" % c, 5 + 8 * c))
             nc.gpsimd.memset(placed[c][:].bitcast(I32), 0)
         Q = QUARTER
@@ -242,38 +261,40 @@ def tile_list_tgn_rnn_kernel(
             nc.scalar.copy(out=factor[:], in_=spreads[0][:, Q:])
             return factor[:]
 
-        product(0, 0, 0, own([P, HALF], F32, "step0_0", 86)[:], early_bias)
-        product(1, 0, 0, own([P, HALF], F32, "step1_0", 88)[:], early_bias)
-        factor = second_quarter_weight("factor0", 84)
-        add_state(0, 0, Q, steps[0, 0][:, :Q])
-        add_state(0, Q, Q, steps[0, 0][:, Q:])
+        step0 = own([P, HALF], F32, "step0_0", 86)
+        product(0, 0, Q, 0, step0[:, :Q], early_bias, state_first=False)
+        product(0, Q, Q, 6, step0[:, Q:], early_bias, state_first=False)
+        product(1, 0, HALF, 3, own([P, HALF], F32, "step1_0")[:], early_bias)
+        product(2, 0, HALF, 0, own([P, HALF], F32, "step2_0", 88)[:], early_bias)
+        add_state(0, 0, Q, steps[0, 0], 98)
+        add_state(0, Q, Q, steps[0, Q])
         place(0, 0, Q)
+        placed.append(own([P, T], F32, "placed3", 98))
+        nc.gpsimd.memset(placed[3][:].bitcast(I32), 0)
         add_state(1, 0, HALF, steps[1, 0], 86)
-        place(0, Q, Q, factor)
+        place(0, Q, Q, early_factor[:])
         place(1, 0, HALF)
+        add_state(2, 0, HALF, steps[2, 0])
+        place(2, 0, HALF)
         quantise(0, HALF, 88, bf_kib=80)
         quantise(1, HALF)
-        step3 = own([P, J], F32, "step3", 55)
-        product(2, 0, 0, own([P, HALF], F32, "step2_0", 53)[:], vec_cols[:, 8:12])
-        product(3, 0, 2, step3[:, :HALF], vec_cols[:, 8:12])
-        late_bias = own([P, 32], F32, "late_bias", 94)
         last_bias = own([P, 8], F32, "last_bias")
-        nc.scalar.copy(out=late_bias[:, :4], in_=turned[:, 8:12])
         nc.scalar.copy(out=last_bias[:, :4], in_=turned[:, 8:12])
-        add_state(2, 0, Q, steps[2, 0][:, :Q])
-        add_state(2, Q, Q, steps[2, 0][:, Q:])
-        place(2, 0, Q)
+        product(3, 0, HALF, 6, own([P, HALF], F32, "step3_0", 53)[:], last_bias)
+        add_state(3, 0, Q, steps[3, 0][:, :Q])
+        add_state(3, Q, Q, steps[3, 0][:, Q:])
+        place(3, 0, Q)
         for c in range(2):
-            product(c, HALF, c, own([P, HALF], F32, "step%d_1" % c)[:], late_bias)
-        factor = second_quarter_weight("factor2", 94 + 1 / 16)
-        product(2, HALF, 2, own([P, HALF], F32, "step2_1")[:], last_bias)
-        product(3, HALF, 0, step3[:, HALF:], last_bias)
+            product(c, HALF, HALF, 3 * c, own([P, HALF], F32, "step%d_1" % c)[:], vec_cols[:, 8:12])
+        factor = second_quarter_weight("factor3", 94 + 1 / 16)
+        for c in range(2, N_TILES):
+            product(c, HALF, HALF, 5 * c - 8, own([P, HALF], F32, "step%d_1" % c)[:], last_bias, pass_order=(1, 0))
         add_state(0, HALF, HALF, steps[0, HALF], 92 + 1 / 16)
-        place(2, Q, Q, factor)
+        place(3, Q, Q, factor)
         add_state(1, HALF, HALF, steps[1, HALF])
         place(0, HALF, HALF)
         add_state(2, HALF, HALF, steps[2, HALF])
         place(1, HALF, HALF)
-        add_state(3, 0, J, step3[:])
+        add_state(3, HALF, HALF, steps[3, HALF])
         place(2, HALF, HALF)
-        place(3, 0, J)
+        place(3, HALF, HALF)

@@ -22,7 +22,7 @@ PACK = 4
 K_PASS = P * PACK
 PASSES = K // K_PASS
 N_TILES = N // P
-QUARTER = 256
+Q = 256
 HALF = 512
 LINE = 4
 BANK_BYTES = 2048
@@ -34,49 +34,63 @@ def tile_list_tgn_rnn_kernel(
     nc = tc.nc
     with ExitStack() as ctx:
         keep = ctx.enter_context(tc.tile_pool(name="keep", bufs=1))
-        staged = ctx.enter_context(tc.tile_pool(name="staged", bufs=1))
+        pinned = ctx.enter_context(tc.tile_pool(name="pinned", bufs=1))
         psum = ctx.enter_context(tc.psum_pool(name="psum", bufs=1))
+
+        offsets = keep.tile([P, J // 16], U16, name="offsets")
+        x_first = keep.tile([P, PACK, Q], F32, name="x_first", align_bytes=64)
+        tab_s = pinned.tile([P, T // 4], I32, name="tab_s", offset=12 * 1024, align_bytes=64)
+        w_s = keep.tile([P, N // 4], I32, name="w_s", align_bytes=64)
+        ident = keep.tile([P, P], F32, name="ident", align_bytes=64)
+        vec_rows = keep.tile([P, P], F32, name="vec_rows", align_bytes=64)
+        placed = [keep.tile([P, T], F32, name="placed0", align_bytes=64)]
+
+        nc.sync.dma_start(offsets[:], offs)
+        nc.sync.dma_start(out=x_first[:], in_=x[:K_PASS, :Q].rearrange("(p i) j -> p i j", i=PACK))
+        nc.gpsimd.memset(tab_s[:], 0)
+        nc.vector.memset(w_s[:], 0)
+        nc.vector.memset(vec_rows[:], 0.0)
+        nc.vector.memset(placed[0][:].bitcast(I32), 0)
+        nc.gpsimd.dma_start(out=vec_rows[8:12, :], in_=bn.rearrange("(c p) -> c p", p=P))
+        nc.gpsimd.dma_start(out=vec_rows[0:8, :], in_=wgo[0].rearrange("(c p) -> c p", p=P))
+        make_identity(nc, ident[:])
+
+        work = ctx.enter_context(tc.tile_pool(name="work", bufs=1))
 
         def bank(name, n):
             return psum.tile([P, HALF], F32, name=name, offset=n * BANK_BYTES)
 
-        def stage(shape, dtype, name, kib):
-            return staged.tile(shape, dtype, name=name, offset=int(kib * 1024), align_bytes=64)
-
         def own(shape, dtype, name, kib=None):
             if kib is None:
-                return keep.tile(shape, dtype, name=name, align_bytes=64)
-            return stage(shape, dtype, name, kib)
+                return work.tile(shape, dtype, name=name, align_bytes=64)
+            return pinned.tile(shape, dtype, name=name, offset=int(kib * 1024), align_bytes=64)
 
-        offsets = keep.tile([P, J // 16], U16, name="offsets")
-        tab_s = stage([P, T // 4], I32, "tab_s", 78)
-        w_s = own([P, N // 4], I32, "w_s")
-        v_s = own([P, J], U8, "v_s")
-        placed = [own([P, T], F32, "placed0")]
-        ident = own([P, P], F32, "ident")
-        vec_rows = own([P, P], F32, "vec_rows")
-        vec_cols = own([P, 32], F32, "vec_cols", 94)
-        steps = {}
-        warm = stage([P, 78 * 256], F32, "warm", 0)
-        x_raw = {}
-        x_w = {}
-        x_s = {}
-        v_w = {}
+        x_raw = {(0, 0): x_first}
         h_all = {}
         wn_w = {}
         un_w = {}
+        steps = {}
         sums = {}
+        picked = {}
+        x_w = {(a, j0): own([P, HALF], U32, "x_w%d_%d" % (a, j0)) for a, j0 in ((1, 0), (0, HALF), (1, HALF))}
+        x_w[0, 0] = own([P, HALF], U32, "x_w0_0", 12)
+        x_s = {(a, j0): own([P, HALF], U8, "x_s%d_%d" % (a, j0)) for a in range(PASSES) for j0 in (0, HALF)}
+        v_s = own([P, J], U8, "v_s")
+        v_w = own([P, J], U32, "v_w")
+        vec_cols = own([P, 16], F32, "vec_cols")
+        weight = own([P, J], F32, "weight")
 
         def listed(j0, width):
             return offsets[:, j0 // 16 : (j0 + width) // 16]
 
-        def load_x(a, j0, raw):
-            rows = x[a * K_PASS : (a + 1) * K_PASS, j0 : j0 + HALF]
+        def load_x(a, j0, width, kib=None):
+            raw = own([P, PACK, width], F32, "x_raw%d_%d" % (a, j0), kib)
             x_raw[a, j0] = raw
+            rows = x[a * K_PASS : (a + 1) * K_PASS, j0 : j0 + width]
             nc.sync.dma_start(out=raw[:], in_=rows.rearrange("(p i) j -> p i j", i=PACK))
 
-        def load_h(c, kib):
-            h_all[c] = stage([P, T], F32, "h_all%d" % c, kib)
+        def load_h(c):
+            h_all[c] = own([P, T], F32, "h_all%d" % c)
             nc.sync.dma_start(out=h_all[c][:], in_=hT[c * P : (c + 1) * P, :])
 
         def load_tab_scales(r):
@@ -90,64 +104,51 @@ def tile_list_tgn_rnn_kernel(
                 out=w_s[32 * q + 4 : 32 * q + 12, :], in_=wn_scales[:, 4 * q : 4 * q + 4, :].bitcast(I32)
             )
 
-        def load_wn(c0, c1, kib):
-            words = stage([P, PASSES, (c1 - c0) * P], I32, "wn_w%d" % c0, kib)
-            for c in range(c0, c1):
-                wn_w[c] = words[:, :, (c - c0) * P : (c - c0 + 1) * P]
+        def load_wn(c):
+            wn_w[c] = own([P, PASSES, P], I32, "wn_w%d" % c)
             wn_all = wn_words.rearrange("a p n i -> p a (n i)").bitcast(I32)
-            nc.sync.dma_start(out=words[:], in_=wn_all[:, :, c0 * P : c1 * P])
+            nc.sync.dma_start(out=wn_w[c][:], in_=wn_all[:, :, c * P : (c + 1) * P])
 
-        def load_un(c0, kib):
-            words = stage([P, P], I32, "un_w%d" % c0, kib)
+        def load_un(c0):
+            words = own([P, P], I32, "un_w%d" % c0)
             for c in range(c0, c0 + 2):
                 un_w[c] = words[:].bitcast(U8)[:, 2 * (c - c0) * P : 2 * (c - c0 + 1) * P]
             nc.sync.dma_start(out=words[:], in_=un_words[0].bitcast(I32)[:, c0 * P // 2 : (c0 + 2) * P // 2])
 
-        def quantise(a, j0, kib=None, shared=False, bf_kib=None):
-            name = "%d_%d" % (a, j0)
-            grouped = own([P, HALF, PACK], BF16, "x_bf" + name, bf_kib)
-            x_w[a, j0] = own([P, HALF], U32, "x_w" + name, kib)
-            x_s[a, j0] = own([P, HALF], U8, "x_s" + name)
-            on_scalar = QUARTER if shared else HALF
+        def quantise(a, j0, width, on_scalar):
+            grouped = own([P, width, PACK], BF16, "x_bf%d_%d" % (a, j0))
+            half, b0 = j0 - j0 % HALF, j0 % HALF
             nc.scalar.activation(
                 out=grouped[:, :on_scalar, :].rearrange("p (g j) i -> p g i j", j=LINE),
                 in_=x_raw[a, j0][:, :, :on_scalar].rearrange("p i (g j) -> p g i j", j=LINE),
                 func=ACT.Copy,
             )
-            if shared:
+            if on_scalar < width:
                 nc.vector.tensor_copy(
                     out=grouped[:, on_scalar:, :].rearrange("p (g j) i -> p g i j", j=LINE),
                     in_=x_raw[a, j0][:, :, on_scalar:].rearrange("p i (g j) -> p g i j", j=LINE),
                 )
             nc.vector.quantize_mx(
-                out=x_w[a, j0][:].bitcast(FP8X4),
-                scales=x_s[a, j0][:],
+                out=x_w[a, half][:, b0 : b0 + width].bitcast(FP8X4),
+                scales=x_s[a, half][:, b0 : b0 + width],
                 in_=grouped[:].rearrange("p j i -> p (j i)"),
             )
 
-        def gather_words(j0, width):
-            v_w[j0] = own([P, HALF], U32, "v_w%d" % j0)
-            for b0 in range(0, HALF, width):
-                nc.vector.tensor_copy(
-                    out=v_w[j0][:, b0 : b0 + width], in_=tab_w[:].bitcast(U32).indirect(listed(j0 + b0, width))
-                )
-
-        def product(c, j0, width, sn_bank, step, bias, state_first=True, pass_order=(0, 1)):
+        def product(c, j0, width, sn_bank, step=None):
             cols = slice(c * P, (c + 1) * P)
             half, b0 = j0 - j0 % HALF, j0 % HALF
             sn = bank("sn%d_%d" % (c, j0), sn_bank)
             group = HALF if width == HALF else P
-            state_passes = [
+            passes = [
                 (
                     slice(g0, g0 + group),
                     un_w[c].bitcast(FP4X4),
                     w_s[:].bitcast(U8)[:, cols],
-                    v_w[half][:, b0 + g0 : b0 + g0 + group],
+                    v_w[:, j0 + g0 : j0 + g0 + group],
                     v_s[:, j0 + g0 : j0 + g0 + group],
                 )
                 for g0 in range(0, width, group)
-            ]
-            message_passes = [
+            ] + [
                 (
                     slice(0, width),
                     wn_w[c][:, a, :].bitcast(FP8X4),
@@ -155,24 +156,44 @@ def tile_list_tgn_rnn_kernel(
                     x_w[a, half][:, b0 : b0 + width],
                     x_s[a, half][:, b0 : b0 + width],
                 )
-                for a in pass_order
+                for a in range(PASSES)
             ]
-            passes = state_passes + message_passes if state_first else message_passes + state_passes
             for n, (span, w_codes, w_scales, codes, scales) in enumerate(passes):
                 nc.tensor.matmul_mx(
                     out=sn[:, span], lhsT=w_codes, lhsT_scale=w_scales, rhs=codes.bitcast(FP8X4), rhs_scale=scales,
                     start=(n == 0), stop=(n == len(passes) - 1),
                 )
-            steps[c, j0] = step
-            nc.scalar.activation(out=step, in_=sn[:, :width], func=ACT.Tanh, bias=bias[:, c : c + 1])
+            if step is None:
+                steps[c, j0] = own([P, width], F32, "step%d_%d" % (c, j0))
+                step = steps[c, j0][:]
+            nc.scalar.activation(out=step, in_=sn[:, :width], func=ACT.Tanh, bias=vec_cols[:, 8 + c : 9 + c])
 
-        def add_state(c, j0, width, step, kib=None):
+        def pick_state(c, j0, width, kib=None):
+            rows = own([P, width], F32, "picked%d_%d" % (c, j0), kib)
+            for b0 in range(0, width, P):
+                picked[c, j0 + b0] = rows[:, b0 : b0 + P]
+            nc.vector.tensor_copy(out=rows[:], in_=h_all[c][:].indirect(listed(j0, width)))
+
+        def add_by_turning(c, j0, width, there_bank, back_bank):
+            there = bank("there%d_%d" % (c, j0), there_bank)
+            for b0 in range(0, width, P):
+                terms = (steps[c, j0][:, b0 : b0 + P], picked[c, j0 + b0])
+                for n, term in enumerate(terms):
+                    nc.tensor.matmul(
+                        there[:, b0 : b0 + P], lhsT=term, rhs=ident[:], is_transpose=True, start=(n == 0), stop=(n == 1)
+                    )
+            turned_sum = own([P, width], F32, "turned_sum%d_%d" % (c, j0))
+            nc.scalar.copy(out=turned_sum[:], in_=there[:, :width])
+            back = bank("back%d_%d" % (c, j0), back_bank)
+            for b0 in range(0, width, P):
+                nc.tensor.transpose(back[:, b0 : b0 + P], turned_sum[:, b0 : b0 + P], ident[:])
+            sums[c, j0] = own([P, width], F32, "sum%d_%d" % (c, j0))
+            nc.scalar.copy(out=sums[c, j0][:], in_=back[:, :width])
+
+        def add_state(c, j0, width, kib=None):
             sums[c, j0] = own([P, width], F32, "sum%d_%d" % (c, j0), kib)
             nc.vector.tensor_tensor(
-                out=sums[c, j0][:],
-                in0=h_all[c][:].indirect(listed(j0, width)),
-                in1=step,
-                op=ALU.add,
+                out=sums[c, j0][:], in0=h_all[c][:].indirect(listed(j0, width)), in1=steps[c, j0][:], op=ALU.add
             )
 
         def place(c, j0, width, factor=None):
@@ -183,118 +204,102 @@ def tile_list_tgn_rnn_kernel(
                 in1=weight[:, j0 : j0 + width] if factor is None else factor,
                 op=ALU.mult,
             )
-            if j0 + width == J:
-                rows = out[c * P : (c + 1) * P, :]
-                if c + 1 < N_TILES:
-                    nc.sync.dma_start(out=rows, in_=window[:])
-                else:
-                    nc.sync.dma_start(out=rows[:, : T // 2], in_=window[:, : T // 2])
-                    nc.scalar.dma_start(out=rows[:, T // 2 :], in_=window[:, T // 2 :])
 
-        nc.vector.memset(tab_s[:], 0)
-        nc.vector.memset(w_s[:], 0)
-        nc.gpsimd.memset(vec_rows[:], 0.0)
+        def store(c, last=False):
+            rows = out[c * P : (c + 1) * P, :]
+            if last:
+                nc.sync.dma_start(out=rows[:, : T // 2], in_=placed[c][:, : T // 2])
+                nc.scalar.dma_start(out=rows[:, T // 2 :], in_=placed[c][:, T // 2 :])
+            else:
+                nc.sync.dma_start(out=rows, in_=placed[c][:])
 
-        nc.sync.dma_start(offsets[:], offs)
-        load_x(0, 0, own([P, PACK, HALF], F32, "x_raw0_0"))
-        nc.gpsimd.dma_start(out=vec_rows[8:12, :], in_=bn.rearrange("(c p) -> c p", p=P))
-        nc.gpsimd.dma_start(out=vec_rows[0:8, :], in_=wgo[0].rearrange("(c p) -> c p", p=P))
-        make_identity(nc, ident[:])
-        nc.scalar.activation(
-            out=warm[:, 0:1],
-            in_=w_s[:, 0:1].bitcast(F32),
-            func=ACT.Tanh,
-        )
-
-        for q in range(4):
-            load_tab_scales(q)
-        load_wn_scales(0)
-        load_wn_scales(1)
-        load_x(1, 0, stage([P, PACK, HALF], F32, "x_raw1_0", 0))
-        load_wn_scales(2)
-        load_wn_scales(3)
-        tab_w = stage([P, T], I32, "tab_w", 17)
+        for r in range(4):
+            load_tab_scales(r)
+        tab_w = own([P, T], I32, "tab_w")
         nc.sync.dma_start(out=tab_w[:], in_=tab_words[0].rearrange("p t i -> p (t i)").bitcast(I32))
+        for r in range(4):
+            load_un_scales(r)
+        load_x(1, 0, Q)
+        load_wn(0)
+        load_h(0)
+        load_un(0)
         for q in range(4):
-            load_un_scales(q)
-        load_wn(0, 1, 8)
-        load_un(0, 12)
-        load_h(0, 29)
-        load_wn(1, 2, 9)
-        load_h(1, 37)
-        early_factor = stage([P, QUARTER], F32, "early_factor", 77)
-        nc.sync.dma_start(out=early_factor[:], in_=wgo[:, QUARTER:HALF])
-        load_wn(2, N_TILES, 10)
-        load_un(2, 12.5)
-        load_h(2, 61)
-        load_x(0, HALF, stage([P, PACK, HALF], F32, "x_raw0_1", 45))
-        load_x(1, HALF, stage([P, PACK, HALF], F32, "x_raw1_1", 53))
-        load_h(3, 69)
+            load_wn_scales(q)
+        load_wn(1)
+        load_h(1)
+        load_x(0, Q, Q, 24)
+        load_x(1, Q, Q, 8)
+        load_wn(2)
+        load_un(2)
+        load_h(2)
+        load_wn(3)
+        load_x(0, HALF, HALF)
+        load_h(3)
+        load_x(1, HALF, HALF, 16)
 
-        nc.vector.memset(placed[0][:].bitcast(I32), 0)
-        nc.vector.tensor_copy(out=v_s[:], in_=tab_s[:].bitcast(U8).indirect(offsets[:]))
-        quantise(0, 0, 78)
-        quantise(1, 0, shared=True)
-        turned = bank("turned", 1)
+        for c in range(1, 3):
+            placed.append(own([P, T], F32, "placed%d" % c))
+            nc.gpsimd.memset(placed[c][:].bitcast(I32), 0)
+
+        turned = bank("turned", 0)
         nc.tensor.transpose(turned[:, :P], vec_rows[:], ident[:])
         nc.scalar.copy(out=vec_cols[:, :12], in_=turned[:, :12])
-        early_bias = stage([P, 8], F32, "early_bias", 80)
-        nc.scalar.copy(out=early_bias[:, :4], in_=turned[:, 8:12])
-        weight = stage([P, J], F32, "weight", 0)
-        spreads = []
-        for j0 in range(0, J, HALF):
-            spread = bank("spread%d" % j0, 4 + j0 // HALF)
-            spreads.append(spread)
+
+        def spread_weights(j0, spread_bank):
+            spread = bank("spread%d" % j0, spread_bank)
             for b0 in range(0, HALF, P):
                 b = (j0 + b0) // P
                 nc.tensor.transpose(spread[:, b0 : b0 + P], vec_cols[:, b : b + 1].to_broadcast([P, P]), ident[:])
             nc.scalar.copy(out=weight[:, j0 : j0 + HALF], in_=spread[:])
-        gather_words(0, QUARTER)
-        gather_words(HALF, HALF)
-        for c in range(1, 3):
-            placed.append(own([P, T], F32, "placed%d" % c, 5 + 8 * c))
-            nc.gpsimd.memset(placed[c][:].bitcast(I32), 0)
-        Q = QUARTER
+            return spread
 
-        def second_quarter_weight(name, kib):
-            factor = own([P, Q], F32, name, kib)
-            nc.scalar.copy(out=factor[:], in_=spreads[0][:, Q:])
-            return factor[:]
-
-        step0 = own([P, HALF], F32, "step0_0", 86)
-        product(0, 0, Q, 0, step0[:, :Q], early_bias, state_first=False)
-        product(0, Q, Q, 6, step0[:, Q:], early_bias, state_first=False)
-        product(1, 0, HALF, 3, own([P, HALF], F32, "step1_0")[:], early_bias)
-        product(2, 0, HALF, 0, own([P, HALF], F32, "step2_0", 88)[:], early_bias)
-        add_state(0, 0, Q, steps[0, 0], 98)
-        add_state(0, Q, Q, steps[0, Q])
+        first_spread = spread_weights(0, 1)
+        spread_weights(HALF, 2)
+        nc.vector.tensor_copy(out=v_s[:], in_=tab_s[:].bitcast(U8).indirect(offsets[:]))
+        nc.vector.tensor_copy(out=v_w[:], in_=tab_w[:].bitcast(U32).indirect(offsets[:]))
+        quantise(0, 0, Q, Q)
+        quantise(1, 0, Q, Q)
+        product(0, 0, Q, 3)
+        product(1, 0, Q, 3)
+        pick_state(0, Q, J - Q)
+        add_state(0, 0, Q, 0)
         place(0, 0, Q)
-        placed.append(own([P, T], F32, "placed3", 98))
+        placed.append(own([P, T], F32, "placed3", 0))
         nc.gpsimd.memset(placed[3][:].bitcast(I32), 0)
-        add_state(1, 0, HALF, steps[1, 0], 86)
-        place(0, Q, Q, early_factor[:])
-        place(1, 0, HALF)
-        add_state(2, 0, HALF, steps[2, 0])
+        add_state(1, 0, Q)
+        pick_state(1, Q, Q)
+        quantise(0, Q, Q, Q)
+        pick_state(1, HALF, HALF, 24)
+        quantise(1, Q, Q, Q)
+        factor = own([P, Q], F32, "factor1", 8)
+        nc.scalar.copy(out=factor[:], in_=first_spread[:, :Q])
+        place(1, 0, Q, factor[:])
+        steps[2, 0] = own([P, HALF], F32, "step2_0")
+        product(2, 0, Q, 5, steps[2, 0][:, :Q])
+        product(2, Q, Q, 3, steps[2, 0][:, Q:])
+        product(0, Q, Q, 6)
+        product(1, Q, Q, 7)
+        add_by_turning(0, Q, Q, 2, 1)
+        add_by_turning(1, Q, Q, 0, 4)
+        add_state(2, 0, HALF)
         place(2, 0, HALF)
-        quantise(0, HALF, 88, bf_kib=80)
-        quantise(1, HALF)
-        last_bias = own([P, 8], F32, "last_bias")
-        nc.scalar.copy(out=last_bias[:, :4], in_=turned[:, 8:12])
-        product(3, 0, HALF, 6, own([P, HALF], F32, "step3_0", 53)[:], last_bias)
-        add_state(3, 0, Q, steps[3, 0][:, :Q])
-        add_state(3, Q, Q, steps[3, 0][:, Q:])
-        place(3, 0, Q)
-        for c in range(2):
-            product(c, HALF, HALF, 3 * c, own([P, HALF], F32, "step%d_1" % c)[:], vec_cols[:, 8:12])
-        factor = second_quarter_weight("factor3", 94 + 1 / 16)
-        for c in range(2, N_TILES):
-            product(c, HALF, HALF, 5 * c - 8, own([P, HALF], F32, "step%d_1" % c)[:], last_bias, pass_order=(1, 0))
-        add_state(0, HALF, HALF, steps[0, HALF], 92 + 1 / 16)
-        place(3, Q, Q, factor)
-        add_state(1, HALF, HALF, steps[1, HALF])
-        place(0, HALF, HALF)
-        add_state(2, HALF, HALF, steps[2, HALF])
-        place(1, HALF, HALF)
-        add_state(3, HALF, HALF, steps[3, HALF])
-        place(2, HALF, HALF)
-        place(3, HALF, HALF)
+        place(0, Q, Q)
+        place(1, Q, Q)
+        product(3, 0, HALF, 0)
+        quantise(0, HALF, HALF, HALF)
+        add_state(3, 0, HALF)
+        quantise(1, HALF, HALF, HALF)
+        factor = own([P, HALF], F32, "factor3", 16)
+        nc.scalar.copy(out=factor[:], in_=weight[:, :HALF])
+        place(3, 0, HALF, factor[:])
+        product(2, HALF, HALF, 1)
+        product(3, HALF, HALF, 4)
+        product(0, HALF, HALF, 1)
+        product(1, HALF, HALF, 4)
+        add_by_turning(0, HALF, HALF, 2, 3)
+        add_by_turning(1, HALF, HALF, 5, 6)
+        add_state(2, HALF, HALF)
+        add_state(3, HALF, HALF)
+        for c in (2, 3, 0, 1):
+            place(c, HALF, HALF)
+            store(c, last=(c == 1))

@@ -78,7 +78,6 @@ def tile_list_tgn_rnn_kernel(
         v_s = own([P, J], U8, "v_s")
         v_w = own([P, J], U32, "v_w")
         vec_cols = own([P, 16], F32, "vec_cols")
-        weight = own([P, J], F32, "weight")
 
         def listed(j0, width):
             return offsets[:, j0 // 16 : (j0 + width) // 16]
@@ -115,8 +114,8 @@ def tile_list_tgn_rnn_kernel(
                 un_w[c] = words[:].bitcast(U8)[:, 2 * (c - c0) * P : 2 * (c - c0 + 1) * P]
             nc.sync.dma_start(out=words[:], in_=un_words[0].bitcast(I32)[:, c0 * P // 2 : (c0 + 2) * P // 2])
 
-        def quantise(a, j0, width, on_scalar):
-            grouped = own([P, width, PACK], BF16, "x_bf%d_%d" % (a, j0))
+        def quantise(a, j0, width, on_scalar, kib=None):
+            grouped = own([P, width, PACK], BF16, "x_bf%d_%d" % (a, j0), kib)
             half, b0 = j0 - j0 % HALF, j0 % HALF
             nc.scalar.activation(
                 out=grouped[:, :on_scalar, :].rearrange("p (g j) i -> p g i j", j=LINE),
@@ -205,6 +204,10 @@ def tile_list_tgn_rnn_kernel(
                 op=ALU.mult,
             )
 
+        def clear_window(kib):
+            placed.append(own([P, T], F32, "placed%d" % len(placed), kib))
+            nc.gpsimd.memset(placed[-1][:].bitcast(I32), 0)
+
         def store(c, last=False):
             rows = out[c * P : (c + 1) * P, :]
             if last:
@@ -219,7 +222,7 @@ def tile_list_tgn_rnn_kernel(
         nc.sync.dma_start(out=tab_w[:], in_=tab_words[0].rearrange("p t i -> p (t i)").bitcast(I32))
         for r in range(4):
             load_un_scales(r)
-        load_x(1, 0, Q)
+        load_x(1, 0, Q, 44)
         load_wn(0)
         load_h(0)
         load_un(0)
@@ -237,10 +240,6 @@ def tile_list_tgn_rnn_kernel(
         load_h(3)
         load_x(1, HALF, HALF, 16)
 
-        for c in range(1, 3):
-            placed.append(own([P, T], F32, "placed%d" % c))
-            nc.gpsimd.memset(placed[c][:].bitcast(I32), 0)
-
         turned = bank("turned", 0)
         nc.tensor.transpose(turned[:, :P], vec_rows[:], ident[:])
         nc.scalar.copy(out=vec_cols[:, :12], in_=turned[:, :12])
@@ -253,28 +252,30 @@ def tile_list_tgn_rnn_kernel(
             nc.scalar.copy(out=weight[:, j0 : j0 + HALF], in_=spread[:])
             return spread
 
-        first_spread = spread_weights(0, 1)
-        spread_weights(HALF, 2)
         nc.vector.tensor_copy(out=v_s[:], in_=tab_s[:].bitcast(U8).indirect(offsets[:]))
         nc.vector.tensor_copy(out=v_w[:], in_=tab_w[:].bitcast(U32).indirect(offsets[:]))
         quantise(0, 0, Q, Q)
         quantise(1, 0, Q, Q)
-        product(0, 0, Q, 3)
+        weight = own([P, J], F32, "weight", 44)
+        first_spread = spread_weights(0, 1)
+        spread_weights(HALF, 2)
+        steps[0, 0] = own([P, Q], F32, "step0_0", 0)
+        product(0, 0, Q, 3, steps[0, 0][:])
         product(1, 0, Q, 3)
         pick_state(0, Q, J - Q)
-        add_state(0, 0, Q, 0)
+        add_state(0, 0, Q)
+        clear_window(0)
         place(0, 0, Q)
-        placed.append(own([P, T], F32, "placed3", 0))
-        nc.gpsimd.memset(placed[3][:].bitcast(I32), 0)
         add_state(1, 0, Q)
         pick_state(1, Q, Q)
         quantise(0, Q, Q, Q)
         pick_state(1, HALF, HALF, 24)
-        quantise(1, Q, Q, Q)
+        quantise(1, Q, Q, Q, 28)
+        clear_window(28)
         factor = own([P, Q], F32, "factor1", 8)
         nc.scalar.copy(out=factor[:], in_=first_spread[:, :Q])
         place(1, 0, Q, factor[:])
-        steps[2, 0] = own([P, HALF], F32, "step2_0")
+        steps[2, 0] = own([P, HALF], F32, "step2_0", 36)
         product(2, 0, Q, 5, steps[2, 0][:, :Q])
         product(2, Q, Q, 3, steps[2, 0][:, Q:])
         product(0, Q, Q, 6)
@@ -282,6 +283,7 @@ def tile_list_tgn_rnn_kernel(
         add_by_turning(0, Q, Q, 2, 1)
         add_by_turning(1, Q, Q, 0, 4)
         add_state(2, 0, HALF)
+        clear_window(36)
         place(2, 0, HALF)
         place(0, Q, Q)
         place(1, Q, Q)

@@ -43,14 +43,15 @@ def tile_list_tgn_rnn_kernel(
         w_s = keep.tile([P, N // 4], I32, name="w_s", align_bytes=64)
         ident = keep.tile([P, P], F32, name="ident", align_bytes=64)
         vec_rows = keep.tile([P, P], F32, name="vec_rows", align_bytes=64)
-        placed = [keep.tile([P, T], F32, name="placed0", align_bytes=64)]
+        placed = [keep.tile([P, T], F32, name="placed%d" % c, align_bytes=64) for c in range(2)]
 
         nc.sync.dma_start(offsets[:], offs)
         nc.sync.dma_start(out=x_first[:], in_=x[:K_PASS, :Q].rearrange("(p i) j -> p i j", i=PACK))
         nc.gpsimd.memset(tab_s[:], 0)
         nc.vector.memset(w_s[:], 0)
         nc.vector.memset(vec_rows[:], 0.0)
-        nc.vector.memset(placed[0][:].bitcast(I32), 0)
+        for window in placed:
+            nc.vector.memset(window[:].bitcast(I32), 0)
         nc.gpsimd.dma_start(out=vec_rows[8:12, :], in_=bn.rearrange("(c p) -> c p", p=P))
         nc.gpsimd.dma_start(out=vec_rows[0:8, :], in_=wgo[0].rearrange("(c p) -> c p", p=P))
         make_identity(nc, ident[:])
@@ -224,10 +225,10 @@ def tile_list_tgn_rnn_kernel(
             load_un_scales(r)
         load_x(1, 0, Q, 44)
         load_wn(0)
-        load_h(0)
         load_un(0)
         for q in range(4):
             load_wn_scales(q)
+        load_h(0)
         load_wn(1)
         load_h(1)
         load_x(0, Q, Q, 24)
@@ -259,12 +260,10 @@ def tile_list_tgn_rnn_kernel(
         weight = own([P, J], F32, "weight", 44)
         first_spread = spread_weights(0, 1)
         spread_weights(HALF, 2)
-        steps[0, 0] = own([P, Q], F32, "step0_0", 0)
-        product(0, 0, Q, 3, steps[0, 0][:])
+        product(0, 0, Q, 3)
         product(1, 0, Q, 3)
-        pick_state(0, Q, J - Q)
         add_state(0, 0, Q)
-        clear_window(0)
+        pick_state(0, Q, J - Q)
         place(0, 0, Q)
         add_state(1, 0, Q)
         pick_state(1, Q, Q)

@@ -134,12 +134,12 @@ def tile_list_tgn_rnn_kernel(
                 in_=grouped[:].rearrange("p j i -> p (j i)"),
             )
 
-        def product(c, j0, width, sn_bank, step=None):
+        def product(c, j0, width, sn_bank, step=None, state_first=True):
             cols = slice(c * P, (c + 1) * P)
             half, b0 = j0 - j0 % HALF, j0 % HALF
             sn = bank("sn%d_%d" % (c, j0), sn_bank)
             group = HALF if width == HALF else P
-            passes = [
+            state_passes = [
                 (
                     slice(g0, g0 + group),
                     un_w[c].bitcast(FP4X4),
@@ -148,7 +148,8 @@ def tile_list_tgn_rnn_kernel(
                     v_s[:, j0 + g0 : j0 + g0 + group],
                 )
                 for g0 in range(0, width, group)
-            ] + [
+            ]
+            message_passes = [
                 (
                     slice(0, width),
                     wn_w[c][:, a, :].bitcast(FP8X4),
@@ -158,6 +159,7 @@ def tile_list_tgn_rnn_kernel(
                 )
                 for a in range(PASSES)
             ]
+            passes = state_passes + message_passes if state_first else message_passes + state_passes
             for n, (span, w_codes, w_scales, codes, scales) in enumerate(passes):
                 nc.tensor.matmul_mx(
                     out=sn[:, span], lhsT=w_codes, lhsT_scale=w_scales, rhs=codes.bitcast(FP8X4), rhs_scale=scales,
@@ -221,14 +223,14 @@ def tile_list_tgn_rnn_kernel(
             load_tab_scales(r)
         tab_w = own([P, T], I32, "tab_w")
         nc.sync.dma_start(out=tab_w[:], in_=tab_words[0].rearrange("p t i -> p (t i)").bitcast(I32))
-        for r in range(4):
-            load_un_scales(r)
-        load_x(1, 0, Q, 44)
-        load_wn(0)
-        load_un(0)
         for q in range(4):
             load_wn_scales(q)
+        load_x(1, 0, Q, 44)
+        load_wn(0)
         load_h(0)
+        load_un(0)
+        for r in range(4):
+            load_un_scales(r)
         load_wn(1)
         load_h(1)
         load_x(0, Q, Q, 24)
@@ -260,10 +262,10 @@ def tile_list_tgn_rnn_kernel(
         weight = own([P, J], F32, "weight", 44)
         first_spread = spread_weights(0, 1)
         spread_weights(HALF, 2)
-        product(0, 0, Q, 3)
+        product(0, 0, Q, 3, state_first=False)
         product(1, 0, Q, 3)
-        add_state(0, 0, Q)
         pick_state(0, Q, J - Q)
+        add_state(0, 0, Q)
         place(0, 0, Q)
         add_state(1, 0, Q)
         pick_state(1, Q, Q)

@@ -43,15 +43,14 @@ def tile_list_tgn_rnn_kernel(
         w_s = keep.tile([P, N // 4], I32, name="w_s", align_bytes=64)
         ident = keep.tile([P, P], F32, name="ident", align_bytes=64)
         vec_rows = keep.tile([P, P], F32, name="vec_rows", align_bytes=64)
-        placed = [keep.tile([P, T], F32, name="placed%d" % c, align_bytes=64) for c in range(2)]
+        placed = [keep.tile([P, T], F32, name="placed0", align_bytes=64)]
 
         nc.sync.dma_start(offsets[:], offs)
         nc.sync.dma_start(out=x_first[:], in_=x[:K_PASS, :Q].rearrange("(p i) j -> p i j", i=PACK))
         nc.gpsimd.memset(tab_s[:], 0)
         nc.vector.memset(w_s[:], 0)
         nc.vector.memset(vec_rows[:], 0.0)
-        for window in placed:
-            nc.vector.memset(window[:].bitcast(I32), 0)
+        nc.vector.memset(placed[0][:].bitcast(I32), 0)
         nc.gpsimd.dma_start(out=vec_rows[8:12, :], in_=bn.rearrange("(c p) -> c p", p=P))
         nc.gpsimd.dma_start(out=vec_rows[0:8, :], in_=wgo[0].rearrange("(c p) -> c p", p=P))
         make_identity(nc, ident[:])
@@ -134,7 +133,7 @@ def tile_list_tgn_rnn_kernel(
                 in_=grouped[:].rearrange("p j i -> p (j i)"),
             )
 
-        def product(c, j0, width, sn_bank, step=None, state_first=True):
+        def product(c, j0, width, sn_bank, step=None, state_first=True, bias=None):
             cols = slice(c * P, (c + 1) * P)
             half, b0 = j0 - j0 % HALF, j0 % HALF
             sn = bank("sn%d_%d" % (c, j0), sn_bank)
@@ -168,7 +167,7 @@ def tile_list_tgn_rnn_kernel(
             if step is None:
                 steps[c, j0] = own([P, width], F32, "step%d_%d" % (c, j0))
                 step = steps[c, j0][:]
-            nc.scalar.activation(out=step, in_=sn[:, :width], func=ACT.Tanh, bias=vec_cols[:, 8 + c : 9 + c])
+            nc.scalar.activation(out=step, in_=sn[:, :width], func=ACT.Tanh, bias=vec_cols[:, 8 + c : 9 + c] if bias is None else bias)
 
         def pick_state(c, j0, width, kib=None):
             rows = own([P, width], F32, "picked%d_%d" % (c, j0), kib)
@@ -262,7 +261,10 @@ def tile_list_tgn_rnn_kernel(
         weight = own([P, J], F32, "weight", 44)
         first_spread = spread_weights(0, 1)
         spread_weights(HALF, 2)
-        product(0, 0, Q, 3, state_first=False)
+        first_bias = own([P, 1], F32, "first_bias", 0)
+        nc.scalar.copy(out=first_bias[:], in_=turned[:, 8:9])
+        product(0, 0, Q, 3, state_first=False, bias=first_bias[:])
+        clear_window(0)
         product(1, 0, Q, 3)
         pick_state(0, Q, J - Q)
         add_state(0, 0, Q)

@@ -184,7 +184,11 @@ def tile_list_tgn_rnn_kernel(
                         there[:, b0 : b0 + P], lhsT=term, rhs=ident[:], is_transpose=True, start=(n == 0), stop=(n == 1)
                     )
             turned_sum = own([P, width], F32, "turned_sum%d_%d" % (c, j0))
-            nc.scalar.copy(out=turned_sum[:], in_=there[:, :width])
+            for b0 in range(0, width, P):
+                b = (j0 + b0) // P
+                nc.scalar.activation(
+                    out=turned_sum[:, b0 : b0 + P], in_=there[:, b0 : b0 + P], func=ACT.Copy, scale=vec_cols[:, b : b + 1]
+                )
             back = bank("back%d_%d" % (c, j0), back_bank)
             for b0 in range(0, width, P):
                 nc.tensor.transpose(back[:, b0 : b0 + P], turned_sum[:, b0 : b0 + P], ident[:])
@@ -205,6 +209,9 @@ def tile_list_tgn_rnn_kernel(
                 in1=weight[:, j0 : j0 + width] if factor is None else factor,
                 op=ALU.mult,
             )
+
+        def place_weighed(c, j0, width):
+            nc.vector.tensor_copy(out=placed[c][:].indirect(listed(j0, width)), in_=sums[c, j0][:])
 
         def clear_window(kib):
             placed.append(own([P, T], F32, "placed%d" % len(placed), kib))
@@ -288,8 +295,8 @@ def tile_list_tgn_rnn_kernel(
         add_state(2, 0, HALF)
         clear_window(36)
         place(2, 0, HALF)
-        place(0, Q, Q)
-        place(1, Q, Q)
+        place_weighed(0, Q, Q)
+        place_weighed(1, Q, Q)
         product(3, 0, HALF, 0)
         quantise(0, HALF, HALF, HALF)
         add_state(3, 0, HALF)
@@ -306,5 +313,8 @@ def tile_list_tgn_rnn_kernel(
         add_state(2, HALF, HALF)
         add_state(3, HALF, HALF)
         for c in (2, 3, 0, 1):
-            place(c, HALF, HALF)
+            if c < 2:
+                place_weighed(c, HALF, HALF)
+            else:
+                place(c, HALF, HALF)
             store(c, last=(c == 1))

@@ -175,7 +175,7 @@ def tile_list_tgn_rnn_kernel(
                 picked[c, j0 + b0] = rows[:, b0 : b0 + P]
             nc.vector.tensor_copy(out=rows[:], in_=h_all[c][:].indirect(listed(j0, width)))
 
-        def add_by_turning(c, j0, width, there_bank, back_bank):
+        def add_by_turning(c, j0, width, there_bank, back_bank, total=None):
             there = bank("there%d_%d" % (c, j0), there_bank)
             for b0 in range(0, width, P):
                 terms = (steps[c, j0][:, b0 : b0 + P], picked[c, j0 + b0])
@@ -186,14 +186,15 @@ def tile_list_tgn_rnn_kernel(
             turned_sum = own([P, width], F32, "turned_sum%d_%d" % (c, j0))
             for b0 in range(0, width, P):
                 b = (j0 + b0) // P
-                nc.scalar.activation(
-                    out=turned_sum[:, b0 : b0 + P], in_=there[:, b0 : b0 + P], func=ACT.Copy, scale=vec_cols[:, b : b + 1]
-                )
+                scale = vec_cols[:, b : b + 1] if total is None else 1.0
+                nc.scalar.activation(out=turned_sum[:, b0 : b0 + P], in_=there[:, b0 : b0 + P], func=ACT.Copy, scale=scale)
             back = bank("back%d_%d" % (c, j0), back_bank)
             for b0 in range(0, width, P):
                 nc.tensor.transpose(back[:, b0 : b0 + P], turned_sum[:, b0 : b0 + P], ident[:])
-            sums[c, j0] = own([P, width], F32, "sum%d_%d" % (c, j0))
-            nc.scalar.copy(out=sums[c, j0][:], in_=back[:, :width])
+            if total is None:
+                sums[c, j0] = own([P, width], F32, "sum%d_%d" % (c, j0))
+                total = sums[c, j0][:]
+            nc.scalar.copy(out=total, in_=back[:, :width])
 
         def add_state(c, j0, width, kib=None):
             sums[c, j0] = own([P, width], F32, "sum%d_%d" % (c, j0), kib)
@@ -270,6 +271,8 @@ def tile_list_tgn_rnn_kernel(
         spread_weights(HALF, 2)
         first_bias = own([P, 1], F32, "first_bias", 0)
         nc.scalar.copy(out=first_bias[:], in_=turned[:, 8:9])
+        third_bias = own([P, 1], F32, "third_bias", 48)
+        nc.scalar.copy(out=third_bias[:], in_=turned[:, 10:11])
         product(0, 0, Q, 3, state_first=False, bias=first_bias[:])
         clear_window(0)
         product(1, 0, Q, 3)
@@ -287,12 +290,13 @@ def tile_list_tgn_rnn_kernel(
         place(1, 0, Q, factor[:])
         steps[2, 0] = own([P, HALF], F32, "step2_0", 36)
         product(2, 0, Q, 5, steps[2, 0][:, :Q])
-        product(2, Q, Q, 3, steps[2, 0][:, Q:])
+        product(2, Q, Q, 3, steps[2, 0][:, Q:], bias=third_bias[:])
         product(0, Q, Q, 6)
         product(1, Q, Q, 7)
         add_by_turning(0, Q, Q, 2, 1)
         add_by_turning(1, Q, Q, 0, 4)
         add_state(2, 0, HALF)
+        pick_state(2, HALF, P, 48)
         clear_window(36)
         place(2, 0, HALF)
         place_weighed(0, Q, Q)
@@ -304,15 +308,20 @@ def tile_list_tgn_rnn_kernel(
         factor = own([P, HALF], F32, "factor3", 16)
         nc.scalar.copy(out=factor[:], in_=weight[:, :HALF])
         place(3, 0, HALF, factor[:])
-        product(2, HALF, HALF, 1)
-        product(3, HALF, HALF, 4)
+        product(3, HALF, HALF, 1)
+        product(2, HALF, HALF, 4)
+        sums[2, HALF] = own([P, HALF], F32, "sum2_late")
+        add_by_turning(2, HALF, P, 0, 7, sums[2, HALF][:, :P])
         product(0, HALF, HALF, 1)
         product(1, HALF, HALF, 4)
         add_by_turning(0, HALF, HALF, 2, 3)
         add_by_turning(1, HALF, HALF, 5, 6)
-        add_state(2, HALF, HALF)
         add_state(3, HALF, HALF)
-        for c in (2, 3, 0, 1):
+        nc.vector.tensor_tensor(
+            out=sums[2, HALF][:, P:], in0=h_all[2][:].indirect(listed(HALF + P, HALF - P)), in1=steps[2, HALF][:, P:],
+            op=ALU.add,
+        )
+        for c in (3, 2, 0, 1):
             if c < 2:
                 place_weighed(c, HALF, HALF)
             else:

@@ -21,11 +21,26 @@ P = 128
 PACK = 4
 K_PASS = P * PACK
 PASSES = K // K_PASS
-N_TILES = N // P
-Q = 256
-HALF = 512
+QUARTER = J // 4
+HALF = J // 2
 LINE = 4
+LIST_ROWS = 16
+QUADRANT = 32
+SCALE_ROWS = 16
+TAB_ROW_STEP = P // SCALE_ROWS
 BANK_BYTES = 2048
+WGO_ROWS = J // P
+VEC_ROWS = WGO_ROWS + N // P
+
+AT_BIAS0_WINDOW1 = 0
+AT_X_SECOND_FACTOR1 = 8
+AT_TAB_SCALES_X_CODES = 12
+AT_X_LAST_FACTOR3 = 16
+AT_X_SECOND_PICKED1 = 24
+AT_X_BF_WINDOW2 = 28
+AT_TANH2_WINDOW3 = 36
+AT_X_FIRST_WEIGHT = 44
+AT_BIAS2_PICKED2 = 48
 
 
 def tile_list_tgn_rnn_kernel(
@@ -37,22 +52,22 @@ def tile_list_tgn_rnn_kernel(
         pinned = ctx.enter_context(tc.tile_pool(name="pinned", bufs=1))
         psum = ctx.enter_context(tc.psum_pool(name="psum", bufs=1))
 
-        offsets = keep.tile([P, J // 16], U16, name="offsets")
-        x_first = keep.tile([P, PACK, Q], F32, name="x_first", align_bytes=64)
-        tab_s = pinned.tile([P, T // 4], I32, name="tab_s", offset=12 * 1024, align_bytes=64)
-        w_s = keep.tile([P, N // 4], I32, name="w_s", align_bytes=64)
+        offsets = keep.tile([P, J // LIST_ROWS], U16, name="offsets")
+        x_first = keep.tile([P, PACK, QUARTER], F32, name="x_first", align_bytes=64)
+        tab_s = pinned.tile([P, T // 4], I32, name="tab_s", offset=AT_TAB_SCALES_X_CODES * 1024, align_bytes=64)
+        w_s = keep.tile([P, PASSES * N // 4], I32, name="w_s", align_bytes=64)
         ident = keep.tile([P, P], F32, name="ident", align_bytes=64)
         vec_rows = keep.tile([P, P], F32, name="vec_rows", align_bytes=64)
-        placed = [keep.tile([P, T], F32, name="placed0", align_bytes=64)]
+        windows = [keep.tile([P, T], F32, name="placed0", align_bytes=64)]
 
         nc.sync.dma_start(offsets[:], offs)
-        nc.sync.dma_start(out=x_first[:], in_=x[:K_PASS, :Q].rearrange("(p i) j -> p i j", i=PACK))
+        nc.sync.dma_start(out=x_first[:], in_=x[:K_PASS, :QUARTER].rearrange("(p i) j -> p i j", i=PACK))
         nc.gpsimd.memset(tab_s[:], 0)
         nc.vector.memset(w_s[:], 0)
         nc.vector.memset(vec_rows[:], 0.0)
-        nc.vector.memset(placed[0][:].bitcast(I32), 0)
-        nc.gpsimd.dma_start(out=vec_rows[8:12, :], in_=bn.rearrange("(c p) -> c p", p=P))
-        nc.gpsimd.dma_start(out=vec_rows[0:8, :], in_=wgo[0].rearrange("(c p) -> c p", p=P))
+        nc.vector.memset(windows[0][:].bitcast(I32), 0)
+        nc.gpsimd.dma_start(out=vec_rows[WGO_ROWS:VEC_ROWS, :], in_=bn.rearrange("(c p) -> c p", p=P))
+        nc.gpsimd.dma_start(out=vec_rows[0:WGO_ROWS, :], in_=wgo[0].rearrange("(c p) -> c p", p=P))
         make_identity(nc, ident[:])
 
         work = ctx.enter_context(tc.tile_pool(name="work", bufs=1))
@@ -60,10 +75,10 @@ def tile_list_tgn_rnn_kernel(
         def bank(name, n):
             return psum.tile([P, HALF], F32, name=name, offset=n * BANK_BYTES)
 
-        def own(shape, dtype, name, kib=None):
-            if kib is None:
+        def own(shape, dtype, name, at=None):
+            if at is None:
                 return work.tile(shape, dtype, name=name, align_bytes=64)
-            return pinned.tile(shape, dtype, name=name, offset=int(kib * 1024), align_bytes=64)
+            return pinned.tile(shape, dtype, name=name, offset=at * 1024, align_bytes=64)
 
         x_raw = {(0, 0): x_first}
         h_all = {}
@@ -73,17 +88,18 @@ def tile_list_tgn_rnn_kernel(
         sums = {}
         picked = {}
         x_w = {(a, j0): own([P, HALF], U32, "x_w%d_%d" % (a, j0)) for a, j0 in ((1, 0), (0, HALF), (1, HALF))}
-        x_w[0, 0] = own([P, HALF], U32, "x_w0_0", 12)
+        x_w[0, 0] = own([P, HALF], U32, "x_w0_0", AT_TAB_SCALES_X_CODES)
         x_s = {(a, j0): own([P, HALF], U8, "x_s%d_%d" % (a, j0)) for a in range(PASSES) for j0 in (0, HALF)}
-        v_s = own([P, J], U8, "v_s")
+        v_s = own([P, J // 4], I32, "v_s")
+        gathered_s = own([P, J], U8, "gathered_s")
         v_w = own([P, J], U32, "v_w")
         vec_cols = own([P, 16], F32, "vec_cols")
 
         def listed(j0, width):
-            return offsets[:, j0 // 16 : (j0 + width) // 16]
+            return offsets[:, j0 // LIST_ROWS : (j0 + width) // LIST_ROWS]
 
-        def load_x(a, j0, width, kib=None):
-            raw = own([P, PACK, width], F32, "x_raw%d_%d" % (a, j0), kib)
+        def load_x(a, j0, width, at=None):
+            raw = own([P, PACK, width], F32, "x_raw%d_%d" % (a, j0), at)
             x_raw[a, j0] = raw
             rows = x[a * K_PASS : (a + 1) * K_PASS, j0 : j0 + width]
             nc.sync.dma_start(out=raw[:], in_=rows.rearrange("(p i) j -> p i j", i=PACK))
@@ -92,15 +108,17 @@ def tile_list_tgn_rnn_kernel(
             h_all[c] = own([P, T], F32, "h_all%d" % c)
             nc.sync.dma_start(out=h_all[c][:], in_=hT[c * P : (c + 1) * P, :])
 
-        def load_tab_scales(r):
-            nc.sync.dma_start(out=tab_s[r:P:32, :], in_=tab_scales[0, r:16:4, :].bitcast(I32))
+        def move_tab_scales(r):
+            rows = gathered_s[:].bitcast(I32)
+            nc.sync.dma_start(out=v_s[r:P:QUADRANT, :], in_=rows[TAB_ROW_STEP * r : P : QUADRANT, :])
 
         def load_un_scales(r):
-            nc.sync.dma_start(out=w_s[r:P:32, :], in_=un_scales[0, r:16:4, :].bitcast(I32))
+            nc.sync.dma_start(out=w_s[r:P:QUADRANT, : N // 4], in_=un_scales[0, r:SCALE_ROWS:4, :].bitcast(I32))
 
-        def load_wn_scales(q):
+        def load_wn_scales(r):
             nc.sync.dma_start(
-                out=w_s[32 * q + 4 : 32 * q + 12, :], in_=wn_scales[:, 4 * q : 4 * q + 4, :].bitcast(I32)
+                out=w_s[4 + r : P : QUADRANT, :].rearrange("q (a n) -> q a n", a=PASSES),
+                in_=wn_scales[:, r:SCALE_ROWS:4, :].rearrange("a q n -> q a n").bitcast(I32),
             )
 
         def load_wn(c):
@@ -114,19 +132,14 @@ def tile_list_tgn_rnn_kernel(
                 un_w[c] = words[:].bitcast(U8)[:, 2 * (c - c0) * P : 2 * (c - c0 + 1) * P]
             nc.sync.dma_start(out=words[:], in_=un_words[0].bitcast(I32)[:, c0 * P // 2 : (c0 + 2) * P // 2])
 
-        def quantise(a, j0, width, on_scalar, kib=None):
-            grouped = own([P, width, PACK], BF16, "x_bf%d_%d" % (a, j0), kib)
+        def quantise(a, j0, width, at=None):
+            grouped = own([P, width, PACK], BF16, "x_bf%d_%d" % (a, j0), at)
             half, b0 = j0 - j0 % HALF, j0 % HALF
             nc.scalar.activation(
-                out=grouped[:, :on_scalar, :].rearrange("p (g j) i -> p g i j", j=LINE),
-                in_=x_raw[a, j0][:, :, :on_scalar].rearrange("p i (g j) -> p g i j", j=LINE),
+                out=grouped[:].rearrange("p (g j) i -> p g i j", j=LINE),
+                in_=x_raw[a, j0][:].rearrange("p i (g j) -> p g i j", j=LINE),
                 func=ACT.Copy,
             )
-            if on_scalar < width:
-                nc.vector.tensor_copy(
-                    out=grouped[:, on_scalar:, :].rearrange("p (g j) i -> p g i j", j=LINE),
-                    in_=x_raw[a, j0][:, :, on_scalar:].rearrange("p i (g j) -> p g i j", j=LINE),
-                )
             nc.vector.quantize_mx(
                 out=x_w[a, half][:, b0 : b0 + width].bitcast(FP8X4),
                 scales=x_s[a, half][:, b0 : b0 + width],
@@ -144,7 +157,7 @@ def tile_list_tgn_rnn_kernel(
                     un_w[c].bitcast(FP4X4),
                     w_s[:].bitcast(U8)[:, cols],
                     v_w[:, j0 + g0 : j0 + g0 + group],
-                    v_s[:, j0 + g0 : j0 + g0 + group],
+                    v_s[:].bitcast(U8)[:, j0 + g0 : j0 + g0 + group],
                 )
                 for g0 in range(0, width, group)
             ]
@@ -152,7 +165,7 @@ def tile_list_tgn_rnn_kernel(
                 (
                     slice(0, width),
                     wn_w[c][:, a, :].bitcast(FP8X4),
-                    w_s[:].bitcast(U8)[4 + 4 * a :, cols],
+                    w_s[:].bitcast(U8)[4:, a * N + c * P : a * N + (c + 1) * P],
                     x_w[a, half][:, b0 : b0 + width],
                     x_s[a, half][:, b0 : b0 + width],
                 )
@@ -167,15 +180,17 @@ def tile_list_tgn_rnn_kernel(
             if step is None:
                 steps[c, j0] = own([P, width], F32, "step%d_%d" % (c, j0))
                 step = steps[c, j0][:]
-            nc.scalar.activation(out=step, in_=sn[:, :width], func=ACT.Tanh, bias=vec_cols[:, 8 + c : 9 + c] if bias is None else bias)
+            if bias is None:
+                bias = vec_cols[:, WGO_ROWS + c : WGO_ROWS + c + 1]
+            nc.scalar.activation(out=step, in_=sn[:, :width], func=ACT.Tanh, bias=bias)
 
-        def pick_state(c, j0, width, kib=None):
-            rows = own([P, width], F32, "picked%d_%d" % (c, j0), kib)
+        def pick_state(c, j0, width, at=None):
+            rows = own([P, width], F32, "picked%d_%d" % (c, j0), at)
             for b0 in range(0, width, P):
                 picked[c, j0 + b0] = rows[:, b0 : b0 + P]
             nc.vector.tensor_copy(out=rows[:], in_=h_all[c][:].indirect(listed(j0, width)))
 
-        def add_by_turning(c, j0, width, there_bank, back_bank, total=None):
+        def add_by_turning(c, j0, width, there_bank, back_bank, unweighed=None):
             there = bank("there%d_%d" % (c, j0), there_bank)
             for b0 in range(0, width, P):
                 terms = (steps[c, j0][:, b0 : b0 + P], picked[c, j0 + b0])
@@ -186,73 +201,79 @@ def tile_list_tgn_rnn_kernel(
             turned_sum = own([P, width], F32, "turned_sum%d_%d" % (c, j0))
             for b0 in range(0, width, P):
                 b = (j0 + b0) // P
-                scale = vec_cols[:, b : b + 1] if total is None else 1.0
-                nc.scalar.activation(out=turned_sum[:, b0 : b0 + P], in_=there[:, b0 : b0 + P], func=ACT.Copy, scale=scale)
+                scale = vec_cols[:, b : b + 1] if unweighed is None else 1.0
+                nc.scalar.activation(
+                    out=turned_sum[:, b0 : b0 + P], in_=there[:, b0 : b0 + P], func=ACT.Copy, scale=scale
+                )
             back = bank("back%d_%d" % (c, j0), back_bank)
             for b0 in range(0, width, P):
                 nc.tensor.transpose(back[:, b0 : b0 + P], turned_sum[:, b0 : b0 + P], ident[:])
+            total = unweighed
             if total is None:
                 sums[c, j0] = own([P, width], F32, "sum%d_%d" % (c, j0))
                 total = sums[c, j0][:]
             nc.scalar.copy(out=total, in_=back[:, :width])
 
-        def add_state(c, j0, width, kib=None):
-            sums[c, j0] = own([P, width], F32, "sum%d_%d" % (c, j0), kib)
-            nc.vector.tensor_tensor(
-                out=sums[c, j0][:], in0=h_all[c][:].indirect(listed(j0, width)), in1=steps[c, j0][:], op=ALU.add
-            )
+        def gather_and_add(c, j0, width, step, total):
+            nc.vector.tensor_tensor(out=total, in0=h_all[c][:].indirect(listed(j0, width)), in1=step, op=ALU.add)
+
+        def add_state(c, j0, width):
+            sums[c, j0] = own([P, width], F32, "sum%d_%d" % (c, j0))
+            gather_and_add(c, j0, width, steps[c, j0][:], sums[c, j0][:])
 
         def place(c, j0, width, factor=None):
-            window = placed[c]
             nc.vector.tensor_tensor(
-                out=window[:].indirect(listed(j0, width)),
+                out=windows[c][:].indirect(listed(j0, width)),
                 in0=sums[c, j0][:],
                 in1=weight[:, j0 : j0 + width] if factor is None else factor,
                 op=ALU.mult,
             )
 
         def place_weighed(c, j0, width):
-            nc.vector.tensor_copy(out=placed[c][:].indirect(listed(j0, width)), in_=sums[c, j0][:])
+            nc.vector.tensor_copy(out=windows[c][:].indirect(listed(j0, width)), in_=sums[c, j0][:])
 
-        def clear_window(kib):
-            placed.append(own([P, T], F32, "placed%d" % len(placed), kib))
-            nc.gpsimd.memset(placed[-1][:].bitcast(I32), 0)
+        def clear_window(at):
+            windows.append(own([P, T], F32, "placed%d" % len(windows), at))
+            nc.gpsimd.memset(windows[-1][:].bitcast(I32), 0)
 
-        def store(c, last=False):
+        def store(c, last):
             rows = out[c * P : (c + 1) * P, :]
             if last:
-                nc.sync.dma_start(out=rows[:, : T // 2], in_=placed[c][:, : T // 2])
-                nc.scalar.dma_start(out=rows[:, T // 2 :], in_=placed[c][:, T // 2 :])
+                nc.sync.dma_start(out=rows[:, : T // 2], in_=windows[c][:, : T // 2])
+                nc.scalar.dma_start(out=rows[:, T // 2 :], in_=windows[c][:, T // 2 :])
             else:
-                nc.sync.dma_start(out=rows, in_=placed[c][:])
+                nc.sync.dma_start(out=rows, in_=windows[c][:])
 
+        nc.sync.dma_start(out=tab_s[0:P:TAB_ROW_STEP, :], in_=tab_scales[0].bitcast(I32))
         for r in range(4):
-            load_tab_scales(r)
+            load_wn_scales(r)
         tab_w = own([P, T], I32, "tab_w")
         nc.sync.dma_start(out=tab_w[:], in_=tab_words[0].rearrange("p t i -> p (t i)").bitcast(I32))
-        for q in range(4):
-            load_wn_scales(q)
-        load_x(1, 0, Q, 44)
+        load_x(1, 0, QUARTER, AT_X_FIRST_WEIGHT)
         load_wn(0)
-        load_h(0)
-        load_un(0)
         for r in range(4):
             load_un_scales(r)
+        load_h(0)
+        nc.vector.tensor_copy(out=gathered_s[:], in_=tab_s[:].bitcast(U8).indirect(offsets[:]))
+        nc.vector.tensor_copy(out=v_s[:], in_=gathered_s[:].bitcast(I32))
+        for r in range(1, 4):
+            move_tab_scales(r)
+        load_un(0)
         load_wn(1)
         load_h(1)
-        load_x(0, Q, Q, 24)
-        load_x(1, Q, Q, 8)
+        load_x(0, QUARTER, QUARTER, AT_X_SECOND_PICKED1)
+        load_x(1, QUARTER, QUARTER, AT_X_SECOND_FACTOR1)
         load_wn(2)
         load_un(2)
         load_h(2)
         load_wn(3)
         load_x(0, HALF, HALF)
         load_h(3)
-        load_x(1, HALF, HALF, 16)
+        load_x(1, HALF, HALF, AT_X_LAST_FACTOR3)
 
         turned = bank("turned", 0)
         nc.tensor.transpose(turned[:, :P], vec_rows[:], ident[:])
-        nc.scalar.copy(out=vec_cols[:, :12], in_=turned[:, :12])
+        nc.scalar.copy(out=vec_cols[:, :VEC_ROWS], in_=turned[:, :VEC_ROWS])
 
         def spread_weights(j0, spread_bank):
             spread = bank("spread%d" % j0, spread_bank)
@@ -262,68 +283,71 @@ def tile_list_tgn_rnn_kernel(
             nc.scalar.copy(out=weight[:, j0 : j0 + HALF], in_=spread[:])
             return spread
 
-        nc.vector.tensor_copy(out=v_s[:], in_=tab_s[:].bitcast(U8).indirect(offsets[:]))
+        def bias_column(c, name, at):
+            column = own([P, 1], F32, name, at)
+            nc.scalar.copy(out=column[:], in_=turned[:, WGO_ROWS + c : WGO_ROWS + c + 1])
+            return column[:]
+
         nc.vector.tensor_copy(out=v_w[:], in_=tab_w[:].bitcast(U32).indirect(offsets[:]))
-        quantise(0, 0, Q, Q)
-        quantise(1, 0, Q, Q)
-        weight = own([P, J], F32, "weight", 44)
+        quantise(0, 0, QUARTER)
+        quantise(1, 0, QUARTER)
+        weight = own([P, J], F32, "weight", AT_X_FIRST_WEIGHT)
         first_spread = spread_weights(0, 1)
         spread_weights(HALF, 2)
-        first_bias = own([P, 1], F32, "first_bias", 0)
-        nc.scalar.copy(out=first_bias[:], in_=turned[:, 8:9])
-        third_bias = own([P, 1], F32, "third_bias", 48)
-        nc.scalar.copy(out=third_bias[:], in_=turned[:, 10:11])
-        product(0, 0, Q, 3, state_first=False, bias=first_bias[:])
-        clear_window(0)
-        product(1, 0, Q, 3)
-        pick_state(0, Q, J - Q)
-        add_state(0, 0, Q)
-        place(0, 0, Q)
-        add_state(1, 0, Q)
-        pick_state(1, Q, Q)
-        quantise(0, Q, Q, Q)
-        pick_state(1, HALF, HALF, 24)
-        quantise(1, Q, Q, Q, 28)
-        clear_window(28)
-        factor = own([P, Q], F32, "factor1", 8)
-        nc.scalar.copy(out=factor[:], in_=first_spread[:, :Q])
-        place(1, 0, Q, factor[:])
-        steps[2, 0] = own([P, HALF], F32, "step2_0", 36)
-        product(2, 0, Q, 5, steps[2, 0][:, :Q])
-        product(2, Q, Q, 3, steps[2, 0][:, Q:], bias=third_bias[:])
-        product(0, Q, Q, 6)
-        product(1, Q, Q, 7)
-        add_by_turning(0, Q, Q, 2, 1)
-        add_by_turning(1, Q, Q, 0, 4)
+        first_bias = bias_column(0, "first_bias", AT_BIAS0_WINDOW1)
+        third_bias = bias_column(2, "third_bias", AT_BIAS2_PICKED2)
+
+        product(0, 0, QUARTER, 3, state_first=False, bias=first_bias)
+        clear_window(AT_BIAS0_WINDOW1)
+        product(1, 0, QUARTER, 3)
+        pick_state(0, QUARTER, J - QUARTER)
+        add_state(0, 0, QUARTER)
+        place(0, 0, QUARTER)
+        add_state(1, 0, QUARTER)
+        pick_state(1, QUARTER, QUARTER)
+        quantise(0, QUARTER, QUARTER)
+        pick_state(1, HALF, HALF, AT_X_SECOND_PICKED1)
+        quantise(1, QUARTER, QUARTER, AT_X_BF_WINDOW2)
+        clear_window(AT_X_BF_WINDOW2)
+        factor = own([P, QUARTER], F32, "factor1", AT_X_SECOND_FACTOR1)
+        nc.scalar.copy(out=factor[:], in_=first_spread[:, :QUARTER])
+        place(1, 0, QUARTER, factor[:])
+
+        steps[2, 0] = own([P, HALF], F32, "step2_0", AT_TANH2_WINDOW3)
+        product(2, 0, QUARTER, 5, steps[2, 0][:, :QUARTER])
+        product(2, QUARTER, QUARTER, 3, steps[2, 0][:, QUARTER:], bias=third_bias)
+        product(0, QUARTER, QUARTER, 6)
+        product(1, QUARTER, QUARTER, 7)
+        add_by_turning(0, QUARTER, QUARTER, 2, 1)
+        add_by_turning(1, QUARTER, QUARTER, 0, 4)
         add_state(2, 0, HALF)
-        pick_state(2, HALF, P, 48)
-        clear_window(36)
+        pick_state(2, HALF, P, AT_BIAS2_PICKED2)
+        clear_window(AT_TANH2_WINDOW3)
         place(2, 0, HALF)
-        place_weighed(0, Q, Q)
-        place_weighed(1, Q, Q)
+        place_weighed(0, QUARTER, QUARTER)
+        place_weighed(1, QUARTER, QUARTER)
+
         product(3, 0, HALF, 0)
-        quantise(0, HALF, HALF, HALF)
+        quantise(0, HALF, HALF)
         add_state(3, 0, HALF)
-        quantise(1, HALF, HALF, HALF)
-        factor = own([P, HALF], F32, "factor3", 16)
+        quantise(1, HALF, HALF)
+        factor = own([P, HALF], F32, "factor3", AT_X_LAST_FACTOR3)
         nc.scalar.copy(out=factor[:], in_=weight[:, :HALF])
         place(3, 0, HALF, factor[:])
+
         product(3, HALF, HALF, 1)
         product(2, HALF, HALF, 4)
         sums[2, HALF] = own([P, HALF], F32, "sum2_late")
-        add_by_turning(2, HALF, P, 0, 7, sums[2, HALF][:, :P])
+        add_by_turning(2, HALF, P, 0, 7, unweighed=sums[2, HALF][:, :P])
         product(0, HALF, HALF, 1)
         product(1, HALF, HALF, 4)
         add_by_turning(0, HALF, HALF, 2, 3)
         add_by_turning(1, HALF, HALF, 5, 6)
         add_state(3, HALF, HALF)
-        nc.vector.tensor_tensor(
-            out=sums[2, HALF][:, P:], in0=h_all[2][:].indirect(listed(HALF + P, HALF - P)), in1=steps[2, HALF][:, P:],
-            op=ALU.add,
-        )
-        for c in (3, 2, 0, 1):
-            if c < 2:
-                place_weighed(c, HALF, HALF)
-            else:
-                place(c, HALF, HALF)
+        gather_and_add(2, HALF + P, HALF - P, steps[2, HALF][:, P:], sums[2, HALF][:, P:])
+        for c in (3, 2):
+            place(c, HALF, HALF)
+            store(c, last=False)
+        for c in (0, 1):
+            place_weighed(c, HALF, HALF)
             store(c, last=(c == 1))

@@ -146,7 +146,7 @@ def tile_list_tgn_rnn_kernel(
                 in_=grouped[:].rearrange("p j i -> p (j i)"),
             )
 
-        def product(c, j0, width, sn_bank, step=None, state_first=True, bias=None):
+        def product(c, j0, width, sn_bank, step=None, state_first=True, bias=None, pass_order=(0, 1)):
             cols = slice(c * P, (c + 1) * P)
             half, b0 = j0 - j0 % HALF, j0 % HALF
             sn = bank("sn%d_%d" % (c, j0), sn_bank)
@@ -169,7 +169,7 @@ def tile_list_tgn_rnn_kernel(
                     x_w[a, half][:, b0 : b0 + width],
                     x_s[a, half][:, b0 : b0 + width],
                 )
-                for a in range(PASSES)
+                for a in pass_order
             ]
             passes = state_passes + message_passes if state_first else message_passes + state_passes
             for n, (span, w_codes, w_scales, codes, scales) in enumerate(passes):
@@ -304,9 +304,9 @@ def tile_list_tgn_rnn_kernel(
         add_state(0, 0, QUARTER)
         place(0, 0, QUARTER)
         add_state(1, 0, QUARTER)
-        pick_state(1, QUARTER, QUARTER)
+        pick_state(1, HALF, HALF)
         quantise(0, QUARTER, QUARTER)
-        pick_state(1, HALF, HALF, AT_X_SECOND_PICKED1)
+        pick_state(1, QUARTER, QUARTER, AT_X_SECOND_PICKED1)
         quantise(1, QUARTER, QUARTER, AT_X_BF_WINDOW2)
         clear_window(AT_X_BF_WINDOW2)
         factor = own([P, QUARTER], F32, "factor1", AT_X_SECOND_FACTOR1)
@@ -316,8 +316,8 @@ def tile_list_tgn_rnn_kernel(
         steps[2, 0] = own([P, HALF], F32, "step2_0", AT_TANH2_WINDOW3)
         product(2, 0, QUARTER, 5, steps[2, 0][:, :QUARTER])
         product(2, QUARTER, QUARTER, 3, steps[2, 0][:, QUARTER:], bias=third_bias)
-        product(0, QUARTER, QUARTER, 6)
-        product(1, QUARTER, QUARTER, 7)
+        product(0, QUARTER, QUARTER, 6, pass_order=(1, 0))
+        product(1, QUARTER, QUARTER, 7, pass_order=(1, 0))
         add_by_turning(0, QUARTER, QUARTER, 2, 1)
         add_by_turning(1, QUARTER, QUARTER, 0, 4)
         add_state(2, 0, HALF)

from contextlib import ExitStack

import concourse.mybir as mybir
from concourse.masks import make_identity

K, M, N, T, J = 1024, 512, 512, 2048, 1024
FLOPS = 2 * (K + M) * N * J

F32 = mybir.dt.float32
BF16 = mybir.dt.bfloat16
I32 = mybir.dt.int32
U32 = mybir.dt.uint32
U16 = mybir.dt.uint16
U8 = mybir.dt.uint8
FP8X4 = mybir.dt.float8_e4m3fn_x4
FP4X4 = mybir.dt.float4_e2m1fn_x4
ACT = mybir.ActivationFunctionType
ALU = mybir.AluOpType

P = 128
PACK = 4
K_PASS = P * PACK
PASSES = K // K_PASS
QUARTER = J // 4
HALF = J // 2
LINE = 4
LIST_ROWS = 16
QUADRANT = 32
SCALE_ROWS = 16
TAB_ROW_STEP = P // SCALE_ROWS
BANK_BYTES = 2048
WGO_ROWS = J // P
VEC_ROWS = WGO_ROWS + N // P

AT_BIAS0_WINDOW1 = 0
AT_X_SECOND_FACTOR1 = 8
AT_TAB_SCALES_X_CODES = 12
AT_X_LAST_FACTOR3 = 16
AT_X_SECOND_PICKED1 = 24
AT_X_BF_WINDOW2 = 28
AT_TANH2_WINDOW3 = 36
AT_X_FIRST_WEIGHT = 44
AT_BIAS2_PICKED2 = 48


def tile_list_tgn_rnn_kernel(
    tc, x, tab_words, tab_scales, wn_words, wn_scales, un_words, un_scales, bn, hT, wgo, offs, out
):
    nc = tc.nc
    with ExitStack() as ctx:
        keep = ctx.enter_context(tc.tile_pool(name="keep", bufs=1))
        pinned = ctx.enter_context(tc.tile_pool(name="pinned", bufs=1))
        psum = ctx.enter_context(tc.psum_pool(name="psum", bufs=1))

        offsets = keep.tile([P, J // LIST_ROWS], U16, name="offsets")
        x_first = keep.tile([P, PACK, QUARTER], F32, name="x_first", align_bytes=64)
        tab_s = pinned.tile([P, T // 4], I32, name="tab_s", offset=AT_TAB_SCALES_X_CODES * 1024, align_bytes=64)
        w_s = keep.tile([P, PASSES * N // 4], I32, name="w_s", align_bytes=64)
        ident = keep.tile([P, P], F32, name="ident", align_bytes=64)
        vec_rows = keep.tile([P, P], F32, name="vec_rows", align_bytes=64)
        windows = [keep.tile([P, T], F32, name="placed0", align_bytes=64)]

        nc.sync.dma_start(offsets[:], offs)
        nc.sync.dma_start(out=x_first[:], in_=x[:K_PASS, :QUARTER].rearrange("(p i) j -> p i j", i=PACK))
        nc.gpsimd.memset(tab_s[:], 0)
        nc.vector.memset(w_s[:], 0)
        nc.vector.memset(vec_rows[:], 0.0)
        nc.vector.memset(windows[0][:].bitcast(I32), 0)
        nc.gpsimd.dma_start(out=vec_rows[WGO_ROWS:VEC_ROWS, :], in_=bn.rearrange("(c p) -> c p", p=P))
        nc.gpsimd.dma_start(out=vec_rows[0:WGO_ROWS, :], in_=wgo[0].rearrange("(c p) -> c p", p=P))
        make_identity(nc, ident[:])

        work = ctx.enter_context(tc.tile_pool(name="work", bufs=1))

        def bank(name, n):
            return psum.tile([P, HALF], F32, name=name, offset=n * BANK_BYTES)

        def own(shape, dtype, name, at=None):
            if at is None:
                return work.tile(shape, dtype, name=name, align_bytes=64)
            return pinned.tile(shape, dtype, name=name, offset=at * 1024, align_bytes=64)

        x_raw = {(0, 0): x_first}
        h_all = {}
        wn_w = {}
        un_w = {}
        steps = {}
        sums = {}
        picked = {}
        x_w = {(a, j0): own([P, HALF], U32, "x_w%d_%d" % (a, j0)) for a, j0 in ((1, 0), (0, HALF), (1, HALF))}
        x_w[0, 0] = own([P, HALF], U32, "x_w0_0", AT_TAB_SCALES_X_CODES)
        x_s = {(a, j0): own([P, HALF], U8, "x_s%d_%d" % (a, j0)) for a in range(PASSES) for j0 in (0, HALF)}
        v_s = own([P, J // 4], I32, "v_s")
        gathered_s = own([P, J], U8, "gathered_s")
        v_w = own([P, J], U32, "v_w")
        vec_cols = own([P, 16], F32, "vec_cols")

        def listed(j0, width):
            return offsets[:, j0 // LIST_ROWS : (j0 + width) // LIST_ROWS]

        def load_x(a, j0, width, at=None):
            raw = own([P, PACK, width], F32, "x_raw%d_%d" % (a, j0), at)
            x_raw[a, j0] = raw
            rows = x[a * K_PASS : (a + 1) * K_PASS, j0 : j0 + width]
            nc.sync.dma_start(out=raw[:], in_=rows.rearrange("(p i) j -> p i j", i=PACK))

        def load_h(c):
            h_all[c] = own([P, T], F32, "h_all%d" % c)
            nc.sync.dma_start(out=h_all[c][:], in_=hT[c * P : (c + 1) * P, :])

        def move_tab_scales(r):
            rows = gathered_s[:].bitcast(I32)
            nc.sync.dma_start(out=v_s[r:P:QUADRANT, :], in_=rows[TAB_ROW_STEP * r : P : QUADRANT, :])

        def load_un_scales(r):
            nc.sync.dma_start(out=w_s[r:P:QUADRANT, : N // 4], in_=un_scales[0, r:SCALE_ROWS:4, :].bitcast(I32))

        def load_wn_scales(r):
            nc.sync.dma_start(
                out=w_s[4 + r : P : QUADRANT, :].rearrange("q (a n) -> q a n", a=PASSES),
                in_=wn_scales[:, r:SCALE_ROWS:4, :].rearrange("a q n -> q a n").bitcast(I32),
            )

        def load_wn(c):
            wn_w[c] = own([P, PASSES, P], I32, "wn_w%d" % c)
            wn_all = wn_words.rearrange("a p n i -> p a (n i)").bitcast(I32)
            nc.sync.dma_start(out=wn_w[c][:], in_=wn_all[:, :, c * P : (c + 1) * P])

        def load_un(c0):
            words = own([P, P], I32, "un_w%d" % c0)
            for c in range(c0, c0 + 2):
                un_w[c] = words[:].bitcast(U8)[:, 2 * (c - c0) * P : 2 * (c - c0 + 1) * P]
            nc.sync.dma_start(out=words[:], in_=un_words[0].bitcast(I32)[:, c0 * P // 2 : (c0 + 2) * P // 2])

        def quantise(a, j0, width, at=None):
            grouped = own([P, width, PACK], BF16, "x_bf%d_%d" % (a, j0), at)
            half, b0 = j0 - j0 % HALF, j0 % HALF
            nc.scalar.activation(
                out=grouped[:].rearrange("p (g j) i -> p g i j", j=LINE),
                in_=x_raw[a, j0][:].rearrange("p i (g j) -> p g i j", j=LINE),
                func=ACT.Copy,
            )
            nc.vector.quantize_mx(
                out=x_w[a, half][:, b0 : b0 + width].bitcast(FP8X4),
                scales=x_s[a, half][:, b0 : b0 + width],
                in_=grouped[:].rearrange("p j i -> p (j i)"),
            )

        def product(c, j0, width, sn_bank, step=None, state_first=True, bias=None, pass_order=(0, 1)):
            cols = slice(c * P, (c + 1) * P)
            half, b0 = j0 - j0 % HALF, j0 % HALF
            sn = bank("sn%d_%d" % (c, j0), sn_bank)
            group = HALF if width == HALF else P
            state_passes = [
                (
                    slice(g0, g0 + group),
                    un_w[c].bitcast(FP4X4),
                    w_s[:].bitcast(U8)[:, cols],
                    v_w[:, j0 + g0 : j0 + g0 + group],
                    v_s[:].bitcast(U8)[:, j0 + g0 : j0 + g0 + group],
                )
                for g0 in range(0, width, group)
            ]
            message_passes = [
                (
                    slice(0, width),
                    wn_w[c][:, a, :].bitcast(FP8X4),
                    w_s[:].bitcast(U8)[4:, a * N + c * P : a * N + (c + 1) * P],
                    x_w[a, half][:, b0 : b0 + width],
                    x_s[a, half][:, b0 : b0 + width],
                )
                for a in pass_order
            ]
            passes = state_passes + message_passes if state_first else message_passes + state_passes
            for n, (span, w_codes, w_scales, codes, scales) in enumerate(passes):
                nc.tensor.matmul_mx(
                    out=sn[:, span], lhsT=w_codes, lhsT_scale=w_scales, rhs=codes.bitcast(FP8X4), rhs_scale=scales,
                    start=(n == 0), stop=(n == len(passes) - 1),
                )
            if step is None:
                steps[c, j0] = own([P, width], F32, "step%d_%d" % (c, j0))
                step = steps[c, j0][:]
            if bias is None:
                bias = vec_cols[:, WGO_ROWS + c : WGO_ROWS + c + 1]
            nc.scalar.activation(out=step, in_=sn[:, :width], func=ACT.Tanh, bias=bias)

        def pick_state(c, j0, width, at=None):
            rows = own([P, width], F32, "picked%d_%d" % (c, j0), at)
            for b0 in range(0, width, P):
                picked[c, j0 + b0] = rows[:, b0 : b0 + P]
            nc.vector.tensor_copy(out=rows[:], in_=h_all[c][:].indirect(listed(j0, width)))

        def add_by_turning(c, j0, width, there_bank, back_bank, unweighed=None):
            there = bank("there%d_%d" % (c, j0), there_bank)
            for b0 in range(0, width, P):
                terms = (steps[c, j0][:, b0 : b0 + P], picked[c, j0 + b0])
                for n, term in enumerate(terms):
                    nc.tensor.matmul(
                        there[:, b0 : b0 + P], lhsT=term, rhs=ident[:], is_transpose=True, start=(n == 0), stop=(n == 1)
                    )
            turned_sum = own([P, width], F32, "turned_sum%d_%d" % (c, j0))
            for b0 in range(0, width, P):
                b = (j0 + b0) // P
                scale = vec_cols[:, b : b + 1] if unweighed is None else 1.0
                nc.scalar.activation(
                    out=turned_sum[:, b0 : b0 + P], in_=there[:, b0 : b0 + P], func=ACT.Copy, scale=scale
                )
            back = bank("back%d_%d" % (c, j0), back_bank)
            for b0 in range(0, width, P):
                nc.tensor.transpose(back[:, b0 : b0 + P], turned_sum[:, b0 : b0 + P], ident[:])
            total = unweighed
            if total is None:
                sums[c, j0] = own([P, width], F32, "sum%d_%d" % (c, j0))
                total = sums[c, j0][:]
            nc.scalar.copy(out=total, in_=back[:, :width])

        def gather_and_add(c, j0, width, step, total):
            nc.vector.tensor_tensor(out=total, in0=h_all[c][:].indirect(listed(j0, width)), in1=step, op=ALU.add)

        def add_state(c, j0, width):
            sums[c, j0] = own([P, width], F32, "sum%d_%d" % (c, j0))
            gather_and_add(c, j0, width, steps[c, j0][:], sums[c, j0][:])

        def place(c, j0, width, factor=None):
            nc.vector.tensor_tensor(
                out=windows[c][:].indirect(listed(j0, width)),
                in0=sums[c, j0][:],
                in1=weight[:, j0 : j0 + width] if factor is None else factor,
                op=ALU.mult,
            )

        def place_weighed(c, j0, width):
            nc.vector.tensor_copy(out=windows[c][:].indirect(listed(j0, width)), in_=sums[c, j0][:])

        def clear_window(at):
            windows.append(own([P, T], F32, "placed%d" % len(windows), at))
            nc.gpsimd.memset(windows[-1][:].bitcast(I32), 0)

        def store(c, last):
            rows = out[c * P : (c + 1) * P, :]
            if last:
                nc.sync.dma_start(out=rows[:, : T // 2], in_=windows[c][:, : T // 2])
                nc.scalar.dma_start(out=rows[:, T // 2 :], in_=windows[c][:, T // 2 :])
            else:
                nc.sync.dma_start(out=rows, in_=windows[c][:])

        nc.sync.dma_start(out=tab_s[0:P:TAB_ROW_STEP, :], in_=tab_scales[0].bitcast(I32))
        for r in range(4):
            load_wn_scales(r)
        tab_w = own([P, T], I32, "tab_w")
        nc.sync.dma_start(out=tab_w[:], in_=tab_words[0].rearrange("p t i -> p (t i)").bitcast(I32))
        load_x(1, 0, QUARTER, AT_X_FIRST_WEIGHT)
        load_wn(0)
        for r in range(4):
            load_un_scales(r)
        load_h(0)
        nc.vector.tensor_copy(out=gathered_s[:], in_=tab_s[:].bitcast(U8).indirect(offsets[:]))
        nc.vector.tensor_copy(out=v_s[:], in_=gathered_s[:].bitcast(I32))
        for r in range(1, 4):
            move_tab_scales(r)
        load_un(0)
        load_wn(1)
        load_h(1)
        load_x(0, QUARTER, QUARTER, AT_X_SECOND_PICKED1)
        load_x(1, QUARTER, QUARTER, AT_X_SECOND_FACTOR1)
        load_wn(2)
        load_un(2)
        load_h(2)
        load_wn(3)
        load_x(0, HALF, HALF)
        load_h(3)
        load_x(1, HALF, HALF, AT_X_LAST_FACTOR3)

        turned = bank("turned", 0)
        nc.tensor.transpose(turned[:, :P], vec_rows[:], ident[:])
        nc.scalar.copy(out=vec_cols[:, :VEC_ROWS], in_=turned[:, :VEC_ROWS])

        def spread_weights(j0, spread_bank):
            spread = bank("spread%d" % j0, spread_bank)
            for b0 in range(0, HALF, P):
                b = (j0 + b0) // P
                nc.tensor.transpose(spread[:, b0 : b0 + P], vec_cols[:, b : b + 1].to_broadcast([P, P]), ident[:])
            nc.scalar.copy(out=weight[:, j0 : j0 + HALF], in_=spread[:])
            return spread

        def bias_column(c, name, at):
            column = own([P, 1], F32, name, at)
            nc.scalar.copy(out=column[:], in_=turned[:, WGO_ROWS + c : WGO_ROWS + c + 1])
            return column[:]

        nc.vector.tensor_copy(out=v_w[:], in_=tab_w[:].bitcast(U32).indirect(offsets[:]))
        quantise(0, 0, QUARTER)
        quantise(1, 0, QUARTER)
        weight = own([P, J], F32, "weight", AT_X_FIRST_WEIGHT)
        first_spread = spread_weights(0, 1)
        spread_weights(HALF, 2)
        first_bias = bias_column(0, "first_bias", AT_BIAS0_WINDOW1)
        third_bias = bias_column(2, "third_bias", AT_BIAS2_PICKED2)

        product(0, 0, QUARTER, 3, state_first=False, bias=first_bias)
        clear_window(AT_BIAS0_WINDOW1)
        product(1, 0, QUARTER, 3)
        pick_state(0, QUARTER, J - QUARTER)
        add_state(0, 0, QUARTER)
        place(0, 0, QUARTER)
        add_state(1, 0, QUARTER)
        pick_state(1, HALF, HALF)
        quantise(0, QUARTER, QUARTER)
        pick_state(1, QUARTER, QUARTER, AT_X_SECOND_PICKED1)
        quantise(1, QUARTER, QUARTER, AT_X_BF_WINDOW2)
        clear_window(AT_X_BF_WINDOW2)
        factor = own([P, QUARTER], F32, "factor1", AT_X_SECOND_FACTOR1)
        nc.scalar.copy(out=factor[:], in_=first_spread[:, :QUARTER])
        place(1, 0, QUARTER, factor[:])

        steps[2, 0] = own([P, HALF], F32, "step2_0", AT_TANH2_WINDOW3)
        product(2, 0, QUARTER, 5, steps[2, 0][:, :QUARTER])
        product(2, QUARTER, QUARTER, 3, steps[2, 0][:, QUARTER:], bias=third_bias)
        product(0, QUARTER, QUARTER, 6, pass_order=(1, 0))
        product(1, QUARTER, QUARTER, 7, pass_order=(1, 0))
        add_by_turning(0, QUARTER, QUARTER, 2, 1)
        add_by_turning(1, QUARTER, QUARTER, 0, 4)
        add_state(2, 0, HALF)
        pick_state(2, HALF, P, AT_BIAS2_PICKED2)
        clear_window(AT_TANH2_WINDOW3)
        place(2, 0, HALF)
        place_weighed(0, QUARTER, QUARTER)
        place_weighed(1, QUARTER, QUARTER)

        product(3, 0, HALF, 0)
        quantise(0, HALF, HALF)
        add_state(3, 0, HALF)
        quantise(1, HALF, HALF)
        factor = own([P, HALF], F32, "factor3", AT_X_LAST_FACTOR3)
        nc.scalar.copy(out=factor[:], in_=weight[:, :HALF])
        place(3, 0, HALF, factor[:])

        product(3, HALF, HALF, 1)
        product(2, HALF, HALF, 4)
        sums[2, HALF] = own([P, HALF], F32, "sum2_late")
        add_by_turning(2, HALF, P, 0, 7, unweighed=sums[2, HALF][:, :P])
        product(0, HALF, HALF, 1)
        product(1, HALF, HALF, 4)
        add_by_turning(0, HALF, HALF, 2, 3)
        add_by_turning(1, HALF, HALF, 5, 6)
        add_state(3, HALF, HALF)
        gather_and_add(2, HALF + P, HALF - P, steps[2, HALF][:, P:], sums[2, HALF][:, P:])
        for c in (3, 2):
            place(c, HALF, HALF)
            store(c, last=False)
        for c in (0, 1):
            place_weighed(c, HALF, HALF)
            store(c, last=(c == 1))
